import numpy as np
import ml_dtypes


def mxq(x, axis, fmt="e4m3"):
    dtype, down = {"e4m3": (ml_dtypes.float8_e4m3fn, 7), "e5m2": (ml_dtypes.float8_e5m2, 14)}[fmt]
    v = np.moveaxis(np.asarray(x, np.float32).astype(ml_dtypes.bfloat16).astype(np.float64), axis, -1)
    blocks = v.reshape(v.shape[:-1] + (-1, 32))
    amax = np.abs(blocks).max(-1, keepdims=True)
    byte = np.maximum(np.where(amax > 0, np.frexp(amax)[1] - 1 + 127, 0) - down, 1)
    scale = np.exp2(byte - 127.0)
    codes = (blocks / scale).astype(np.float32).astype(dtype).astype(np.float64)
    return np.moveaxis((codes * scale).reshape(v.shape), -1, axis)


WIDE = False


def mx_kscale(k):
    if not WIDE:
        return np.ones(k)
    levels = np.array([10, -10, 5, -5, 0])
    if k % 512:
        return np.exp2(np.random.permutation(np.resize(levels, k // 32))).repeat(32)
    a = np.empty((k // 512, 16))
    for p in range(k // 512):
        a[p, :8] = np.random.permutation(np.resize(levels, 8))
        for g in range(8):
            far = levels[np.abs(levels - a[p, g]) >= 10]
            a[p, g + 8] = far[np.random.randint(len(far))]
    return np.exp2(a.ravel()).repeat(32)


BF16 = ml_dtypes.bfloat16


def bf(x):
    return np.asarray(x, np.float32).astype(BF16)


def f64(x):
    return np.asarray(x).astype(np.float64)


E2M1 = np.array([0.0, 0.5, 1.0, 1.5, 2.0, 3.0, 4.0, 6.0, -0.0, -0.5, -1.0, -1.5, -2.0, -3.0, -4.0, -6.0])


def pack_weight(w, fmt):
    k, n = w.shape
    w = f64(bf(w)).reshape(k // 32, 32, n)
    amax = np.abs(w).max(1)
    if fmt == "e4m3":
        byte = np.frexp(amax)[1] - 1 + 127 - 7
    else:
        mant, ex = np.frexp(amax / 6.0)
        byte = np.where(mant > 0.5, ex, ex - 1) + 127
    byte = np.clip(np.where(amax > 0, byte, 1), 1, 254)
    scaled = (w * np.exp2(127.0 - byte)[:, None, :]).reshape(k, n).astype(np.float32)
    by_word = np.ascontiguousarray(scaled.reshape(k // 512, 128, 4, n).transpose(0, 1, 3, 2))
    if fmt == "e4m3":
        words = by_word.astype(ml_dtypes.float8_e4m3fn).view(np.uint8)
    else:
        c = by_word.astype(ml_dtypes.float4_e2m1fn).view(np.uint8) & 0xF
        words = c[..., 0::2] | (c[..., 1::2] << 4)
    return np.ascontiguousarray(words), np.ascontiguousarray(byte.astype(np.uint8).reshape(k // 512, 16, n))


def unpack_weight(words, scales, fmt):
    g, p, n, _ = words.shape
    if fmt == "e4m3":
        vals = np.ascontiguousarray(words).view(ml_dtypes.float8_e4m3fn).astype(np.float64)
    else:
        nib = np.empty((g, p, n, 4), np.uint8)
        nib[..., 0::2] = words & 0xF
        nib[..., 1::2] = words >> 4
        vals = E2M1[nib]
    vals = vals * np.repeat(np.exp2(scales.astype(np.float64) - 127.0), 8, axis=1)[..., None]
    return vals.transpose(0, 1, 3, 2).reshape(g * 512, n)
def pack4(w):
    words, scales = pack_weight(w, "e2m1")
    return words.reshape(words.shape[0], 128, -1), scales


def unpack4(words, scales):
    return unpack_weight(words.reshape(words.shape[0], 128, -1, 2), scales, "e2m1")


E4M3FN = np.array([(-1.0 if i & 128 else 1.0) * ((1.0 + (i & 7) / 8.0) * 2.0 ** (((i >> 3) & 15) - 7) if i & 120 else (i & 7) * 2.0 ** -9) for i in range(256)])


def e4m3fn_bytes(y):
    return np.clip(np.asarray(y, np.float64), -448.0, 448.0).astype(np.float32).astype(ml_dtypes.float8_e4m3fn).view(np.uint8)


def e4m3fn_values(b):
    return E4M3FN[b]


P, N, D, K = 2, 512, 1024, 512


def softplus(v):
    return np.maximum(v, 0.0) + np.log(1.0 + np.exp(-np.abs(v)))


def draw0():
    s, t = mx_kscale(D), mx_kscale(K)
    h = bf(np.random.standard_normal((P, N, D)) * s)
    wa_words, wa_scales = pack4(np.random.standard_normal((D, K)) / np.sqrt(D) / s[:, None] * t)
    wb_words, wb_scales = pack4(np.random.standard_normal((D, K)) / np.sqrt(D) / s[:, None] / t)
    return {"h": h,
            "wa_words": wa_words, "wa_scales": wa_scales,
            "wb_words": wb_words, "wb_scales": wb_scales,
            "gate": bf(np.random.standard_normal((P, K)))}


def core(h, wa_words, wa_scales, wb_words, wb_scales, gate):
    hq = mxq(f64(h), 2, "e4m3")
    a = hq @ unpack4(wa_words, wa_scales)
    b = hq @ unpack4(wb_words, wb_scales)
    lam = softplus(f64(gate))
    al = a * lam[:, None, :]
    x = mxq(al, 2, "e4m3") @ mxq(b, 2, "e4m3").transpose(0, 2, 1)
    s = (x - np.swapaxes(x, 1, 2)) / np.sqrt(K)
    return -softplus(-s)


def setup_inputs():
    drawn = draw0()
    full = np.asarray(drawn['h']).astype(np.float64)
    scale = (np.abs(full).reshape(2, 4, 128, 8, 128).max(axis=(2, 4)) / 448.0).astype(np.float32)
    given = {}
    for key, value in drawn.items():
        if key == 'h':
            given['h_bytes'] = e4m3fn_bytes(full / np.repeat(np.repeat(scale.astype(np.float64), 128, axis=1), 128, axis=2))
            given['h_scale'] = scale
        else:
            given[key] = value
    return given


def reference(h_bytes, h_scale, wa_words, wa_scales, wb_words, wb_scales, gate):
    return core(e4m3fn_values(h_bytes) * np.repeat(np.repeat(h_scale.astype(np.float64), 128, axis=1), 128, axis=2), wa_words, wa_scales, wb_words, wb_scales, gate)

@@ -1,0 +1,296 @@
+from contextlib import ExitStack
+
+import concourse.mybir as mybir
+from concourse.masks import make_identity
+
+NP, N, D, K = 2, 512, 1024, 512
+P = 128
+NT = N // P
+G = D // 512
+FLOPS = 2 * NP * (2 * N * D * K + N * N * K)
+C = K ** -0.5
+TINY = 2.0 ** -60
+
+F32 = mybir.dt.float32
+BF16 = mybir.dt.bfloat16
+I32 = mybir.dt.int32
+U32 = mybir.dt.uint32
+U8 = mybir.dt.uint8
+FP8 = mybir.dt.float8_e4m3fn
+FP8X4 = mybir.dt.float8_e4m3fn_x4
+FP4X4 = mybir.dt.float4_e2m1fn_x4
+ALU = mybir.AluOpType
+ACT = mybir.ActivationFunctionType
+
+
+def tile_generalpreferenceskewembeddingscores_d2p_kernel(
+    tc, h_bytes, h_scale, wa_words, wa_scales, wb_words, wb_scales, gate, out
+):
+    nc = tc.nc
+    with ExitStack() as ctx:
+        sb = ctx.enter_context(tc.tile_pool(name="sb", bufs=1))
+        ps = ctx.enter_context(tc.psum_pool(name="ps", bufs=1))
+        ctx.enter_context(tc.manual_schedule())
+
+        def bank(b, shape, name, dtype=F32):
+            return ps.tile(shape, dtype, name=name, tag=f"bank{b}")
+
+        gate_rows = sb.tile([P, NP * P], BF16, name="gate_rows")
+        ident = sb.tile([P, P], F32, name="ident")
+        ident16 = sb.tile([P, P], BF16, name="ident16")
+        w_raw = [sb.tile([P, G, 1024], U8, name=f"w_raw{w}", align_bytes=64) for w in range(2)]
+        w_perm = [sb.tile([P, G, 4, 256], U8, name=f"w_perm{w}", align_bytes=64) for w in range(2)]
+        s_raw = [sb.tile([P, G, K], U8, name=f"s_raw{w}", align_bytes=64) for w in range(2)]
+        s_perm = [sb.tile([P, G, 4, P], U8, name=f"s_perm{w}", align_bytes=64) for w in range(2)]
+        scales = sb.tile([P, NP * NT * 8], F32, name="scales")
+        tiny = sb.tile([P, 1], F32, name="tiny")
+
+        nc.vector.memset(gate_rows[:], 0.0)
+        for w in range(2):
+            nc.vector.memset(s_raw[w][:].rearrange("p g k -> p (g k)").bitcast(I32), 0)
+        nc.vector.memset(tiny[:], TINY)
+
+        nc.gpsimd.dma_start(
+            out=gate_rows[0:4, :].rearrange("t (q r) -> t q r", r=8),
+            in_=gate.rearrange("a (q t r) -> t (a q) r", t=4, r=8),
+        )
+        make_identity(nc, ident[:])
+        make_identity(nc, ident16[:])
+        nc.scalar.dma_start(
+            out=scales[:], in_=h_scale.rearrange("a i j -> (a i j)").partition_broadcast(P)
+        )
+
+        codes_in = {}
+
+        def load_h(a, first, count):
+            t = sb.tile([P, count, D], U8, name=f"h_bytes{a}_{first}", align_bytes=64)
+            nc.sync.dma_start(
+                out=t[:],
+                in_=h_bytes[a, first * P : (first + count) * P, :].rearrange("(i p) k -> p i k", p=P),
+            )
+            for i in range(count):
+                codes_in[a * NT + first + i] = (t, i)
+
+        def load_words(w, words):
+            nc.sync.dma_start(
+                out=w_raw[w][:].rearrange("p g b -> p (g b)").bitcast(I32).rearrange("p (g c) -> p g c", g=G),
+                in_=words.bitcast(I32).rearrange("g p c -> p g c"),
+            )
+
+        def load_scales(w, src):
+            v = src.bitcast(I32).rearrange("g (q r) c -> q r g c", r=4)
+            d = s_raw[w][:].rearrange("p g k -> p (g k)").bitcast(I32).rearrange("p (g c) -> p g c", g=G)
+            for q in range(4):
+                nc.sync.dma_start(out=d[32 * q : 32 * q + 4], in_=v[q])
+
+        load_h(0, 0, 1)
+        load_h(0, 1, 3)
+        load_words(0, wa_words)
+        load_scales(0, wa_scales)
+        load_words(1, wb_words)
+        load_scales(1, wb_scales)
+        load_h(1, 0, 4)
+
+        wide, pt, hg, hc, hs = {}, {}, {}, {}, {}
+        pa, pb, ab, nal = {}, {}, {}, {}
+        kc = [sb.tile([P, 3, N], U32, name=f"kc{a}", align_bytes=64) for a in range(NP)]
+        ks = [sb.tile([P, 3, N], U8, name=f"ks{a}", align_bytes=64) for a in range(NP)]
+        px, sig, logs = {}, {}, {}
+        lam = sb.tile([P, NP, 4], F32, name="lam")
+        g_sb = sb.tile([P, NP, 4], F32, name="g_sb")
+        g_abs = sb.tile([P, NP, 4], F32, name="g_abs")
+        g_exp = sb.tile([P, NP, 4], F32, name="g_exp")
+        g_ln = sb.tile([P, NP, 4], F32, name="g_ln")
+
+        ps_gate = {}
+
+        def gate_turn():
+            pg = bank(7, [P, NP, P], "pg", BF16)
+            ps_gate["pg"] = pg
+            for a in range(NP):
+                nc.tensor.transpose(pg[:, a, :], gate_rows[:, P * a : P * (a + 1)], ident16[:])
+
+        def gate_out():
+            pg = ps_gate["pg"]
+            nc.scalar.activation(out=g_abs[:], in_=pg[:, :, 0:4], func=ACT.Abs)
+            nc.scalar.copy(out=g_sb[:], in_=pg[:, :, 0:4])
+
+        def gate_exp():
+            nc.scalar.activation(out=g_exp[:], in_=g_abs[:], func=ACT.Exp, scale=-1.0)
+
+        def gate_ln():
+            nc.scalar.activation(out=g_ln[:], in_=g_exp[:], func=ACT.Ln, bias=1.0)
+
+        def gate_lam():
+            nc.vector.scalar_tensor_tensor(
+                out=lam[:], in0=g_sb[:], scalar=0.0, in1=g_ln[:], op0=ALU.max, op1=ALU.add
+            )
+
+        def W(T):
+            t, i = codes_in[T]
+            wide[T] = sb.tile([P, D], BF16, name=f"wide{T}", align_bytes=64)
+            for j in range(8):
+                nc.vector.tensor_scalar(
+                    out=wide[T][:, 512 * (j // 4) : 512 * (j // 4 + 1)].rearrange("p (u w e) -> p w u e", u=2, e=2)[
+                        :, 32 * (j % 4) : 32 * (j % 4 + 1)
+                    ],
+                    in0=t[:, i, P * j : P * (j + 1)].bitcast(FP8).rearrange("p (w u e) -> p w u e", u=2, e=2),
+                    scalar1=scales[:, 8 * T + j : 8 * T + j + 1],
+                    scalar2=None,
+                    op0=ALU.mult,
+                )
+
+        def X(T):
+            pt[T] = bank(T % 2, [P, 2 * G, P], f"pt{T}")
+            words = wide[T][:].bitcast(F32)
+            for g in range(G):
+                for u in range(2):
+                    nc.tensor.transpose(
+                        pt[T][:, 2 * g + u, :], words[:, 256 * g + P * u : 256 * g + P * (u + 1)], ident[:]
+                    )
+
+        def E(T):
+            hg[T] = sb.tile([P, G * P * 4], BF16, name=f"hg{T}", align_bytes=64)
+            nc.scalar.copy(
+                out=hg[T][:].bitcast(F32).rearrange("p (g n u) -> p g n u", g=G, u=2),
+                in_=pt[T][:].rearrange("p (g u) n -> p g n u", g=G),
+            )
+
+        def Q(T):
+            hc[T] = sb.tile([P, G * P], U32, name=f"hc{T}", align_bytes=64)
+            hs[T] = sb.tile([P, G * P], U8, name=f"hs{T}", align_bytes=64)
+            nc.vector.quantize_mx(out=hc[T][:].bitcast(FP8X4), scales=hs[T][:], in_=hg[T][:])
+
+        def PERM(w):
+            for dst, src, x in (
+                (w_perm[w][:].rearrange("p g t b -> p (g t b)"), w_raw[w][:].rearrange("p g b -> p (g b)"), 4),
+                (s_perm[w][:].rearrange("p g t b -> p (g t b)"), s_raw[w][:].rearrange("p g b -> p (g b)"), 2),
+            ):
+                nc.vector.tensor_copy(
+                    out=dst.bitcast(I32).rearrange("p (g t q x) -> p g q t x", g=G, t=4, x=x),
+                    in_=src.bitcast(I32).rearrange("p (g q t x) -> p g q t x", g=G, t=4, x=x),
+                )
+
+        def M(w, T):
+            for store in ((pa, pb)[w],):
+                store[T] = bank((2, 4, 6, 2, 4, 6, 2, 2)[T] + w, [P, 4, P], f"p{w}_{T}")
+                for t in range(4):
+                    for g in range(G):
+                        nc.tensor.matmul_mx(
+                            out=store[T][:, t, :],
+                            lhsT=w_perm[w][:, g, t, :].bitcast(FP4X4),
+                            lhsT_scale=s_perm[w][:, g, t, :],
+                            rhs=hc[T][:, P * g : P * (g + 1)].bitcast(FP8X4),
+                            rhs_scale=hs[T][:, P * g : P * (g + 1)],
+                            start=(g == 0),
+                            stop=(g == G - 1),
+                        )
+
+        def pair_tile(T):
+            r = T // 2
+            if r not in ab:
+                ab[r] = sb.tile([P, 2, 2, 512], BF16, name=f"ab{r}", align_bytes=64)
+            return ab[r]
+
+        def A(T):
+            a = T // NT
+            nc.vector.tensor_tensor(
+                out=pair_tile(T)[:, 0, T % 2, :].rearrange("p (n t) -> p n t", t=4),
+                in0=pa[T][:].rearrange("p t n -> p n t"),
+                in1=lam[:, a : a + 1, :].to_broadcast([P, P, 4]),
+                op=ALU.mult,
+            )
+
+        def B(T):
+            nc.scalar.copy(
+                out=pair_tile(T)[:, 1, T % 2, :].rearrange("p (n t) -> p n t", t=4),
+                in_=pb[T][:].rearrange("p t n -> p n t"),
+            )
+
+        GROUPS = ((0, 1), (2, 3), (4, 5), (6,), (7,))
+
+        def group_src(k, gi):
+            g = GROUPS[gi]
+            r = g[0] // 2
+            cols = slice(512 * (g[0] % 2), 512 * (g[-1] % 2 + 1))
+            if k == 2:
+                return nal[r][:, cols]
+            return ab[r][:, k].rearrange("p i n -> p (i n)")[:, cols]
+
+        def NEG(gi):
+            r = GROUPS[gi][0] // 2
+            if r not in nal:
+                nal[r] = sb.tile([P, 1024], BF16, name=f"nal{r}", align_bytes=64)
+            nc.vector.tensor_scalar(
+                out=group_src(2, gi), in0=group_src(0, gi), scalar1=-1.0, scalar2=None, op0=ALU.mult
+            )
+
+        def R(k, gi):
+            g = GROUPS[gi]
+            a, cols = g[0] // NT, slice(P * (g[0] % NT), P * (g[-1] % NT + 1))
+            nc.vector.quantize_mx(
+                out=kc[a][:, k, cols].bitcast(FP8X4), scales=ks[a][:, k, cols], in_=group_src(k, gi)
+            )
+
+        def XX(a, n):
+            x = px[a, n] = bank((6, 7, 4, 5)[n] if a == 0 else n, [P, N], f"px{a}_{n}")
+            rows = slice(P * n, P * (n + 1))
+            for s, m in ((0, 1), (1, 2)):
+                nc.tensor.matmul_mx(
+                    out=x[:],
+                    lhsT=kc[a][:, s, rows].bitcast(FP8X4),
+                    lhsT_scale=ks[a][:, s, rows],
+                    rhs=kc[a][:, m, :].bitcast(FP8X4),
+                    rhs_scale=ks[a][:, m, :],
+                    start=(s == 0),
+                    stop=(s == 1),
+                )
+
+        def SIG(a, n):
+            sig[a, n] = sb.tile([P, N], F32, name=f"sig{a}_{n}")
+            nc.scalar.activation(out=sig[a, n][:], in_=px[a, n][:], func=ACT.Sigmoid, scale=C)
+
+        def col_cuts(a, n):
+            last = (a, n) == (NP - 1, NT - 1)
+            return [slice(0, N // 2), slice(N // 2, N)] if last else [slice(0, N)]
+
+        def LOG(a, n):
+            logs[a, n] = sb.tile([P, N], F32, name=f"logs{a}_{n}")
+            for cut in col_cuts(a, n):
+                nc.scalar.activation(
+                    out=logs[a, n][:, cut], in_=sig[a, n][:, cut], func=ACT.Ln, bias=tiny[:]
+                )
+
+        def FIN(a, n):
+            o = sb.tile([P, N], F32, name=f"o{a}_{n}")
+            for cut in col_cuts(a, n):
+                nc.vector.scalar_tensor_tensor(
+                    out=o[:, cut], in0=px[a, n][:, cut], scalar=C, in1=logs[a, n][:, cut],
+                    op0=ALU.mult, op1=ALU.min,
+                )
+                nc.sync.dma_start(out=out[a, P * n : P * (n + 1), cut], in_=o[:, cut])
+
+        ORDER = (
+            "W0 W1 X0 W2 E0 X1 W3 gP E1 X2 Pa g1 Q0 X3 W4 E2 Ma0 g2 Pb X4 Q2 Q1 Mb0 W5 Ma2 g3 W7 E3 "
+            "Ma1 E4 lam W6 X5 Q3 Mb1 A0 E5 X6 Q4 B1 A2 Ma3 B0 A1 Mb2 E6 Q5 X7 A3 B2 Ma5 N0 E7 Q6 Mb3 "
+            "Ra1 N1 Ma6 A5 B3 Mb5 Q7 Ra0 Mb4 A6 B5 Mb6 Rb0 B4 Rn0 Ma4 Ra3 N3 B6 Rb1 Ma7 Rn1 Rn3 Rb2 "
+            "XX00 A4 Mb7 A7 XX01 S00 Rb3 N2 N4 XX02 B7 Ra4 Ra2 XX03 Rn4 S01 Rn2 Rb4 S02 XX10 S03 XX11 "
+            "S10 XX12 S11 XX13 S12 S13 G00 G01 F00 G02 F01 G03 F02 G10 F03 G11 F10 G12 F11 G13 F12 "
+            "F13 "
+        )
+        steps = {"gP": gate_turn, "g1": gate_out, "g2": gate_exp, "g3": gate_ln, "lam": gate_lam}
+        kinds = {
+            "W": W, "X": X, "E": E, "Q": Q, "A": A, "B": B, "N": NEG,
+            "Ma": lambda T: M(0, T), "Mb": lambda T: M(1, T),
+            "Ra": lambda g: R(0, g), "Rb": lambda g: R(1, g), "Rn": lambda g: R(2, g),
+            "XX": lambda k: XX(k // 10, k % 10), "S": lambda k: SIG(k // 10, k % 10),
+            "G": lambda k: LOG(k // 10, k % 10), "F": lambda k: FIN(k // 10, k % 10),
+        }
+        for step in ORDER.split():
+            if step in steps:
+                steps[step]()
+            elif step in ("Pa", "Pb"):
+                PERM(0 if step == "Pa" else 1)
+            else:
+                head = "".join([ch for ch in step if ch not in "0123456789"])
+                kinds[head](int(step[len(head):]))

@@ -1,3 +1,4 @@
+import math
 from contextlib import ExitStack
 
 import concourse.mybir as mybir
@@ -6,10 +7,12 @@ from concourse.masks import make_identity
 NP, N, D, K = 2, 512, 1024, 512
 P = 128
 NT = N // P
+TILES = NP * NT
 G = D // 512
 FLOPS = 2 * NP * (2 * N * D * K + N * N * K)
 C = K ** -0.5
 TINY = 2.0 ** -60
+TERMS = 9
 
 F32 = mybir.dt.float32
 BF16 = mybir.dt.bfloat16
@@ -22,6 +25,9 @@ FP4X4 = mybir.dt.float4_e2m1fn_x4
 ALU = mybir.AluOpType
 ACT = mybir.ActivationFunctionType
 
+WB, WA = 0, 1
+AL, BP, BN = 0, 1, 2
+
 
 def tile_generalpreferenceskewembeddingscores_d2p_kernel(
     tc, h_bytes, h_scale, wa_words, wa_scales, wb_words, wb_scales, gate, out
@@ -32,33 +38,41 @@ def tile_generalpreferenceskewembeddingscores_d2p_kernel(
         ps = ctx.enter_context(tc.psum_pool(name="ps", bufs=1))
         ctx.enter_context(tc.manual_schedule())
 
-        def bank(b, shape, name, dtype=F32):
-            return ps.tile(shape, dtype, name=name, tag=f"bank{b}")
+        def bank(b, shape, name):
+            return ps.tile(shape, F32, name=name, tag=f"bank{b}")
 
         gate_rows = sb.tile([P, NP * P], BF16, name="gate_rows")
         ident = sb.tile([P, P], F32, name="ident")
-        ident16 = sb.tile([P, P], BF16, name="ident16")
+        pick4 = sb.tile([P, 4], BF16, name="pick4")
         w_raw = [sb.tile([P, G, 1024], U8, name=f"w_raw{w}", align_bytes=64) for w in range(2)]
         w_perm = [sb.tile([P, G, 4, 256], U8, name=f"w_perm{w}", align_bytes=64) for w in range(2)]
         s_raw = [sb.tile([P, G, K], U8, name=f"s_raw{w}", align_bytes=64) for w in range(2)]
         s_perm = [sb.tile([P, G, 4, P], U8, name=f"s_perm{w}", align_bytes=64) for w in range(2)]
-        scales = sb.tile([P, NP * NT * 8], F32, name="scales")
+        scales = sb.tile([P, TILES * 8], F32, name="scales")
         tiny = sb.tile([P, 1], F32, name="tiny")
 
-        nc.vector.memset(gate_rows[:], 0.0)
-        for w in range(2):
-            nc.vector.memset(s_raw[w][:].rearrange("p g k -> p (g k)").bitcast(I32), 0)
-        nc.vector.memset(tiny[:], TINY)
+        odd = sb.tile([P, NP * 4, TERMS], F32, name="odd")
+        half_odd = sb.tile([P, NP * 4, TERMS], F32, name="half_odd")
+        neg_ln2 = sb.tile([P, 1], F32, name="neg_ln2")
+        factor = sb.tile([P, NP * 4, TERMS + 1], F32, name="factor")
+        addend = sb.tile([P, NP * 4, TERMS + 1], F32, name="addend")
 
-        nc.gpsimd.dma_start(
-            out=gate_rows[0:4, :].rearrange("t (q r) -> t q r", r=8),
-            in_=gate.rearrange("a (q t r) -> t (a q) r", t=4, r=8),
+        nc.gpsimd.iota(
+            odd[:], pattern=[[0, NP * 4], [-2, TERMS]], base=2 * TERMS - 1, channel_multiplier=0,
+            allow_small_or_imprecise_dtypes=True,
         )
         make_identity(nc, ident[:])
-        make_identity(nc, ident16[:])
-        nc.scalar.dma_start(
-            out=scales[:], in_=h_scale.rearrange("a i j -> (a i j)").partition_broadcast(P)
+        for w in range(2):
+            nc.vector.memset(s_raw[w][:].rearrange("p g k -> p (g k)").bitcast(I32), 0)
+        nc.vector.memset(gate_rows[:], 0.0)
+        nc.vector.memset(tiny[:], TINY)
+        nc.vector.memset(factor[:, :, 0:1], 0.0)
+        nc.vector.tensor_scalar(out=half_odd[:], in0=odd[:], scalar1=0.5, scalar2=None, op0=ALU.mult)
+        nc.vector.tensor_scalar(
+            out=neg_ln2[:], in0=odd[:, 0, TERMS - 1 : TERMS], scalar1=-math.log(2.0), scalar2=None, op0=ALU.mult
         )
+        nc.vector.reciprocal(out=addend[:, :, 0:TERMS], in_=half_odd[:])
+        nc.vector.tensor_copy(out=pick4[:], in_=ident[:, 0:4])
 
         codes_in = {}
 
@@ -77,59 +91,70 @@ def tile_generalpreferenceskewembeddingscores_d2p_kernel(
                 in_=words.bitcast(I32).rearrange("g p c -> p g c"),
             )
 
-        def load_scales(w, src):
-            v = src.bitcast(I32).rearrange("g (q r) c -> q r g c", r=4)
+        def load_scale_rows(w, wscales, queue):
+            v = wscales.bitcast(I32).rearrange("g (q r) c -> q r g c", r=4)
             d = s_raw[w][:].rearrange("p g k -> p (g k)").bitcast(I32).rearrange("p (g c) -> p g c", g=G)
             for q in range(4):
-                nc.sync.dma_start(out=d[32 * q : 32 * q + 4], in_=v[q])
+                queue.dma_start(out=d[32 * q : 32 * q + 4], in_=v[q])
 
         load_h(0, 0, 1)
+        nc.scalar.dma_start(
+            out=scales[:], in_=h_scale.rearrange("a i j -> (a i j)").partition_broadcast(P)
+        )
         load_h(0, 1, 3)
-        load_words(0, wa_words)
-        load_scales(0, wa_scales)
-        load_words(1, wb_words)
-        load_scales(1, wb_scales)
+        load_words(WB, wb_words)
+        load_scale_rows(WB, wb_scales, nc.scalar)
+        nc.sync.dma_start(
+            out=gate_rows[0:4, :].rearrange("t (q r) -> t q r", r=8),
+            in_=gate.rearrange("a (q t r) -> t (a q) r", t=4, r=8),
+        )
+        load_words(WA, wa_words)
+        load_scale_rows(WA, wa_scales, nc.sync)
         load_h(1, 0, 4)
 
-        wide, pt, hg, hc, hs = {}, {}, {}, {}, {}
-        pa, pb, ab, nal = {}, {}, {}, {}
+        wide_hi = {}
+        wide, pt, hg, hc, hs, prod, emb = {}, {}, {}, {}, {}, {}, {}
         kc = [sb.tile([P, 3, N], U32, name=f"kc{a}", align_bytes=64) for a in range(NP)]
         ks = [sb.tile([P, 3, N], U8, name=f"ks{a}", align_bytes=64) for a in range(NP)]
-        px, sig, logs = {}, {}, {}
+        px, neg_s, sig, logs, res, up = {}, {}, {}, {}, {}, {}
         lam = sb.tile([P, NP, 4], F32, name="lam")
-        g_sb = sb.tile([P, NP, 4], F32, name="g_sb")
-        g_abs = sb.tile([P, NP, 4], F32, name="g_abs")
-        g_exp = sb.tile([P, NP, 4], F32, name="g_exp")
-        g_ln = sb.tile([P, NP, 4], F32, name="g_ln")
-
-        ps_gate = {}
+        z_pos = sb.tile([P, NP * 4], F32, name="z_pos")
+        z_neg = sb.tile([P, NP * 4], F32, name="z_neg")
+        horner = sb.tile([P, NP * 4, TERMS + 1], F32, name="horner")
 
         def gate_turn():
-            pg = bank(7, [P, NP, P], "pg", BF16)
-            ps_gate["pg"] = pg
+            pg = bank(5, [P, NP * 4], "pg")
             for a in range(NP):
-                nc.tensor.transpose(pg[:, a, :], gate_rows[:, P * a : P * (a + 1)], ident16[:])
+                nc.tensor.matmul(
+                    pg[:, 4 * a : 4 * a + 4], lhsT=gate_rows[:, P * a : P * (a + 1)], rhs=pick4[:], start=True, stop=True
+                )
+            nc.scalar.activation(out=z_pos[:], in_=pg[:], func=ACT.Sigmoid, scale=1.0, bias=neg_ln2[:])
+            nc.scalar.activation(out=z_neg[:], in_=pg[:], func=ACT.Sigmoid, scale=-1.0, bias=neg_ln2[:])
+            nc.scalar.activation(out=addend[:, :, TERMS], in_=pg[:], func=ACT.Relu)
 
-        def gate_out():
-            pg = ps_gate["pg"]
-            nc.scalar.activation(out=g_abs[:], in_=pg[:, :, 0:4], func=ACT.Abs)
-            nc.scalar.copy(out=g_sb[:], in_=pg[:, :, 0:4])
+        def gate_z():
+            nc.vector.tensor_tensor(out=factor[:, :, TERMS], in0=z_pos[:], in1=z_neg[:], op=ALU.min)
 
-        def gate_exp():
-            nc.scalar.activation(out=g_exp[:], in_=g_abs[:], func=ACT.Exp, scale=-1.0)
+        def gate_z2():
+            z = factor[:, :, TERMS : TERMS + 1].to_broadcast([P, NP * 4, TERMS - 1])
+            nc.vector.tensor_tensor(out=factor[:, :, 1:TERMS], in0=z, in1=z, op=ALU.mult)
 
-        def gate_ln():
-            nc.scalar.activation(out=g_ln[:], in_=g_exp[:], func=ACT.Ln, bias=1.0)
-
-        def gate_lam():
-            nc.vector.scalar_tensor_tensor(
-                out=lam[:], in0=g_sb[:], scalar=0.0, in1=g_ln[:], op0=ALU.max, op1=ALU.add
+        def gate_series():
+            nc.vector.tensor_tensor_scan(
+                out=horner[:].rearrange("p c n -> p (c n)"),
+                data0=factor[:].rearrange("p c n -> p (c n)"),
+                data1=addend[:].rearrange("p c n -> p (c n)"),
+                initial=0.0,
+                op0=ALU.mult,
+                op1=ALU.add,
             )
+            nc.scalar.copy(out=lam[:].rearrange("p a t -> p (a t)"), in_=horner[:, :, TERMS])
 
-        def W(T):
+        def widen(T, blocks):
             t, i = codes_in[T]
-            wide[T] = sb.tile([P, D], BF16, name=f"wide{T}", align_bytes=64)
-            for j in range(8):
+            if T not in wide:
+                wide[T] = sb.tile([P, D], BF16, name=f"wide{T}", align_bytes=64)
+            for j in blocks:
                 nc.vector.tensor_scalar(
                     out=wide[T][:, 512 * (j // 4) : 512 * (j // 4 + 1)].rearrange("p (u w e) -> p w u e", u=2, e=2)[
                         :, 32 * (j % 4) : 32 * (j % 4 + 1)
@@ -140,28 +165,41 @@ def tile_generalpreferenceskewembeddingscores_d2p_kernel(
                     op0=ALU.mult,
                 )
 
-        def X(T):
-            pt[T] = bank(T % 2, [P, 2 * G, P], f"pt{T}")
+        def widen_plain(T):
+            t, i = codes_in[T]
+            wide_hi[T] = sb.tile([P, 512], BF16, name=f"wide_hi{T}", align_bytes=64)
+            for j in range(4, 8):
+                nc.scalar.activation(
+                    out=wide_hi[T][:, P * (j - 4) : P * (j - 3)],
+                    in_=t[:, i, P * j : P * (j + 1)].bitcast(FP8),
+                    func=ACT.Copy,
+                    scale=scales[:, 8 * T + j : 8 * T + j + 1],
+                )
+
+        def turn(T):
+            pt[T] = bank((0, 1, 6, 7)[T % 4], [P, 2 * G, P], f"pt{T}")
             words = wide[T][:].bitcast(F32)
             for g in range(G):
                 for u in range(2):
-                    nc.tensor.transpose(
-                        pt[T][:, 2 * g + u, :], words[:, 256 * g + P * u : 256 * g + P * (u + 1)], ident[:]
-                    )
+                    if g == 1 and T in wide_hi:
+                        src = wide_hi[T][:].bitcast(F32)[:, u : 256 : 2]
+                    else:
+                        src = words[:, 256 * g + P * u : 256 * g + P * (u + 1)]
+                    nc.tensor.transpose(pt[T][:, 2 * g + u, :], src, ident[:])
 
-        def E(T):
+        def empty(T):
             hg[T] = sb.tile([P, G * P * 4], BF16, name=f"hg{T}", align_bytes=64)
             nc.scalar.copy(
                 out=hg[T][:].bitcast(F32).rearrange("p (g n u) -> p g n u", g=G, u=2),
                 in_=pt[T][:].rearrange("p (g u) n -> p g n u", g=G),
             )
 
-        def Q(T):
+        def quant_h(T):
             hc[T] = sb.tile([P, G * P], U32, name=f"hc{T}", align_bytes=64)
             hs[T] = sb.tile([P, G * P], U8, name=f"hs{T}", align_bytes=64)
             nc.vector.quantize_mx(out=hc[T][:].bitcast(FP8X4), scales=hs[T][:], in_=hg[T][:])
 
-        def PERM(w):
+        def permute(w):
             for dst, src, x in (
                 (w_perm[w][:].rearrange("p g t b -> p (g t b)"), w_raw[w][:].rearrange("p g b -> p (g b)"), 4),
                 (s_perm[w][:].rearrange("p g t b -> p (g t b)"), s_raw[w][:].rearrange("p g b -> p (g b)"), 2),
@@ -171,126 +209,223 @@ def tile_generalpreferenceskewembeddingscores_d2p_kernel(
                     in_=src.bitcast(I32).rearrange("p (g q t x) -> p g q t x", g=G, t=4, x=x),
                 )
 
-        def M(w, T):
-            for store in ((pa, pb)[w],):
-                store[T] = bank((2, 4, 6, 2, 4, 6, 2, 2)[T] + w, [P, 4, P], f"p{w}_{T}")
-                for t in range(4):
-                    for g in range(G):
-                        nc.tensor.matmul_mx(
-                            out=store[T][:, t, :],
-                            lhsT=w_perm[w][:, g, t, :].bitcast(FP4X4),
-                            lhsT_scale=s_perm[w][:, g, t, :],
-                            rhs=hc[T][:, P * g : P * (g + 1)].bitcast(FP8X4),
-                            rhs_scale=hs[T][:, P * g : P * (g + 1)],
-                            start=(g == 0),
-                            stop=(g == G - 1),
-                        )
+        def project(w, T):
+            acc = prod[w, T] = bank(2 + 2 * (T % 2) + w, [P, 4, P], f"p{w}_{T}")
+            for t in range(4):
+                for g in range(G):
+                    nc.tensor.matmul_mx(
+                        out=acc[:, t, :],
+                        lhsT=w_perm[w][:, g, t, :].bitcast(FP4X4),
+                        lhsT_scale=s_perm[w][:, g, t, :],
+                        rhs=hc[T][:, P * g : P * (g + 1)].bitcast(FP8X4),
+                        rhs_scale=hs[T][:, P * g : P * (g + 1)],
+                        start=(g == 0),
+                        stop=(g == G - 1),
+                    )
 
-        def pair_tile(T):
-            r = T // 2
-            if r not in ab:
-                ab[r] = sb.tile([P, 2, 2, 512], BF16, name=f"ab{r}", align_bytes=64)
-            return ab[r]
+        def emb_tile(k, T):
+            emb[k, T] = sb.tile([P, 512], BF16, name=f"emb{k}_{T}", align_bytes=64)
+            return emb[k, T]
 
-        def A(T):
+        def make_al(T):
             a = T // NT
             nc.vector.tensor_tensor(
-                out=pair_tile(T)[:, 0, T % 2, :].rearrange("p (n t) -> p n t", t=4),
-                in0=pa[T][:].rearrange("p t n -> p n t"),
+                out=emb_tile(AL, T)[:].rearrange("p (n t) -> p n t", t=4),
+                in0=prod[WA, T][:].rearrange("p t n -> p n t"),
                 in1=lam[:, a : a + 1, :].to_broadcast([P, P, 4]),
                 op=ALU.mult,
             )
 
-        def B(T):
+        def make_b(T):
             nc.scalar.copy(
-                out=pair_tile(T)[:, 1, T % 2, :].rearrange("p (n t) -> p n t", t=4),
-                in_=pb[T][:].rearrange("p t n -> p n t"),
+                out=emb_tile(BP, T)[:].rearrange("p (n t) -> p n t", t=4),
+                in_=prod[WB, T][:].rearrange("p t n -> p n t"),
             )
 
-        GROUPS = ((0, 1), (2, 3), (4, 5), (6,), (7,))
-
-        def group_src(k, gi):
-            g = GROUPS[gi]
-            r = g[0] // 2
-            cols = slice(512 * (g[0] % 2), 512 * (g[-1] % 2 + 1))
-            if k == 2:
-                return nal[r][:, cols]
-            return ab[r][:, k].rearrange("p i n -> p (i n)")[:, cols]
-
-        def NEG(gi):
-            r = GROUPS[gi][0] // 2
-            if r not in nal:
-                nal[r] = sb.tile([P, 1024], BF16, name=f"nal{r}", align_bytes=64)
+        def negate_b(T):
             nc.vector.tensor_scalar(
-                out=group_src(2, gi), in0=group_src(0, gi), scalar1=-1.0, scalar2=None, op0=ALU.mult
+                out=emb_tile(BN, T)[:], in0=emb[BP, T][:], scalar1=-1.0, scalar2=None, op0=ALU.mult
             )
 
-        def R(k, gi):
-            g = GROUPS[gi]
-            a, cols = g[0] // NT, slice(P * (g[0] % NT), P * (g[-1] % NT + 1))
-            nc.vector.quantize_mx(
-                out=kc[a][:, k, cols].bitcast(FP8X4), scales=ks[a][:, k, cols], in_=group_src(k, gi)
+        def quant_emb(k, T):
+            a, cols = T // NT, slice(P * (T % NT), P * (T % NT + 1))
+            nc.vector.quantize_mx(out=kc[a][:, k, cols].bitcast(FP8X4), scales=ks[a][:, k, cols], in_=emb[k, T][:])
+
+        PACKS = ((3,), (0, 2), (1, 5), (4, 6), (7,))
+        PACK_BANK = (6, 0, 1, 7, 2)
+        place = {}
+        for n, pack in enumerate(PACKS):
+            first = 0
+            for T in pack:
+                place[T] = (n, slice(first, first + P * (T % NT + 1)))
+                first = place[T][1].stop
+
+        def scores(n):
+            px[n] = bank(PACK_BANK[n], [P, N], f"px{n}")
+            for T in PACKS[n]:
+                a, j = divmod(T, NT)
+                width = P * (j + 1)
+                x = px[n][:, place[T][1]]
+                rows = slice(P * j, P * (j + 1))
+                cuts = [(0, 256), (256, 384)] if width == 384 else [(0, width)]
+                for lo, hi in cuts:
+                    for s, m in ((BN, AL), (AL, BP)):
+                        nc.tensor.matmul_mx(
+                            out=x[:, lo:hi],
+                            lhsT=kc[a][:, s, rows].bitcast(FP8X4),
+                            lhsT_scale=ks[a][:, s, rows],
+                            rhs=kc[a][:, m, lo:hi].bitcast(FP8X4),
+                            rhs_scale=ks[a][:, m, lo:hi],
+                            start=(s == BN),
+                            stop=(s == AL),
+                        )
+
+        def keep_neg_s(n):
+            neg_s[n] = sb.tile([P, N], F32, name=f"neg_s{n}")
+            nc.vector.tensor_scalar(out=neg_s[n][:], in0=px[n][:], scalar1=-C, scalar2=None, op0=ALU.mult)
+
+        def sigmoid(n):
+            sig[n] = sb.tile([P, N], F32, name=f"sig{n}")
+            nc.scalar.activation(out=sig[n][:], in_=px[n][:], func=ACT.Sigmoid, scale=C)
+
+        def log(n):
+            logs[n] = sb.tile([P, N], F32, name=f"logs{n}")
+            nc.scalar.activation(out=logs[n][:], in_=sig[n][:], func=ACT.Ln, bias=tiny[:])
+
+        def res_tile(T):
+            if T not in res:
+                res[T] = sb.tile([P, N], F32, name=f"res{T}")
+            return res[T]
+
+        def lower(T):
+            n, cols = place[T]
+            nc.vector.scalar_tensor_tensor(
+                out=res_tile(T)[:, 0 : P * (T % NT + 1)],
+                in0=neg_s[n][:, cols], scalar=-1.0, in1=logs[n][:, cols], op0=ALU.mult, op1=ALU.min,
             )
 
-        def XX(a, n):
-            x = px[a, n] = bank((6, 7, 4, 5)[n] if a == 0 else n, [P, N], f"px{a}_{n}")
-            rows = slice(P * n, P * (n + 1))
-            for s, m in ((0, 1), (1, 2)):
-                nc.tensor.matmul_mx(
-                    out=x[:],
-                    lhsT=kc[a][:, s, rows].bitcast(FP8X4),
-                    lhsT_scale=ks[a][:, s, rows],
-                    rhs=kc[a][:, m, :].bitcast(FP8X4),
-                    rhs_scale=ks[a][:, m, :],
-                    start=(s == 0),
-                    stop=(s == 1),
+        def mirror(src, T, first):
+            a, j = divmod(T, NT)
+            for i in range(j):
+                R = a * NT + i
+                if R not in up:
+                    up[R] = bank((3, 4, 5, 0, 0, 6, 1)[R], [P, N - P * (i + 1)], f"up{R}")
+                nc.tensor.matmul(
+                    up[R][:, P * (j - i - 1) : P * (j - i)],
+                    lhsT=src[:, P * i : P * (i + 1)],
+                    rhs=ident[:],
+                    is_transpose=True,
+                    start=(first and j == NT - 1),
+                    stop=(not first and j == i + 1),
                 )
 
-        def SIG(a, n):
-            sig[a, n] = sb.tile([P, N], F32, name=f"sig{a}_{n}")
-            nc.scalar.activation(out=sig[a, n][:], in_=px[a, n][:], func=ACT.Sigmoid, scale=C)
-
-        def col_cuts(a, n):
-            last = (a, n) == (NP - 1, NT - 1)
-            return [slice(0, N // 2), slice(N // 2, N)] if last else [slice(0, N)]
-
-        def LOG(a, n):
-            logs[a, n] = sb.tile([P, N], F32, name=f"logs{a}_{n}")
-            for cut in col_cuts(a, n):
-                nc.scalar.activation(
-                    out=logs[a, n][:, cut], in_=sig[a, n][:, cut], func=ACT.Ln, bias=tiny[:]
-                )
-
-        def FIN(a, n):
-            o = sb.tile([P, N], F32, name=f"o{a}_{n}")
-            for cut in col_cuts(a, n):
-                nc.vector.scalar_tensor_tensor(
-                    out=o[:, cut], in0=px[a, n][:, cut], scalar=C, in1=logs[a, n][:, cut],
-                    op0=ALU.mult, op1=ALU.min,
-                )
-                nc.sync.dma_start(out=out[a, P * n : P * (n + 1), cut], in_=o[:, cut])
-
-        ORDER = (
-            "W0 W1 X0 W2 E0 X1 W3 gP E1 X2 Pa g1 Q0 X3 W4 E2 Ma0 g2 Pb X4 Q2 Q1 Mb0 W5 Ma2 g3 W7 E3 "
-            "Ma1 E4 lam W6 X5 Q3 Mb1 A0 E5 X6 Q4 B1 A2 Ma3 B0 A1 Mb2 E6 Q5 X7 A3 B2 Ma5 N0 E7 Q6 Mb3 "
-            "Ra1 N1 Ma6 A5 B3 Mb5 Q7 Ra0 Mb4 A6 B5 Mb6 Rb0 B4 Rn0 Ma4 Ra3 N3 B6 Rb1 Ma7 Rn1 Rn3 Rb2 "
-            "XX00 A4 Mb7 A7 XX01 S00 Rb3 N2 N4 XX02 B7 Ra4 Ra2 XX03 Rn4 S01 Rn2 Rb4 S02 XX10 S03 XX11 "
-            "S10 XX12 S11 XX13 S12 S13 G00 G01 F00 G02 F01 G03 F02 G10 F03 G11 F10 G12 F11 G13 F12 "
-            "F13 "
-        )
-        steps = {"gP": gate_turn, "g1": gate_out, "g2": gate_exp, "g3": gate_ln, "lam": gate_lam}
-        kinds = {
-            "W": W, "X": X, "E": E, "Q": Q, "A": A, "B": B, "N": NEG,
-            "Ma": lambda T: M(0, T), "Mb": lambda T: M(1, T),
-            "Ra": lambda g: R(0, g), "Rb": lambda g: R(1, g), "Rn": lambda g: R(2, g),
-            "XX": lambda k: XX(k // 10, k % 10), "S": lambda k: SIG(k // 10, k % 10),
-            "G": lambda k: LOG(k // 10, k % 10), "F": lambda k: FIN(k // 10, k % 10),
-        }
-        for step in ORDER.split():
-            if step in steps:
-                steps[step]()
-            elif step in ("Pa", "Pb"):
-                PERM(0 if step == "Pa" else 1)
+        def upper(T, eng):
+            lo = P * (T % NT + 1)
+            if eng == 0:
+                nc.scalar.copy(out=res_tile(T)[:, lo:N], in_=up[T][:])
             else:
-                head = "".join([ch for ch in step if ch not in "0123456789"])
-                kinds[head](int(step[len(head):]))
+                nc.vector.tensor_copy(out=res_tile(T)[:, lo:N], in_=up[T][:])
+
+        def store(T):
+            a, j = divmod(T, NT)
+            nc.sync.dma_start(out=out[a, P * j : P * (j + 1), :], in_=res[T][:])
+
+        LO, HI = range(0, 4), range(4, 8)
+        ON_SCALAR = ()
+        TURNS = {0: (3,), 1: (4, 5), 3: (6, 7)}
+        FILL = ((0,2),(1,1),(2,2),(2,1),(2,1),(2,1),(2,1),(2,0))
+        QUANT = {0: (1,), 1: (2,), 2: (3,), 3: (4,), 4: (5, 6), 5: (7,)}
+        SCORES = {6: (0,), 7: (1,)}
+
+        def at(f, T, *more):
+            if 0 <= T < TILES:
+                f(T, *more)
+
+        def widen_hi(T):
+            if T in ON_SCALAR:
+                widen_plain(T)
+            else:
+                widen(T, HI)
+
+        def second_b(T):
+            negate_b(T)
+            quant_emb(BP, T)
+
+        def second_a(T):
+            quant_emb(AL, T)
+            quant_emb(BN, T)
+
+        filler = []
+        for T in range(3, TILES):
+            filler.append((lambda T: widen(T, LO), T))
+            filler.append((widen_hi, T))
+        for T in range(TILES - 1):
+            filler.append((second_b, T))
+            filler.append((second_a, T))
+
+        def fill(count):
+            for f, T in filler[:count]:
+                f(T)
+            for x in filler[:count]:
+                filler.remove(x)
+
+
+        for T in (0, 1, 2):
+            widen(T, LO)
+            widen_hi(T)
+            turn(T)
+            empty(T)
+
+        permute(WB)
+        quant_h(0)
+        gate_turn()
+        fill(2)
+        permute(WA)
+        gate_z()
+        for s in range(TILES):
+            project(WB, s)
+            at(make_al, s - 1)
+            fill(FILL[s][0])
+            for T in QUANT.get(s, ()):
+                quant_h(T)
+            if s == 0:
+                gate_z2()
+            fill(FILL[s][1])
+            if s == 0:
+                gate_series()
+            project(WA, s)
+            make_b(s)
+            for T in TURNS.get(s, ()):
+                turn(T)
+                empty(T)
+            for n in SCORES.get(s, ()):
+                scores(n)
+                sigmoid(n)
+        fill(len(filler))
+        last = TILES - 1
+        make_al(last)
+        negate_b(last)
+        for k in (BP, AL, BN):
+            quant_emb(k, last)
+        for n in range(len(PACKS)):
+            if n not in px:
+                scores(n)
+                sigmoid(n)
+        for n in range(len(PACKS)):
+            keep_neg_s(n)
+        for a in range(NP):
+            for j in range(NT - 1, 0, -1):
+                n, cols = place[a * NT + j]
+                mirror(neg_s[n][:, cols], a * NT + j, True)
+        for n in (0, 4, 1, 3, 2):
+            log(n)
+        for T in (3, 7, 2, 6, 1, 5):
+            lower(T)
+            mirror(res[T], T, False)
+            if T % NT == NT - 1:
+                store(T)
+        for T in (0, 4):
+            lower(T)
+        for T in (2, 6, 1, 5, 0, 4):
+            upper(T, 0 if T != 4 else 1)
+            store(T)

@@ -66,6 +66,8 @@ def tile_generalpreferenceskewembeddingscores_d2p_kernel(
             nc.vector.memset(s_raw[w][:].rearrange("p g k -> p (g k)").bitcast(I32), 0)
         nc.vector.memset(gate_rows[:], 0.0)
         nc.vector.memset(tiny[:], TINY)
+        zeros = sb.tile([P, N], BF16, name="zeros")
+        nc.vector.memset(zeros[:], 0.0)
         nc.vector.memset(factor[:, :, 0:1], 0.0)
         nc.vector.tensor_scalar(out=half_odd[:], in0=odd[:], scalar1=0.5, scalar2=None, op0=ALU.mult)
         nc.vector.tensor_scalar(
@@ -131,6 +133,11 @@ def tile_generalpreferenceskewembeddingscores_d2p_kernel(
             nc.scalar.activation(out=z_pos[:], in_=pg[:], func=ACT.Sigmoid, scale=1.0, bias=neg_ln2[:])
             nc.scalar.activation(out=z_neg[:], in_=pg[:], func=ACT.Sigmoid, scale=-1.0, bias=neg_ln2[:])
             nc.scalar.activation(out=addend[:, :, TERMS], in_=pg[:], func=ACT.Relu)
+
+        def warm(count):
+            for i in range(count):
+                wp = bank(4, [P, N], "warm")
+                nc.tensor.matmul(wp[:], lhsT=zeros[:, 0:P], rhs=zeros[:], start=True, stop=True)
 
         def gate_z():
             nc.vector.tensor_tensor(out=factor[:, :, TERMS], in0=z_pos[:], in1=z_neg[:], op=ALU.min)
@@ -288,20 +295,21 @@ def tile_generalpreferenceskewembeddingscores_d2p_kernel(
             sig[n] = sb.tile([P, N], F32, name=f"sig{n}")
             nc.scalar.activation(out=sig[n][:], in_=px[n][:], func=ACT.Sigmoid, scale=C)
 
-        def log(n):
-            logs[n] = sb.tile([P, N], F32, name=f"logs{n}")
-            nc.scalar.activation(out=logs[n][:], in_=sig[n][:], func=ACT.Ln, bias=tiny[:])
+        def log(n, cols):
+            if n not in logs:
+                logs[n] = sb.tile([P, N], F32, name=f"logs{n}")
+            nc.scalar.activation(out=logs[n][:, cols], in_=sig[n][:, cols], func=ACT.Ln, bias=tiny[:])
 
         def res_tile(T):
             if T not in res:
                 res[T] = sb.tile([P, N], F32, name=f"res{T}")
             return res[T]
 
-        def lower(T):
+        def lower(T, part):
             n, cols = place[T]
             nc.vector.scalar_tensor_tensor(
-                out=res_tile(T)[:, 0 : P * (T % NT + 1)],
-                in0=neg_s[n][:, cols], scalar=-1.0, in1=logs[n][:, cols], op0=ALU.mult, op1=ALU.min,
+                out=res_tile(T)[:, part],
+                in0=neg_s[n][:, cols][:, part], scalar=-1.0, in1=logs[n][:, cols][:, part], op0=ALU.mult, op1=ALU.min,
             )
 
         def mirror(src, T, first):
@@ -326,12 +334,12 @@ def tile_generalpreferenceskewembeddingscores_d2p_kernel(
             else:
                 nc.vector.tensor_copy(out=res_tile(T)[:, lo:N], in_=up[T][:])
 
-        def store(T):
+        def store(T, part):
             a, j = divmod(T, NT)
-            nc.sync.dma_start(out=out[a, P * j : P * (j + 1), :], in_=res[T][:])
+            nc.sync.dma_start(out=out[a, P * j : P * (j + 1), part], in_=res[T][:, part])
 
         LO, HI = range(0, 4), range(4, 8)
-        ON_SCALAR = ()
+        ON_SCALAR = (3,4,5,6,7)
         TURNS = {0: (3,), 1: (4, 5), 3: (6, 7)}
         FILL = ((0,2),(1,1),(2,2),(2,1),(2,1),(2,1),(2,1),(2,0))
         QUANT = {0: (1,), 1: (2,), 2: (3,), 3: (4,), 4: (5, 6), 5: (7,)}
@@ -369,13 +377,14 @@ def tile_generalpreferenceskewembeddingscores_d2p_kernel(
             for x in filler[:count]:
                 filler.remove(x)
 
-
+        nc.scalar.activation(out=z_pos[:, 0:1], in_=tiny[:], func=ACT.Sigmoid)
+        warm(3)
         for T in (0, 1, 2):
             widen(T, LO)
             widen_hi(T)
             turn(T)
             empty(T)
-
+            warm(1)
         permute(WB)
         quant_h(0)
         gate_turn()
@@ -417,15 +426,21 @@ def tile_generalpreferenceskewembeddingscores_d2p_kernel(
             for j in range(NT - 1, 0, -1):
                 n, cols = place[a * NT + j]
                 mirror(neg_s[n][:, cols], a * NT + j, True)
-        for n in (0, 4, 1, 3, 2):
-            log(n)
-        for T in (3, 7, 2, 6, 1, 5):
-            lower(T)
+        whole = slice(0, N)
+        for half in (slice(0, N // 2), slice(N // 2, N)):
+            log(0, half)
+            lower(3, half)
+            store(3, half)
+        mirror(res[3], 3, False)
+        for n in (4, 1, 3, 2):
+            log(n, whole)
+        for T in (7, 2, 6, 1, 5):
+            lower(T, slice(0, P * (T % NT + 1)))
             mirror(res[T], T, False)
             if T % NT == NT - 1:
-                store(T)
+                store(T, whole)
         for T in (0, 4):
-            lower(T)
+            lower(T, slice(0, P))
         for T in (2, 6, 1, 5, 0, 4):
             upper(T, 0 if T != 4 else 1)
-            store(T)
+            store(T, whole)

@@ -49,6 +49,7 @@ def tile_generalpreferenceskewembeddingscores_d2p_kernel(
         s_raw = [sb.tile([P, G, K], U8, name=f"s_raw{w}", align_bytes=64) for w in range(2)]
         s_perm = [sb.tile([P, G, 4, P], U8, name=f"s_perm{w}", align_bytes=64) for w in range(2)]
         scales = sb.tile([P, TILES * 8], F32, name="scales")
+        scale_col = sb.tile([P, 1], F32, name="scale_col")
         tiny = sb.tile([P, 1], F32, name="tiny")
 
         odd = sb.tile([P, NP * 4, TERMS], F32, name="odd")
@@ -64,17 +65,12 @@ def tile_generalpreferenceskewembeddingscores_d2p_kernel(
         make_identity(nc, ident[:])
         for w in range(2):
             nc.vector.memset(s_raw[w][:].rearrange("p g k -> p (g k)").bitcast(I32), 0)
-        nc.vector.memset(gate_rows[:], 0.0)
+        nc.vector.memset(gate_rows[0 : P - 4, :], 0.0)
+        nc.vector.memset(scale_col[TILES * 8 : P, :], 0.0)
         nc.vector.memset(tiny[:], TINY)
         zeros = sb.tile([P, N], BF16, name="zeros")
         nc.vector.memset(zeros[:], 0.0)
         nc.vector.memset(factor[:, :, 0:1], 0.0)
-        nc.vector.tensor_scalar(out=half_odd[:], in0=odd[:], scalar1=0.5, scalar2=None, op0=ALU.mult)
-        nc.vector.tensor_scalar(
-            out=neg_ln2[:], in0=odd[:, 0, TERMS - 1 : TERMS], scalar1=-math.log(2.0), scalar2=None, op0=ALU.mult
-        )
-        nc.vector.reciprocal(out=addend[:, :, 0:TERMS], in_=half_odd[:])
-        nc.vector.tensor_copy(out=pick4[:], in_=ident[:, 0:4])
 
         codes_in = {}
 
@@ -100,16 +96,14 @@ def tile_generalpreferenceskewembeddingscores_d2p_kernel(
                 queue.dma_start(out=d[32 * q : 32 * q + 4], in_=v[q])
 
         load_h(0, 0, 1)
+        nc.scalar.dma_start(out=scale_col[0 : TILES * 8, :], in_=h_scale.rearrange("a i (j o) -> (a i j) o", o=1))
         nc.scalar.dma_start(
-            out=scales[:], in_=h_scale.rearrange("a i j -> (a i j)").partition_broadcast(P)
+            out=gate_rows[P - 4 : P, :].rearrange("t (q r) -> t q r", r=8),
+            in_=gate.rearrange("a (q t r) -> t (a q) r", t=4, r=8),
         )
         load_h(0, 1, 3)
         load_words(WB, wb_words)
-        load_scale_rows(WB, wb_scales, nc.scalar)
-        nc.sync.dma_start(
-            out=gate_rows[0:4, :].rearrange("t (q r) -> t q r", r=8),
-            in_=gate.rearrange("a (q t r) -> t (a q) r", t=4, r=8),
-        )
+        load_scale_rows(WB, wb_scales, nc.sync)
         load_words(WA, wa_words)
         load_scale_rows(WA, wa_scales, nc.sync)
         load_h(1, 0, 4)
@@ -138,6 +132,19 @@ def tile_generalpreferenceskewembeddingscores_d2p_kernel(
             for i in range(count):
                 wp = bank(4, [P, N], "warm")
                 nc.tensor.matmul(wp[:], lhsT=zeros[:, 0:P], rhs=zeros[:], start=True, stop=True)
+
+        def spread_scales():
+            sp = bank(3, [P, P], "spread")
+            nc.tensor.transpose(sp[:], scale_col[:].to_broadcast([P, P]), ident[:])
+            nc.vector.tensor_copy(out=scales[:], in_=sp[:, 0 : TILES * 8])
+
+        def gate_constants():
+            nc.vector.tensor_scalar(out=half_odd[:], in0=odd[:], scalar1=0.5, scalar2=None, op0=ALU.mult)
+            nc.vector.tensor_scalar(
+                out=neg_ln2[:], in0=odd[:, 0, TERMS - 1 : TERMS], scalar1=-math.log(2.0), scalar2=None, op0=ALU.mult
+            )
+            nc.vector.reciprocal(out=addend[:, :, 0:TERMS], in_=half_odd[:])
+            nc.vector.tensor_copy(out=pick4[:], in_=ident[:, P - 4 : P])
 
         def gate_z():
             nc.vector.tensor_tensor(out=factor[:, :, TERMS], in0=z_pos[:], in1=z_neg[:], op=ALU.min)
@@ -378,30 +385,36 @@ def tile_generalpreferenceskewembeddingscores_d2p_kernel(
                 filler.remove(x)
 
         nc.scalar.activation(out=z_pos[:, 0:1], in_=tiny[:], func=ACT.Sigmoid)
-        warm(3)
-        for T in (0, 1, 2):
-            widen(T, LO)
-            widen_hi(T)
-            turn(T)
-            empty(T)
-            warm(1)
+        warm(1)
+        gate_constants()
+        spread_scales()
+        warm(2)
+        widen(0, range(8))
+        turn(0)
+        warm(1)
+        empty(0)
+        widen(1, range(8))
+        turn(1)
+        gate_turn()
+        empty(1)
+        warm(1)
+        widen(2, range(8))
+        turn(2)
+        empty(2)
         permute(WB)
         quant_h(0)
-        gate_turn()
-        fill(2)
-        permute(WA)
         gate_z()
+        fill(2)
+        gate_z2()
+        permute(WA)
+        gate_series()
         for s in range(TILES):
             project(WB, s)
             at(make_al, s - 1)
             fill(FILL[s][0])
             for T in QUANT.get(s, ()):
                 quant_h(T)
-            if s == 0:
-                gate_z2()
             fill(FILL[s][1])
-            if s == 0:
-                gate_series()
             project(WA, s)
             make_b(s)
             for T in TURNS.get(s, ()):

@@ -58,18 +58,20 @@ def tile_generalpreferenceskewembeddingscores_d2p_kernel(
         factor = sb.tile([P, NP * 4, TERMS + 1], F32, name="factor")
         addend = sb.tile([P, NP * 4, TERMS + 1], F32, name="addend")
 
+        zeros = sb.tile([P, N], BF16, name="zeros")
+        nc.vector.memset(zeros[:], 0.0)
+        nc.vector.memset(ident[:], 0.0)
+        make_identity(nc, ident[:], nomemset=True)
         nc.gpsimd.iota(
             odd[:], pattern=[[0, NP * 4], [-2, TERMS]], base=2 * TERMS - 1, channel_multiplier=0,
             allow_small_or_imprecise_dtypes=True,
         )
-        make_identity(nc, ident[:])
         for w in range(2):
             nc.vector.memset(s_raw[w][:].rearrange("p g k -> p (g k)").bitcast(I32), 0)
         nc.vector.memset(gate_rows[0 : P - 4, :], 0.0)
         nc.vector.memset(scale_col[TILES * 8 : P, :], 0.0)
         nc.vector.memset(tiny[:], TINY)
-        zeros = sb.tile([P, N], BF16, name="zeros")
-        nc.vector.memset(zeros[:], 0.0)
+
         nc.vector.memset(factor[:, :, 0:1], 0.0)
 
         codes_in = {}
@@ -95,8 +97,8 @@ def tile_generalpreferenceskewembeddingscores_d2p_kernel(
             for q in range(4):
                 queue.dma_start(out=d[32 * q : 32 * q + 4], in_=v[q])
 
-        load_h(0, 0, 1)
         nc.scalar.dma_start(out=scale_col[0 : TILES * 8, :], in_=h_scale.rearrange("a i (j o) -> (a i j) o", o=1))
+        load_h(0, 0, 1)
         nc.scalar.dma_start(
             out=gate_rows[P - 4 : P, :].rearrange("t (q r) -> t q r", r=8),
             in_=gate.rearrange("a (q t r) -> t (a q) r", t=4, r=8),
@@ -104,9 +106,10 @@ def tile_generalpreferenceskewembeddingscores_d2p_kernel(
         load_h(0, 1, 3)
         load_words(WB, wb_words)
         load_scale_rows(WB, wb_scales, nc.sync)
+        load_h(1, 0, 2)
         load_words(WA, wa_words)
         load_scale_rows(WA, wa_scales, nc.sync)
-        load_h(1, 0, 4)
+        load_h(1, 2, 2)
 
         wide_hi = {}
         wide, pt, hg, hc, hs, prod, emb = {}, {}, {}, {}, {}, {}, {}
@@ -346,11 +349,11 @@ def tile_generalpreferenceskewembeddingscores_d2p_kernel(
             nc.sync.dma_start(out=out[a, P * j : P * (j + 1), part], in_=res[T][:, part])
 
         LO, HI = range(0, 4), range(4, 8)
-        ON_SCALAR = (3,4,5,6,7)
-        TURNS = {0: (3,), 1: (4, 5), 3: (6, 7)}
-        FILL = ((0,2),(1,1),(2,2),(2,1),(2,1),(2,1),(2,1),(2,0))
-        QUANT = {0: (1,), 1: (2,), 2: (3,), 3: (4,), 4: (5, 6), 5: (7,)}
-        SCORES = {6: (0,), 7: (1,)}
+        ON_SCALAR = (1,2)
+        TURNS = {1: (3, 4, 5), 3: (6, 7)}
+        FILL = ((1,2),(2,0),(0,3),(2,1),(2,1),(2,1),(1,1),(2,0))
+        QUANT = {0: (2,), 2: (3,), 3: (4, 5), 4: (6,), 5: (7,)}
+        SCORES = {7: (1,)}
 
         def at(f, T, *more):
             if 0 <= T < TILES:
@@ -389,24 +392,28 @@ def tile_generalpreferenceskewembeddingscores_d2p_kernel(
         gate_constants()
         spread_scales()
         warm(2)
-        widen(0, range(8))
+        for T in (0, 1, 2):
+            widen(T, LO)
+            widen_hi(T)
         turn(0)
         warm(1)
         empty(0)
-        widen(1, range(8))
         turn(1)
-        gate_turn()
-        empty(1)
         warm(1)
-        widen(2, range(8))
-        turn(2)
-        empty(2)
+        empty(1)
         permute(WB)
+        turn(2)
+        gate_turn()
+        fill(1)
         quant_h(0)
-        gate_z()
-        fill(2)
-        gate_z2()
+        warm(0)
+        empty(2)
+        fill(1)
         permute(WA)
+        gate_z()
+        quant_h(1)
+        gate_z2()
+        fill(1)
         gate_series()
         for s in range(TILES):
             project(WB, s)
@@ -415,8 +422,13 @@ def tile_generalpreferenceskewembeddingscores_d2p_kernel(
             for T in QUANT.get(s, ()):
                 quant_h(T)
             fill(FILL[s][1])
+            if s == TILES - 1:
+                make_b(s)
+                scores(0)
+                sigmoid(0)
             project(WA, s)
-            make_b(s)
+            if s < TILES - 1:
+                make_b(s)
             for T in TURNS.get(s, ()):
                 turn(T)
                 empty(T)
@@ -425,10 +437,11 @@ def tile_generalpreferenceskewembeddingscores_d2p_kernel(
                 sigmoid(n)
         fill(len(filler))
         last = TILES - 1
-        make_al(last)
         negate_b(last)
-        for k in (BP, AL, BN):
-            quant_emb(k, last)
+        quant_emb(BP, last)
+        make_al(last)
+        quant_emb(BN, last)
+        quant_emb(AL, last)
         for n in range(len(PACKS)):
             if n not in px:
                 scores(n)
@@ -440,20 +453,29 @@ def tile_generalpreferenceskewembeddingscores_d2p_kernel(
                 n, cols = place[a * NT + j]
                 mirror(neg_s[n][:, cols], a * NT + j, True)
         whole = slice(0, N)
-        for half in (slice(0, N // 2), slice(N // 2, N)):
-            log(0, half)
-            lower(3, half)
-            store(3, half)
-        mirror(res[3], 3, False)
-        for n in (4, 1, 3, 2):
-            log(n, whole)
-        for T in (7, 2, 6, 1, 5):
-            lower(T, slice(0, P * (T % NT + 1)))
+        for T in (3, 7):
+            for half in (slice(0, N // 2), slice(N // 2, N)):
+                log(place[T][0], half)
+                lower(T, half)
+                store(T, half)
             mirror(res[T], T, False)
-            if T % NT == NT - 1:
-                store(T, whole)
+        for T in (2, 6):
+            log(*place[T])
+        log(2, whole)
+        for T in (0, 4):
+            log(*place[T])
+        for T in (2, 6):
+            lower(T, slice(0, 3 * P))
+            upper(T, 1)
+            store(T, whole)
+            mirror(res[T], T, False)
+        for T in (1, 5):
+            lower(T, slice(0, 2 * P))
+            mirror(res[T], T, False)
+            upper(T, 0)
+            store(T, whole)
         for T in (0, 4):
             lower(T, slice(0, P))
-        for T in (2, 6, 1, 5, 0, 4):
+        for T in (0, 4):
             upper(T, 0 if T != 4 else 1)
             store(T, whole)

@@ -41,9 +41,10 @@ def tile_generalpreferenceskewembeddingscores_d2p_kernel(
         def bank(b, shape, name):
             return ps.tile(shape, F32, name=name, tag=f"bank{b}")
 
-        gate_rows = sb.tile([P, NP * P], BF16, name="gate_rows")
+        gate_in = sb.tile([P, K], BF16, name="gate_in")
+        gate_rows = sb.tile([P, K], BF16, name="gate_rows")
         ident = sb.tile([P, P], F32, name="ident")
-        pick4 = sb.tile([P, 4], BF16, name="pick4")
+        pick = sb.tile([P, NP], BF16, name="pick")
         w_raw = [sb.tile([P, G, 1024], U8, name=f"w_raw{w}", align_bytes=64) for w in range(2)]
         w_perm = [sb.tile([P, G, 4, 256], U8, name=f"w_perm{w}", align_bytes=64) for w in range(2)]
         s_raw = [sb.tile([P, G, K], U8, name=f"s_raw{w}", align_bytes=64) for w in range(2)]
@@ -68,7 +69,7 @@ def tile_generalpreferenceskewembeddingscores_d2p_kernel(
         )
         for w in range(2):
             nc.vector.memset(s_raw[w][:].rearrange("p g k -> p (g k)").bitcast(I32), 0)
-        nc.vector.memset(gate_rows[0 : P - 4, :], 0.0)
+        nc.vector.memset(gate_rows[:], 0.0)
         nc.vector.memset(scale_col[TILES * 8 : P, :], 0.0)
         nc.vector.memset(tiny[:], TINY)
 
@@ -99,10 +100,7 @@ def tile_generalpreferenceskewembeddingscores_d2p_kernel(
 
         nc.scalar.dma_start(out=scale_col[0 : TILES * 8, :], in_=h_scale.rearrange("a i (j o) -> (a i j) o", o=1))
         load_h(0, 0, 1)
-        nc.scalar.dma_start(
-            out=gate_rows[P - 4 : P, :].rearrange("t (q r) -> t q r", r=8),
-            in_=gate.rearrange("a (q t r) -> t (a q) r", t=4, r=8),
-        )
+        nc.scalar.dma_start(out=gate_in[0:NP, :], in_=gate)
         load_h(0, 1, 3)
         load_words(WB, wb_words)
         load_scale_rows(WB, wb_scales, nc.sync)
@@ -123,9 +121,9 @@ def tile_generalpreferenceskewembeddingscores_d2p_kernel(
 
         def gate_turn():
             pg = bank(5, [P, NP * 4], "pg")
-            for a in range(NP):
+            for t in range(4):
                 nc.tensor.matmul(
-                    pg[:, 4 * a : 4 * a + 4], lhsT=gate_rows[:, P * a : P * (a + 1)], rhs=pick4[:], start=True, stop=True
+                    pg[:, NP * t : NP * (t + 1)], lhsT=gate_rows[:, P * t : P * (t + 1)], rhs=pick[:], start=True, stop=True
                 )
             nc.scalar.activation(out=z_pos[:], in_=pg[:], func=ACT.Sigmoid, scale=1.0, bias=neg_ln2[:])
             nc.scalar.activation(out=z_neg[:], in_=pg[:], func=ACT.Sigmoid, scale=-1.0, bias=neg_ln2[:])
@@ -147,7 +145,13 @@ def tile_generalpreferenceskewembeddingscores_d2p_kernel(
                 out=neg_ln2[:], in0=odd[:, 0, TERMS - 1 : TERMS], scalar1=-math.log(2.0), scalar2=None, op0=ALU.mult
             )
             nc.vector.reciprocal(out=addend[:, :, 0:TERMS], in_=half_odd[:])
-            nc.vector.tensor_copy(out=pick4[:], in_=ident[:, P - 4 : P])
+            nc.vector.tensor_copy(out=pick[:], in_=ident[:, 0:NP])
+
+        def gate_order():
+            nc.scalar.copy(
+                out=gate_rows[0:NP, :].rearrange("a (t q r) -> a t q r", t=4, r=8),
+                in_=gate_in[0:NP, :].rearrange("a (q t r) -> a t q r", t=4, r=8),
+            )
 
         def gate_z():
             nc.vector.tensor_tensor(out=factor[:, :, TERMS], in0=z_pos[:], in1=z_neg[:], op=ALU.min)
@@ -165,7 +169,7 @@ def tile_generalpreferenceskewembeddingscores_d2p_kernel(
                 op0=ALU.mult,
                 op1=ALU.add,
             )
-            nc.scalar.copy(out=lam[:].rearrange("p a t -> p (a t)"), in_=horner[:, :, TERMS])
+            nc.scalar.copy(out=lam[:], in_=horner[:, :, TERMS].rearrange("p (t a) -> p a t", a=NP))
 
         def widen(T, blocks):
             t, i = codes_in[T]
@@ -241,13 +245,18 @@ def tile_generalpreferenceskewembeddingscores_d2p_kernel(
                     )
 
         def emb_tile(k, T):
-            emb[k, T] = sb.tile([P, 512], BF16, name=f"emb{k}_{T}", align_bytes=64)
-            return emb[k, T]
+            if (k, T // 2) not in emb:
+                emb[k, T // 2] = sb.tile([P, 2, 512], BF16, name=f"emb{k}_{T // 2}", align_bytes=64)
+            return emb[k, T // 2][:, T % 2, :]
+
+        def emb_run(k, T, count):
+            emb_tile(k, T)
+            return emb[k, T // 2][:, T % 2 : T % 2 + count, :].rearrange("p i n -> p (i n)")
 
         def make_al(T):
             a = T // NT
             nc.vector.tensor_tensor(
-                out=emb_tile(AL, T)[:].rearrange("p (n t) -> p n t", t=4),
+                out=emb_tile(AL, T).rearrange("p (n t) -> p n t", t=4),
                 in0=prod[WA, T][:].rearrange("p t n -> p n t"),
                 in1=lam[:, a : a + 1, :].to_broadcast([P, P, 4]),
                 op=ALU.mult,
@@ -255,18 +264,20 @@ def tile_generalpreferenceskewembeddingscores_d2p_kernel(
 
         def make_b(T):
             nc.scalar.copy(
-                out=emb_tile(BP, T)[:].rearrange("p (n t) -> p n t", t=4),
+                out=emb_tile(BP, T).rearrange("p (n t) -> p n t", t=4),
                 in_=prod[WB, T][:].rearrange("p t n -> p n t"),
             )
 
-        def negate_b(T):
+        def negate_b(T, count):
             nc.vector.tensor_scalar(
-                out=emb_tile(BN, T)[:], in0=emb[BP, T][:], scalar1=-1.0, scalar2=None, op0=ALU.mult
+                out=emb_run(BN, T, count), in0=emb_run(BP, T, count), scalar1=-1.0, scalar2=None, op0=ALU.mult
             )
 
-        def quant_emb(k, T):
-            a, cols = T // NT, slice(P * (T % NT), P * (T % NT + 1))
-            nc.vector.quantize_mx(out=kc[a][:, k, cols].bitcast(FP8X4), scales=ks[a][:, k, cols], in_=emb[k, T][:])
+        def quant_emb(k, T, count):
+            a, cols = T // NT, slice(P * (T % NT), P * (T % NT + count))
+            nc.vector.quantize_mx(
+                out=kc[a][:, k, cols].bitcast(FP8X4), scales=ks[a][:, k, cols], in_=emb_run(k, T, count)
+            )
 
         PACKS = ((3,), (0, 2), (1, 5), (4, 6), (7,))
         PACK_BANK = (6, 0, 1, 7, 2)
@@ -349,9 +360,9 @@ def tile_generalpreferenceskewembeddingscores_d2p_kernel(
             nc.sync.dma_start(out=out[a, P * j : P * (j + 1), part], in_=res[T][:, part])
 
         LO, HI = range(0, 4), range(4, 8)
-        ON_SCALAR = (1,2)
+        ON_SCALAR = (1,2,5,6,7)
         TURNS = {1: (3, 4, 5), 3: (6, 7)}
-        FILL = ((1,2),(2,0),(0,3),(2,1),(2,1),(2,1),(1,1),(2,0))
+        FILL = ((1,2),(2,0),(0,2),(1,1),(1,0),(1,0),(1,0),(2,0))
         QUANT = {0: (2,), 2: (3,), 3: (4, 5), 4: (6,), 5: (7,)}
         SCORES = {7: (1,)}
 
@@ -365,19 +376,22 @@ def tile_generalpreferenceskewembeddingscores_d2p_kernel(
             else:
                 widen(T, HI)
 
+        def run(T):
+            return 2 if T < TILES - 2 else 1
+
         def second_b(T):
-            negate_b(T)
-            quant_emb(BP, T)
+            negate_b(T, run(T))
+            quant_emb(BP, T, run(T))
 
         def second_a(T):
-            quant_emb(AL, T)
-            quant_emb(BN, T)
+            quant_emb(AL, T, run(T))
+            quant_emb(BN, T, run(T))
 
         filler = []
         for T in range(3, TILES):
             filler.append((lambda T: widen(T, LO), T))
             filler.append((widen_hi, T))
-        for T in range(TILES - 1):
+        for T in range(0, TILES - 1, 2):
             filler.append((second_b, T))
             filler.append((second_a, T))
 
@@ -389,6 +403,7 @@ def tile_generalpreferenceskewembeddingscores_d2p_kernel(
 
         nc.scalar.activation(out=z_pos[:, 0:1], in_=tiny[:], func=ACT.Sigmoid)
         warm(1)
+        gate_order()
         gate_constants()
         spread_scales()
         warm(2)
@@ -437,11 +452,11 @@ def tile_generalpreferenceskewembeddingscores_d2p_kernel(
                 sigmoid(n)
         fill(len(filler))
         last = TILES - 1
-        negate_b(last)
-        quant_emb(BP, last)
+        negate_b(last, 1)
+        quant_emb(BP, last, 1)
         make_al(last)
-        quant_emb(BN, last)
-        quant_emb(AL, last)
+        quant_emb(BN, last, 1)
+        quant_emb(AL, last, 1)
         for n in range(len(PACKS)):
             if n not in px:
                 scores(n)

@@ -101,22 +101,23 @@ def tile_generalpreferenceskewembeddingscores_d2p_kernel(
         nc.scalar.dma_start(out=scale_col[0 : TILES * 8, :], in_=h_scale.rearrange("a i (j o) -> (a i j) o", o=1))
         load_h(0, 0, 1)
         nc.scalar.dma_start(out=gate_in[0:NP, :], in_=gate)
-        load_h(0, 1, 3)
+        load_h(0, 1, 1)
+        load_h(0, 2, 2)
         load_words(WB, wb_words)
         load_scale_rows(WB, wb_scales, nc.sync)
-        load_h(1, 0, 2)
         load_words(WA, wa_words)
         load_scale_rows(WA, wa_scales, nc.sync)
+        load_h(1, 0, 2)
         load_h(1, 2, 2)
 
-        wide_hi = {}
+        plain = {}
         wide, pt, hg, hc, hs, prod, emb = {}, {}, {}, {}, {}, {}, {}
         kc = [sb.tile([P, 3, N], U32, name=f"kc{a}", align_bytes=64) for a in range(NP)]
         ks = [sb.tile([P, 3, N], U8, name=f"ks{a}", align_bytes=64) for a in range(NP)]
         px, neg_s, sig, logs, res, up = {}, {}, {}, {}, {}, {}
         lam = sb.tile([P, NP, 4], F32, name="lam")
-        z_pos = sb.tile([P, NP * 4], F32, name="z_pos")
-        z_neg = sb.tile([P, NP * 4], F32, name="z_neg")
+        g_abs = sb.tile([P, NP * 4], F32, name="g_abs")
+        preload = sb.tile([P, 1], F32, name="preload")
         horner = sb.tile([P, NP * 4, TERMS + 1], F32, name="horner")
 
         def gate_turn():
@@ -125,9 +126,13 @@ def tile_generalpreferenceskewembeddingscores_d2p_kernel(
                 nc.tensor.matmul(
                     pg[:, NP * t : NP * (t + 1)], lhsT=gate_rows[:, P * t : P * (t + 1)], rhs=pick[:], start=True, stop=True
                 )
-            nc.scalar.activation(out=z_pos[:], in_=pg[:], func=ACT.Sigmoid, scale=1.0, bias=neg_ln2[:])
-            nc.scalar.activation(out=z_neg[:], in_=pg[:], func=ACT.Sigmoid, scale=-1.0, bias=neg_ln2[:])
+            nc.scalar.activation(out=g_abs[:], in_=pg[:], func=ACT.Abs)
             nc.scalar.activation(out=addend[:, :, TERMS], in_=pg[:], func=ACT.Relu)
+            nc.scalar.activation(out=factor[:, :, TERMS], in_=g_abs[:], func=ACT.Sigmoid, scale=-1.0, bias=neg_ln2[:])
+
+        def gate_square():
+            z = factor[:, :, TERMS : TERMS + 1].to_broadcast([P, NP * 4, TERMS - 1])
+            nc.scalar.activation(out=factor[:, :, 1:TERMS], in_=z, func=ACT.Square)
 
         def warm(count):
             for i in range(count):
@@ -152,13 +157,6 @@ def tile_generalpreferenceskewembeddingscores_d2p_kernel(
                 out=gate_rows[0:NP, :].rearrange("a (t q r) -> a t q r", t=4, r=8),
                 in_=gate_in[0:NP, :].rearrange("a (q t r) -> a t q r", t=4, r=8),
             )
-
-        def gate_z():
-            nc.vector.tensor_tensor(out=factor[:, :, TERMS], in0=z_pos[:], in1=z_neg[:], op=ALU.min)
-
-        def gate_z2():
-            z = factor[:, :, TERMS : TERMS + 1].to_broadcast([P, NP * 4, TERMS - 1])
-            nc.vector.tensor_tensor(out=factor[:, :, 1:TERMS], in0=z, in1=z, op=ALU.mult)
 
         def gate_series():
             nc.vector.tensor_tensor_scan(
@@ -186,39 +184,40 @@ def tile_generalpreferenceskewembeddingscores_d2p_kernel(
                     op0=ALU.mult,
                 )
 
-        def widen_plain(T):
+        def widen_plain(T, g):
             t, i = codes_in[T]
-            wide_hi[T] = sb.tile([P, 512], BF16, name=f"wide_hi{T}", align_bytes=64)
-            for j in range(4, 8):
+            plain[T, g] = sb.tile([P, 512], BF16, name=f"plain{T}_{g}", align_bytes=64)
+            for j in range(4 * g, 4 * g + 4):
                 nc.scalar.activation(
-                    out=wide_hi[T][:, P * (j - 4) : P * (j - 3)],
+                    out=plain[T, g][:, P * (j % 4) : P * (j % 4 + 1)],
                     in_=t[:, i, P * j : P * (j + 1)].bitcast(FP8),
                     func=ACT.Copy,
                     scale=scales[:, 8 * T + j : 8 * T + j + 1],
                 )
 
-        def turn(T):
-            pt[T] = bank((0, 1, 6, 7)[T % 4], [P, 2 * G, P], f"pt{T}")
-            words = wide[T][:].bitcast(F32)
-            for g in range(G):
+        def turn(T, passes, b):
+            pt[T, passes] = bank(b, [P, 2 * len(passes), P], f"pt{T}_{passes[0]}")
+            for n, g in enumerate(passes):
                 for u in range(2):
-                    if g == 1 and T in wide_hi:
-                        src = wide_hi[T][:].bitcast(F32)[:, u : 256 : 2]
+                    if (T, g) in plain:
+                        src = plain[T, g][:].bitcast(F32)[:, u : 256 : 2]
                     else:
-                        src = words[:, 256 * g + P * u : 256 * g + P * (u + 1)]
-                    nc.tensor.transpose(pt[T][:, 2 * g + u, :], src, ident[:])
+                        src = wide[T][:].bitcast(F32)[:, 256 * g + P * u : 256 * g + P * (u + 1)]
+                    nc.tensor.transpose(pt[T, passes][:, 2 * n + u, :], src, ident[:])
 
-        def empty(T):
-            hg[T] = sb.tile([P, G * P * 4], BF16, name=f"hg{T}", align_bytes=64)
+        def empty(T, passes):
+            hg[T, passes] = sb.tile([P, len(passes) * P * 4], BF16, name=f"hg{T}_{passes[0]}", align_bytes=64)
             nc.scalar.copy(
-                out=hg[T][:].bitcast(F32).rearrange("p (g n u) -> p g n u", g=G, u=2),
-                in_=pt[T][:].rearrange("p (g u) n -> p g n u", g=G),
+                out=hg[T, passes][:].bitcast(F32).rearrange("p (g n u) -> p g n u", n=P, u=2),
+                in_=pt[T, passes][:].rearrange("p (g u) n -> p g n u", u=2),
             )
 
-        def quant_h(T):
-            hc[T] = sb.tile([P, G * P], U32, name=f"hc{T}", align_bytes=64)
-            hs[T] = sb.tile([P, G * P], U8, name=f"hs{T}", align_bytes=64)
-            nc.vector.quantize_mx(out=hc[T][:].bitcast(FP8X4), scales=hs[T][:], in_=hg[T][:])
+        def quant_h(T, passes):
+            if T not in hc:
+                hc[T] = sb.tile([P, G * P], U32, name=f"hc{T}", align_bytes=64)
+                hs[T] = sb.tile([P, G * P], U8, name=f"hs{T}", align_bytes=64)
+            cols = slice(P * passes[0], P * (passes[-1] + 1))
+            nc.vector.quantize_mx(out=hc[T][:, cols].bitcast(FP8X4), scales=hs[T][:, cols], in_=hg[T, passes][:])
 
         def permute(w):
             for dst, src, x in (
@@ -266,6 +265,14 @@ def tile_generalpreferenceskewembeddingscores_d2p_kernel(
             nc.scalar.copy(
                 out=emb_tile(BP, T).rearrange("p (n t) -> p n t", t=4),
                 in_=prod[WB, T][:].rearrange("p t n -> p n t"),
+            )
+
+        def make_neg_b(T):
+            nc.scalar.activation(
+                out=emb_tile(BN, T).rearrange("p (n t) -> p n t", t=4),
+                in_=prod[WB, T][:].rearrange("p t n -> p n t"),
+                func=ACT.Copy,
+                scale=-1.0,
             )
 
         def negate_b(T, count):
@@ -359,108 +366,121 @@ def tile_generalpreferenceskewembeddingscores_d2p_kernel(
             a, j = divmod(T, NT)
             nc.sync.dma_start(out=out[a, P * j : P * (j + 1), part], in_=res[T][:, part])
 
-        LO, HI = range(0, 4), range(4, 8)
-        ON_SCALAR = (1,2,5,6,7)
-        TURNS = {1: (3, 4, 5), 3: (6, 7)}
-        FILL = ((1,2),(2,0),(0,2),(1,1),(1,0),(1,0),(1,0),(2,0))
-        QUANT = {0: (2,), 2: (3,), 3: (4, 5), 4: (6,), 5: (7,)}
-        SCORES = {7: (1,)}
+        ON_SCALAR = ((1, 1), (2, 1), (5, 1), (6, 1), (7, 1))
+        BOTH = (0, 1)
 
-        def at(f, T, *more):
-            if 0 <= T < TILES:
-                f(T, *more)
-
-        def widen_hi(T):
-            if T in ON_SCALAR:
-                widen_plain(T)
+        def widen_half(T, g):
+            if (T, g) in ON_SCALAR:
+                widen_plain(T, g)
             else:
-                widen(T, HI)
+                widen(T, range(4 * g, 4 * g + 4))
 
-        def run(T):
-            return 2 if T < TILES - 2 else 1
+        def second_b(T, count):
+            negate_b(T, count)
+            quant_emb(BP, T, count)
 
-        def second_b(T):
-            negate_b(T, run(T))
-            quant_emb(BP, T, run(T))
-
-        def second_a(T):
-            quant_emb(AL, T, run(T))
-            quant_emb(BN, T, run(T))
-
-        filler = []
-        for T in range(3, TILES):
-            filler.append((lambda T: widen(T, LO), T))
-            filler.append((widen_hi, T))
-        for T in range(0, TILES - 1, 2):
-            filler.append((second_b, T))
-            filler.append((second_a, T))
-
-        def fill(count):
-            for f, T in filler[:count]:
-                f(T)
-            for x in filler[:count]:
-                filler.remove(x)
-
-        nc.scalar.activation(out=z_pos[:, 0:1], in_=tiny[:], func=ACT.Sigmoid)
+        nc.scalar.activation(out=preload[:], in_=tiny[:], func=ACT.Sigmoid)
         warm(1)
         gate_order()
         gate_constants()
         spread_scales()
         warm(2)
         for T in (0, 1, 2):
-            widen(T, LO)
-            widen_hi(T)
-        turn(0)
+            widen_half(T, 0)
+            widen_half(T, 1)
+        turn(0, BOTH, 0)
         warm(1)
-        empty(0)
-        turn(1)
+        empty(0, BOTH)
+        turn(1, BOTH, 1)
         warm(1)
-        empty(1)
+        empty(1, BOTH)
         permute(WB)
-        turn(2)
+        turn(2, BOTH, 6)
         gate_turn()
-        fill(1)
-        quant_h(0)
-        warm(0)
-        empty(2)
-        fill(1)
+        widen_half(3, 0)
+        quant_h(0, BOTH)
+        empty(2, BOTH)
+        gate_square()
         permute(WA)
-        gate_z()
-        quant_h(1)
-        gate_z2()
-        fill(1)
+        widen_half(3, 1)
+        quant_h(1, BOTH)
+        project(WB, 0)
+        project(WA, 0)
+        make_b(0)
+        widen_half(4, 0)
+        widen_half(5, 1)
         gate_series()
-        for s in range(TILES):
-            project(WB, s)
-            at(make_al, s - 1)
-            fill(FILL[s][0])
-            for T in QUANT.get(s, ()):
-                quant_h(T)
-            fill(FILL[s][1])
-            if s == TILES - 1:
-                make_b(s)
-                scores(0)
-                sigmoid(0)
-            project(WA, s)
-            if s < TILES - 1:
-                make_b(s)
-            for T in TURNS.get(s, ()):
-                turn(T)
-                empty(T)
-            for n in SCORES.get(s, ()):
-                scores(n)
-                sigmoid(n)
-        fill(len(filler))
-        last = TILES - 1
-        negate_b(last, 1)
-        quant_emb(BP, last, 1)
-        make_al(last)
-        quant_emb(BN, last, 1)
-        quant_emb(AL, last, 1)
-        for n in range(len(PACKS)):
-            if n not in px:
-                scores(n)
-                sigmoid(n)
+        widen_half(4, 1)
+        quant_h(2, BOTH)
+        widen_half(5, 0)
+        project(WB, 1)
+        make_al(0)
+        project(WA, 1)
+        make_b(1)
+        widen_half(6, 1)
+        widen_half(6, 0)
+        for T, b in ((3, 7), (4, 0), (5, 1)):
+            turn(T, BOTH, b)
+            empty(T, BOTH)
+        project(WB, 2)
+        make_al(1)
+        quant_h(3, BOTH)
+        widen_half(7, 0)
+        second_b(0, 2)
+        project(WA, 2)
+        make_b(2)
+        widen_half(7, 1)
+        project(WB, 3)
+        quant_h(4, BOTH)
+        make_al(2)
+        quant_h(5, BOTH)
+        quant_emb(AL, 0, 2)
+        quant_emb(BN, 0, 2)
+        project(WA, 3)
+        make_b(3)
+        for T, b in ((6, 6), (7, 7)):
+            turn(T, BOTH, b)
+            empty(T, BOTH)
+        project(WB, 4)
+        make_al(3)
+        second_b(2, 2)
+        project(WA, 4)
+        make_b(4)
+        make_neg_b(4)
+        quant_h(6, BOTH)
+        project(WB, 5)
+        quant_emb(AL, 2, 2)
+        quant_emb(BN, 2, 2)
+        make_al(4)
+        quant_h(7, BOTH)
+        project(WA, 5)
+        make_b(5)
+        make_neg_b(5)
+        project(WB, 6)
+        make_al(5)
+        quant_emb(BP, 4, 2)
+        project(WA, 6)
+        make_b(6)
+        make_neg_b(6)
+        project(WB, 7)
+        make_b(7)
+        make_neg_b(7)
+        quant_emb(AL, 4, 2)
+        quant_emb(BN, 4, 2)
+        make_al(6)
+        quant_emb(BP, 6, 1)
+        scores(0)
+        sigmoid(0)
+        project(WA, 7)
+        quant_emb(AL, 6, 1)
+        quant_emb(BN, 6, 1)
+        quant_emb(BP, 7, 1)
+        make_al(7)
+        quant_emb(BN, 7, 1)
+        quant_emb(AL, 7, 1)
+        for n in range(1, len(PACKS)):
+            scores(n)
+            sigmoid(n)
         for n in range(len(PACKS)):
             keep_neg_s(n)
         for a in range(NP):

@@ -9,6 +9,7 @@ P = 128
 NT = N // P
 TILES = NP * NT
 G = D // 512
+BLOCKS = D // P
 FLOPS = 2 * NP * (2 * N * D * K + N * N * K)
 C = K ** -0.5
 TINY = 2.0 ** -60
@@ -27,6 +28,15 @@ ACT = mybir.ActivationFunctionType
 
 WB, WA = 0, 1
 AL, BP, BN = 0, 1, 2
+
+SCALAR_WIDENS = (1, 2, 5, 6, 7)
+SCALAR_NEGATES = 5
+PACKS = ((3,), (0, 2), (1, 5), (4, 6), (7,))
+
+TURN_BANKS = (0, 1, 6, 7)
+PACK_BANKS = (6, 0, 1, 7, 2)
+UPPER_BANKS = {0: 3, 1: 4, 2: 5, 4: 0, 5: 6, 6: 1}
+SPREAD_BANK, WARM_BANK, GATE_BANK = 3, 4, 5
 
 
 def tile_generalpreferenceskewembeddingscores_d2p_kernel(
@@ -49,30 +59,28 @@ def tile_generalpreferenceskewembeddingscores_d2p_kernel(
         w_perm = [sb.tile([P, G, 4, 256], U8, name=f"w_perm{w}", align_bytes=64) for w in range(2)]
         s_raw = [sb.tile([P, G, K], U8, name=f"s_raw{w}", align_bytes=64) for w in range(2)]
         s_perm = [sb.tile([P, G, 4, P], U8, name=f"s_perm{w}", align_bytes=64) for w in range(2)]
-        scales = sb.tile([P, TILES * 8], F32, name="scales")
+        scales = sb.tile([P, TILES * BLOCKS], F32, name="scales")
         scale_col = sb.tile([P, 1], F32, name="scale_col")
         tiny = sb.tile([P, 1], F32, name="tiny")
-
         odd = sb.tile([P, NP * 4, TERMS], F32, name="odd")
         half_odd = sb.tile([P, NP * 4, TERMS], F32, name="half_odd")
         neg_ln2 = sb.tile([P, 1], F32, name="neg_ln2")
         factor = sb.tile([P, NP * 4, TERMS + 1], F32, name="factor")
         addend = sb.tile([P, NP * 4, TERMS + 1], F32, name="addend")
-
         zeros = sb.tile([P, N], BF16, name="zeros")
-        nc.vector.memset(zeros[:], 0.0)
-        nc.vector.memset(ident[:], 0.0)
-        make_identity(nc, ident[:], nomemset=True)
+
         nc.gpsimd.iota(
             odd[:], pattern=[[0, NP * 4], [-2, TERMS]], base=2 * TERMS - 1, channel_multiplier=0,
             allow_small_or_imprecise_dtypes=True,
         )
+        nc.vector.memset(ident[:], 0.0)
+        make_identity(nc, ident[:], nomemset=True)
+        nc.vector.memset(zeros[:], 0.0)
         for w in range(2):
             nc.vector.memset(s_raw[w][:].rearrange("p g k -> p (g k)").bitcast(I32), 0)
         nc.vector.memset(gate_rows[:], 0.0)
-        nc.vector.memset(scale_col[TILES * 8 : P, :], 0.0)
+        nc.vector.memset(scale_col[TILES * BLOCKS : P, :], 0.0)
         nc.vector.memset(tiny[:], TINY)
-
         nc.vector.memset(factor[:, :, 0:1], 0.0)
 
         codes_in = {}
@@ -86,63 +94,52 @@ def tile_generalpreferenceskewembeddingscores_d2p_kernel(
             for i in range(count):
                 codes_in[a * NT + first + i] = (t, i)
 
-        def load_words(w, words):
+        def load_weight(w, words, scale_rows):
             nc.sync.dma_start(
                 out=w_raw[w][:].rearrange("p g b -> p (g b)").bitcast(I32).rearrange("p (g c) -> p g c", g=G),
                 in_=words.bitcast(I32).rearrange("g p c -> p g c"),
             )
-
-        def load_scale_rows(w, wscales, queue):
-            v = wscales.bitcast(I32).rearrange("g (q r) c -> q r g c", r=4)
-            d = s_raw[w][:].rearrange("p g k -> p (g k)").bitcast(I32).rearrange("p (g c) -> p g c", g=G)
+            src = scale_rows.bitcast(I32).rearrange("g (q r) c -> q r g c", r=4)
+            dst = s_raw[w][:].rearrange("p g k -> p (g k)").bitcast(I32).rearrange("p (g c) -> p g c", g=G)
             for q in range(4):
-                queue.dma_start(out=d[32 * q : 32 * q + 4], in_=v[q])
+                nc.sync.dma_start(out=dst[32 * q : 32 * q + 4], in_=src[q])
 
-        nc.scalar.dma_start(out=scale_col[0 : TILES * 8, :], in_=h_scale.rearrange("a i (j o) -> (a i j) o", o=1))
+        nc.scalar.dma_start(
+            out=scale_col[0 : TILES * BLOCKS, :], in_=h_scale.rearrange("a i (j o) -> (a i j) o", o=1)
+        )
         load_h(0, 0, 1)
         nc.scalar.dma_start(out=gate_in[0:NP, :], in_=gate)
         load_h(0, 1, 1)
         load_h(0, 2, 2)
-        load_words(WB, wb_words)
-        load_scale_rows(WB, wb_scales, nc.sync)
-        load_words(WA, wa_words)
-        load_scale_rows(WA, wa_scales, nc.sync)
+        load_weight(WB, wb_words, wb_scales)
+        load_weight(WA, wa_words, wa_scales)
         load_h(1, 0, 2)
         load_h(1, 2, 2)
 
-        plain = {}
-        wide, pt, hg, hc, hs, prod, emb = {}, {}, {}, {}, {}, {}, {}
-        kc = [sb.tile([P, 3, N], U32, name=f"kc{a}", align_bytes=64) for a in range(NP)]
-        ks = [sb.tile([P, 3, N], U8, name=f"ks{a}", align_bytes=64) for a in range(NP)]
-        px, neg_s, sig, logs, res, up = {}, {}, {}, {}, {}, {}
+        wide, plain, turned, grouped, h_codes, h_scales, prod, emb = {}, {}, {}, {}, {}, {}, {}, {}
+        e_codes = [sb.tile([P, 3, N], U32, name=f"e_codes{a}", align_bytes=64) for a in range(NP)]
+        e_scales = [sb.tile([P, 3, N], U8, name=f"e_scales{a}", align_bytes=64) for a in range(NP)]
+        score, neg_s, sig, logs, res, upper = {}, {}, {}, {}, {}, {}
         lam = sb.tile([P, NP, 4], F32, name="lam")
         g_abs = sb.tile([P, NP * 4], F32, name="g_abs")
         preload = sb.tile([P, 1], F32, name="preload")
         horner = sb.tile([P, NP * 4, TERMS + 1], F32, name="horner")
 
-        def gate_turn():
-            pg = bank(5, [P, NP * 4], "pg")
-            for t in range(4):
-                nc.tensor.matmul(
-                    pg[:, NP * t : NP * (t + 1)], lhsT=gate_rows[:, P * t : P * (t + 1)], rhs=pick[:], start=True, stop=True
-                )
-            nc.scalar.activation(out=g_abs[:], in_=pg[:], func=ACT.Abs)
-            nc.scalar.activation(out=addend[:, :, TERMS], in_=pg[:], func=ACT.Relu)
-            nc.scalar.activation(out=factor[:, :, TERMS], in_=g_abs[:], func=ACT.Sigmoid, scale=-1.0, bias=neg_ln2[:])
-
-        def gate_square():
-            z = factor[:, :, TERMS : TERMS + 1].to_broadcast([P, NP * 4, TERMS - 1])
-            nc.scalar.activation(out=factor[:, :, 1:TERMS], in_=z, func=ACT.Square)
-
-        def warm(count):
+        def warm_tensor(count):
             for i in range(count):
-                wp = bank(4, [P, N], "warm")
-                nc.tensor.matmul(wp[:], lhsT=zeros[:, 0:P], rhs=zeros[:], start=True, stop=True)
+                unread = bank(WARM_BANK, [P, N], "unread")
+                nc.tensor.matmul(unread[:], lhsT=zeros[:, 0:P], rhs=zeros[:], start=True, stop=True)
 
         def spread_scales():
-            sp = bank(3, [P, P], "spread")
-            nc.tensor.transpose(sp[:], scale_col[:].to_broadcast([P, P]), ident[:])
-            nc.vector.tensor_copy(out=scales[:], in_=sp[:, 0 : TILES * 8])
+            spread = bank(SPREAD_BANK, [P, P], "spread")
+            nc.tensor.transpose(spread[:], scale_col[:].to_broadcast([P, P]), ident[:])
+            nc.vector.tensor_copy(out=scales[:], in_=spread[:, 0 : TILES * BLOCKS])
+
+        def gate_order():
+            nc.scalar.copy(
+                out=gate_rows[0:NP, :].rearrange("a (t q r) -> a t q r", t=4, r=8),
+                in_=gate_in[0:NP, :].rearrange("a (q t r) -> a t q r", t=4, r=8),
+            )
 
         def gate_constants():
             nc.vector.tensor_scalar(out=half_odd[:], in0=odd[:], scalar1=0.5, scalar2=None, op0=ALU.mult)
@@ -152,11 +149,22 @@ def tile_generalpreferenceskewembeddingscores_d2p_kernel(
             nc.vector.reciprocal(out=addend[:, :, 0:TERMS], in_=half_odd[:])
             nc.vector.tensor_copy(out=pick[:], in_=ident[:, 0:NP])
 
-        def gate_order():
-            nc.scalar.copy(
-                out=gate_rows[0:NP, :].rearrange("a (t q r) -> a t q r", t=4, r=8),
-                in_=gate_in[0:NP, :].rearrange("a (q t r) -> a t q r", t=4, r=8),
+        def gate_turn():
+            v = bank(GATE_BANK, [P, NP * 4], "v")
+            for t in range(4):
+                nc.tensor.matmul(
+                    v[:, NP * t : NP * (t + 1)], lhsT=gate_rows[:, P * t : P * (t + 1)], rhs=pick[:],
+                    start=True, stop=True,
+                )
+            nc.scalar.activation(out=g_abs[:], in_=v[:], func=ACT.Abs)
+            nc.scalar.activation(out=addend[:, :, TERMS], in_=v[:], func=ACT.Relu)
+            nc.scalar.activation(
+                out=factor[:, :, TERMS], in_=g_abs[:], func=ACT.Sigmoid, scale=-1.0, bias=neg_ln2[:]
             )
+
+        def gate_square():
+            z = factor[:, :, TERMS : TERMS + 1].to_broadcast([P, NP * 4, TERMS - 1])
+            nc.scalar.activation(out=factor[:, :, 1:TERMS], in_=z, func=ACT.Square)
 
         def gate_series():
             nc.vector.tensor_tensor_scan(
@@ -169,55 +177,49 @@ def tile_generalpreferenceskewembeddingscores_d2p_kernel(
             )
             nc.scalar.copy(out=lam[:], in_=horner[:, :, TERMS].rearrange("p (t a) -> p a t", a=NP))
 
-        def widen(T, blocks):
+        def widen(T, g):
             t, i = codes_in[T]
-            if T not in wide:
+            on_scalar = g == 1 and T in SCALAR_WIDENS
+            if on_scalar:
+                plain[T] = sb.tile([P, 512], BF16, name=f"plain{T}", align_bytes=64)
+            elif T not in wide:
                 wide[T] = sb.tile([P, D], BF16, name=f"wide{T}", align_bytes=64)
-            for j in blocks:
-                nc.vector.tensor_scalar(
-                    out=wide[T][:, 512 * (j // 4) : 512 * (j // 4 + 1)].rearrange("p (u w e) -> p w u e", u=2, e=2)[
-                        :, 32 * (j % 4) : 32 * (j % 4 + 1)
-                    ],
-                    in0=t[:, i, P * j : P * (j + 1)].bitcast(FP8).rearrange("p (w u e) -> p w u e", u=2, e=2),
-                    scalar1=scales[:, 8 * T + j : 8 * T + j + 1],
-                    scalar2=None,
-                    op0=ALU.mult,
-                )
+            for j in range(4):
+                src = t[:, i, P * (4 * g + j) : P * (4 * g + j + 1)].bitcast(FP8)
+                scale = scales[:, BLOCKS * T + 4 * g + j : BLOCKS * T + 4 * g + j + 1]
+                if on_scalar:
+                    nc.scalar.activation(out=plain[T][:, P * j : P * (j + 1)], in_=src, func=ACT.Copy, scale=scale)
+                else:
+                    pairs = wide[T][:, 512 * g : 512 * (g + 1)].rearrange("p (u w e) -> p w u e", u=2, e=2)
+                    nc.vector.tensor_scalar(
+                        out=pairs[:, 32 * j : 32 * (j + 1)],
+                        in0=src.rearrange("p (w u e) -> p w u e", u=2, e=2),
+                        scalar1=scale,
+                        scalar2=None,
+                        op0=ALU.mult,
+                    )
 
-        def widen_plain(T, g):
-            t, i = codes_in[T]
-            plain[T, g] = sb.tile([P, 512], BF16, name=f"plain{T}_{g}", align_bytes=64)
-            for j in range(4 * g, 4 * g + 4):
-                nc.scalar.activation(
-                    out=plain[T, g][:, P * (j % 4) : P * (j % 4 + 1)],
-                    in_=t[:, i, P * j : P * (j + 1)].bitcast(FP8),
-                    func=ACT.Copy,
-                    scale=scales[:, 8 * T + j : 8 * T + j + 1],
-                )
-
-        def turn(T, passes, b):
-            pt[T, passes] = bank(b, [P, 2 * len(passes), P], f"pt{T}_{passes[0]}")
-            for n, g in enumerate(passes):
+        def turn(T):
+            turned[T] = bank(TURN_BANKS[T % 4], [P, 2 * G, P], f"turned{T}")
+            for g in range(G):
                 for u in range(2):
-                    if (T, g) in plain:
-                        src = plain[T, g][:].bitcast(F32)[:, u : 256 : 2]
+                    if g == 1 and T in SCALAR_WIDENS:
+                        src = plain[T][:].bitcast(F32)[:, u : 256 : 2]
                     else:
                         src = wide[T][:].bitcast(F32)[:, 256 * g + P * u : 256 * g + P * (u + 1)]
-                    nc.tensor.transpose(pt[T, passes][:, 2 * n + u, :], src, ident[:])
+                    nc.tensor.transpose(turned[T][:, 2 * g + u, :], src, ident[:])
 
-        def empty(T, passes):
-            hg[T, passes] = sb.tile([P, len(passes) * P * 4], BF16, name=f"hg{T}_{passes[0]}", align_bytes=64)
+        def copy_turned(T):
+            grouped[T] = sb.tile([P, G * P * 4], BF16, name=f"grouped{T}", align_bytes=64)
             nc.scalar.copy(
-                out=hg[T, passes][:].bitcast(F32).rearrange("p (g n u) -> p g n u", n=P, u=2),
-                in_=pt[T, passes][:].rearrange("p (g u) n -> p g n u", u=2),
+                out=grouped[T][:].bitcast(F32).rearrange("p (g n u) -> p g n u", n=P, u=2),
+                in_=turned[T][:].rearrange("p (g u) n -> p g n u", u=2),
             )
 
-        def quant_h(T, passes):
-            if T not in hc:
-                hc[T] = sb.tile([P, G * P], U32, name=f"hc{T}", align_bytes=64)
-                hs[T] = sb.tile([P, G * P], U8, name=f"hs{T}", align_bytes=64)
-            cols = slice(P * passes[0], P * (passes[-1] + 1))
-            nc.vector.quantize_mx(out=hc[T][:, cols].bitcast(FP8X4), scales=hs[T][:, cols], in_=hg[T, passes][:])
+        def quant_h(T):
+            h_codes[T] = sb.tile([P, G * P], U32, name=f"h_codes{T}", align_bytes=64)
+            h_scales[T] = sb.tile([P, G * P], U8, name=f"h_scales{T}", align_bytes=64)
+            nc.vector.quantize_mx(out=h_codes[T][:].bitcast(FP8X4), scales=h_scales[T][:], in_=grouped[T][:])
 
         def permute(w):
             for dst, src, x in (
@@ -230,64 +232,53 @@ def tile_generalpreferenceskewembeddingscores_d2p_kernel(
                 )
 
         def project(w, T):
-            acc = prod[w, T] = bank(2 + 2 * (T % 2) + w, [P, 4, P], f"p{w}_{T}")
+            acc = prod[w, T] = bank(2 + 2 * (T % 2) + w, [P, 4, P], f"prod{w}_{T}")
             for t in range(4):
                 for g in range(G):
                     nc.tensor.matmul_mx(
                         out=acc[:, t, :],
                         lhsT=w_perm[w][:, g, t, :].bitcast(FP4X4),
                         lhsT_scale=s_perm[w][:, g, t, :],
-                        rhs=hc[T][:, P * g : P * (g + 1)].bitcast(FP8X4),
-                        rhs_scale=hs[T][:, P * g : P * (g + 1)],
+                        rhs=h_codes[T][:, P * g : P * (g + 1)].bitcast(FP8X4),
+                        rhs_scale=h_scales[T][:, P * g : P * (g + 1)],
                         start=(g == 0),
                         stop=(g == G - 1),
                     )
 
-        def emb_tile(k, T):
+        def emb_run(k, T, count):
             if (k, T // 2) not in emb:
                 emb[k, T // 2] = sb.tile([P, 2, 512], BF16, name=f"emb{k}_{T // 2}", align_bytes=64)
-            return emb[k, T // 2][:, T % 2, :]
-
-        def emb_run(k, T, count):
-            emb_tile(k, T)
             return emb[k, T // 2][:, T % 2 : T % 2 + count, :].rearrange("p i n -> p (i n)")
 
         def make_al(T):
             a = T // NT
             nc.vector.tensor_tensor(
-                out=emb_tile(AL, T).rearrange("p (n t) -> p n t", t=4),
+                out=emb_run(AL, T, 1).rearrange("p (n t) -> p n t", t=4),
                 in0=prod[WA, T][:].rearrange("p t n -> p n t"),
                 in1=lam[:, a : a + 1, :].to_broadcast([P, P, 4]),
                 op=ALU.mult,
             )
 
         def make_b(T):
-            nc.scalar.copy(
-                out=emb_tile(BP, T).rearrange("p (n t) -> p n t", t=4),
-                in_=prod[WB, T][:].rearrange("p t n -> p n t"),
-            )
-
-        def make_neg_b(T):
-            nc.scalar.activation(
-                out=emb_tile(BN, T).rearrange("p (n t) -> p n t", t=4),
-                in_=prod[WB, T][:].rearrange("p t n -> p n t"),
-                func=ACT.Copy,
-                scale=-1.0,
-            )
+            src = prod[WB, T][:].rearrange("p t n -> p n t")
+            nc.scalar.copy(out=emb_run(BP, T, 1).rearrange("p (n t) -> p n t", t=4), in_=src)
+            if T >= SCALAR_NEGATES:
+                nc.scalar.activation(
+                    out=emb_run(BN, T, 1).rearrange("p (n t) -> p n t", t=4), in_=src, func=ACT.Copy, scale=-1.0
+                )
 
         def negate_b(T, count):
             nc.vector.tensor_scalar(
                 out=emb_run(BN, T, count), in0=emb_run(BP, T, count), scalar1=-1.0, scalar2=None, op0=ALU.mult
             )
 
-        def quant_emb(k, T, count):
+        def quant_emb(kinds, T, count):
             a, cols = T // NT, slice(P * (T % NT), P * (T % NT + count))
-            nc.vector.quantize_mx(
-                out=kc[a][:, k, cols].bitcast(FP8X4), scales=ks[a][:, k, cols], in_=emb_run(k, T, count)
-            )
+            for k in kinds:
+                nc.vector.quantize_mx(
+                    out=e_codes[a][:, k, cols].bitcast(FP8X4), scales=e_scales[a][:, k, cols], in_=emb_run(k, T, count)
+                )
 
-        PACKS = ((3,), (0, 2), (1, 5), (4, 6), (7,))
-        PACK_BANK = (6, 0, 1, 7, 2)
         place = {}
         for n, pack in enumerate(PACKS):
             first = 0
@@ -296,197 +287,172 @@ def tile_generalpreferenceskewembeddingscores_d2p_kernel(
                 first = place[T][1].stop
 
         def scores(n):
-            px[n] = bank(PACK_BANK[n], [P, N], f"px{n}")
+            score[n] = bank(PACK_BANKS[n], [P, N], f"score{n}")
             for T in PACKS[n]:
                 a, j = divmod(T, NT)
                 width = P * (j + 1)
-                x = px[n][:, place[T][1]]
+                x = score[n][:, place[T][1]]
                 rows = slice(P * j, P * (j + 1))
                 cuts = [(0, 256), (256, 384)] if width == 384 else [(0, width)]
                 for lo, hi in cuts:
-                    for s, m in ((BN, AL), (AL, BP)):
+                    for stationary, moving in ((BN, AL), (AL, BP)):
                         nc.tensor.matmul_mx(
                             out=x[:, lo:hi],
-                            lhsT=kc[a][:, s, rows].bitcast(FP8X4),
-                            lhsT_scale=ks[a][:, s, rows],
-                            rhs=kc[a][:, m, lo:hi].bitcast(FP8X4),
-                            rhs_scale=ks[a][:, m, lo:hi],
-                            start=(s == BN),
-                            stop=(s == AL),
+                            lhsT=e_codes[a][:, stationary, rows].bitcast(FP8X4),
+                            lhsT_scale=e_scales[a][:, stationary, rows],
+                            rhs=e_codes[a][:, moving, lo:hi].bitcast(FP8X4),
+                            rhs_scale=e_scales[a][:, moving, lo:hi],
+                            start=(stationary == BN),
+                            stop=(stationary == AL),
                         )
+            sig[n] = sb.tile([P, N], F32, name=f"sig{n}")
+            nc.scalar.activation(out=sig[n][:], in_=score[n][:], func=ACT.Sigmoid, scale=C)
 
         def keep_neg_s(n):
             neg_s[n] = sb.tile([P, N], F32, name=f"neg_s{n}")
-            nc.vector.tensor_scalar(out=neg_s[n][:], in0=px[n][:], scalar1=-C, scalar2=None, op0=ALU.mult)
-
-        def sigmoid(n):
-            sig[n] = sb.tile([P, N], F32, name=f"sig{n}")
-            nc.scalar.activation(out=sig[n][:], in_=px[n][:], func=ACT.Sigmoid, scale=C)
+            nc.vector.tensor_scalar(out=neg_s[n][:], in0=score[n][:], scalar1=-C, scalar2=None, op0=ALU.mult)
 
         def log(n, cols):
             if n not in logs:
                 logs[n] = sb.tile([P, N], F32, name=f"logs{n}")
             nc.scalar.activation(out=logs[n][:, cols], in_=sig[n][:, cols], func=ACT.Ln, bias=tiny[:])
 
-        def res_tile(T):
-            if T not in res:
-                res[T] = sb.tile([P, N], F32, name=f"res{T}")
-            return res[T]
-
         def lower(T, part):
             n, cols = place[T]
+            if T not in res:
+                res[T] = sb.tile([P, N], F32, name=f"res{T}")
             nc.vector.scalar_tensor_tensor(
-                out=res_tile(T)[:, part],
-                in0=neg_s[n][:, cols][:, part], scalar=-1.0, in1=logs[n][:, cols][:, part], op0=ALU.mult, op1=ALU.min,
+                out=res[T][:, part],
+                in0=neg_s[n][:, cols][:, part],
+                scalar=-1.0,
+                in1=logs[n][:, cols][:, part],
+                op0=ALU.mult,
+                op1=ALU.min,
             )
 
-        def mirror(src, T, first):
+        def mirror(src, T, opening):
             a, j = divmod(T, NT)
             for i in range(j):
-                R = a * NT + i
-                if R not in up:
-                    up[R] = bank((3, 4, 5, 0, 0, 6, 1)[R], [P, N - P * (i + 1)], f"up{R}")
+                row = a * NT + i
+                if row not in upper:
+                    upper[row] = bank(UPPER_BANKS[row], [P, N - P * (i + 1)], f"upper{row}")
                 nc.tensor.matmul(
-                    up[R][:, P * (j - i - 1) : P * (j - i)],
+                    upper[row][:, P * (j - i - 1) : P * (j - i)],
                     lhsT=src[:, P * i : P * (i + 1)],
                     rhs=ident[:],
                     is_transpose=True,
-                    start=(first and j == NT - 1),
-                    stop=(not first and j == i + 1),
+                    start=(opening and j == NT - 1),
+                    stop=(not opening and j == i + 1),
                 )
 
-        def upper(T, eng):
-            lo = P * (T % NT + 1)
-            if eng == 0:
-                nc.scalar.copy(out=res_tile(T)[:, lo:N], in_=up[T][:])
+        def copy_upper(T, on_vector):
+            cols = slice(P * (T % NT + 1), N)
+            if on_vector:
+                nc.vector.tensor_copy(out=res[T][:, cols], in_=upper[T][:])
             else:
-                nc.vector.tensor_copy(out=res_tile(T)[:, lo:N], in_=up[T][:])
+                nc.scalar.copy(out=res[T][:, cols], in_=upper[T][:])
 
         def store(T, part):
             a, j = divmod(T, NT)
             nc.sync.dma_start(out=out[a, P * j : P * (j + 1), part], in_=res[T][:, part])
 
-        ON_SCALAR = ((1, 1), (2, 1), (5, 1), (6, 1), (7, 1))
-        BOTH = (0, 1)
-
-        def widen_half(T, g):
-            if (T, g) in ON_SCALAR:
-                widen_plain(T, g)
-            else:
-                widen(T, range(4 * g, 4 * g + 4))
-
-        def second_b(T, count):
-            negate_b(T, count)
-            quant_emb(BP, T, count)
+        def begin(T):
+            project(WB, T)
+            make_b(T)
+            if T > 0:
+                make_al(T - 1)
 
         nc.scalar.activation(out=preload[:], in_=tiny[:], func=ACT.Sigmoid)
-        warm(1)
+        warm_tensor(1)
         gate_order()
         gate_constants()
         spread_scales()
-        warm(2)
-        for T in (0, 1, 2):
-            widen_half(T, 0)
-            widen_half(T, 1)
-        turn(0, BOTH, 0)
-        warm(1)
-        empty(0, BOTH)
-        turn(1, BOTH, 1)
-        warm(1)
-        empty(1, BOTH)
+        warm_tensor(2)
+        for T in range(3):
+            for g in range(G):
+                widen(T, g)
+        for T in range(2):
+            turn(T)
+            warm_tensor(1)
+            copy_turned(T)
         permute(WB)
-        turn(2, BOTH, 6)
+        turn(2)
         gate_turn()
-        widen_half(3, 0)
-        quant_h(0, BOTH)
-        empty(2, BOTH)
+        warm_tensor(1)
+        widen(3, 0)
+        quant_h(0)
+        copy_turned(2)
         gate_square()
         permute(WA)
-        widen_half(3, 1)
-        quant_h(1, BOTH)
-        project(WB, 0)
-        project(WA, 0)
-        make_b(0)
-        widen_half(4, 0)
-        widen_half(5, 1)
+        widen(3, 1)
+        quant_h(1)
+
+        begin(0)
+        widen(4, 0)
+        widen(5, 1)
         gate_series()
-        widen_half(4, 1)
-        quant_h(2, BOTH)
-        widen_half(5, 0)
-        project(WB, 1)
-        make_al(0)
+        widen(4, 1)
+        quant_h(2)
+        widen(5, 0)
+        project(WA, 0)
+
+        begin(1)
+        widen(6, 0)
         project(WA, 1)
-        make_b(1)
-        widen_half(6, 1)
-        widen_half(6, 0)
-        for T, b in ((3, 7), (4, 0), (5, 1)):
-            turn(T, BOTH, b)
-            empty(T, BOTH)
-        project(WB, 2)
-        make_al(1)
-        quant_h(3, BOTH)
-        widen_half(7, 0)
-        second_b(0, 2)
+        for T in (3, 4, 5):
+            turn(T)
+            copy_turned(T)
+            if T != 4:
+                widen(6 if T == 3 else 7, 1)
+
+        begin(2)
+        quant_h(3)
+        widen(7, 0)
+        negate_b(0, 2)
+        quant_emb((BP,), 0, 2)
+        quant_h(4)
         project(WA, 2)
-        make_b(2)
-        widen_half(7, 1)
-        project(WB, 3)
-        quant_h(4, BOTH)
-        make_al(2)
-        quant_h(5, BOTH)
-        quant_emb(AL, 0, 2)
-        quant_emb(BN, 0, 2)
+
+        begin(3)
+        quant_h(5)
+        quant_emb((AL, BN), 0, 2)
         project(WA, 3)
-        make_b(3)
-        for T, b in ((6, 6), (7, 7)):
-            turn(T, BOTH, b)
-            empty(T, BOTH)
-        project(WB, 4)
-        make_al(3)
-        second_b(2, 2)
+        for T in (6, 7):
+            turn(T)
+            copy_turned(T)
+
+        begin(4)
+        negate_b(2, 2)
+        quant_emb((BP,), 2, 2)
+        quant_h(6)
+        quant_emb((AL, BN), 2, 2)
         project(WA, 4)
-        make_b(4)
-        make_neg_b(4)
-        quant_h(6, BOTH)
-        project(WB, 5)
-        quant_emb(AL, 2, 2)
-        quant_emb(BN, 2, 2)
-        make_al(4)
-        quant_h(7, BOTH)
+
+        begin(5)
+        quant_h(7)
+        negate_b(4, 1)
         project(WA, 5)
-        make_b(5)
-        make_neg_b(5)
-        project(WB, 6)
-        make_al(5)
-        quant_emb(BP, 4, 2)
+
+        begin(6)
+        quant_emb((BP, AL, BN), 4, 2)
         project(WA, 6)
-        make_b(6)
-        make_neg_b(6)
-        project(WB, 7)
-        make_b(7)
-        make_neg_b(7)
-        quant_emb(AL, 4, 2)
-        quant_emb(BN, 4, 2)
-        make_al(6)
-        quant_emb(BP, 6, 1)
+
+        begin(7)
+        quant_emb((BP, AL, BN), 6, 1)
+        quant_emb((BP,), 7, 1)
         scores(0)
-        sigmoid(0)
         project(WA, 7)
-        quant_emb(AL, 6, 1)
-        quant_emb(BN, 6, 1)
-        quant_emb(BP, 7, 1)
         make_al(7)
-        quant_emb(BN, 7, 1)
-        quant_emb(AL, 7, 1)
+        quant_emb((BN, AL), 7, 1)
         for n in range(1, len(PACKS)):
             scores(n)
-            sigmoid(n)
+
         for n in range(len(PACKS)):
             keep_neg_s(n)
         for a in range(NP):
-            for j in range(NT - 1, 0, -1):
-                n, cols = place[a * NT + j]
-                mirror(neg_s[n][:, cols], a * NT + j, True)
+            for T in range(a * NT + NT - 1, a * NT, -1):
+                n, cols = place[T]
+                mirror(neg_s[n][:, cols], T, True)
         whole = slice(0, N)
         for T in (3, 7):
             for half in (slice(0, N // 2), slice(N // 2, N)):
@@ -496,21 +462,21 @@ def tile_generalpreferenceskewembeddingscores_d2p_kernel(
             mirror(res[T], T, False)
         for T in (2, 6):
             log(*place[T])
-        log(2, whole)
+        log(place[1][0], whole)
         for T in (0, 4):
             log(*place[T])
         for T in (2, 6):
             lower(T, slice(0, 3 * P))
-            upper(T, 1)
+            copy_upper(T, True)
             store(T, whole)
             mirror(res[T], T, False)
         for T in (1, 5):
             lower(T, slice(0, 2 * P))
             mirror(res[T], T, False)
-            upper(T, 0)
+            copy_upper(T, False)
             store(T, whole)
         for T in (0, 4):
             lower(T, slice(0, P))
         for T in (0, 4):
-            upper(T, 0 if T != 4 else 1)
+            copy_upper(T, T == 4)
             store(T, whole)

@@ -29,8 +29,8 @@ ACT = mybir.ActivationFunctionType
 WB, WA = 0, 1
 AL, BP, BN = 0, 1, 2
 
-SCALAR_WIDENS = (1, 2, 5, 6, 7)
-SCALAR_NEGATES = 5
+SCALAR_WIDENS = ((1, 1), (2, 1), (5, 1), (6, 0), (6, 1), (7, 1))
+SCALAR_NEGATES = (4, 5, 6, 7)
 PACKS = ((3,), (0, 2), (1, 5), (4, 6), (7,))
 
 TURN_BANKS = (0, 1, 6, 7)
@@ -75,9 +75,9 @@ def tile_generalpreferenceskewembeddingscores_d2p_kernel(
         )
         nc.vector.memset(ident[:], 0.0)
         make_identity(nc, ident[:], nomemset=True)
-        nc.vector.memset(zeros[:], 0.0)
         for w in range(2):
             nc.vector.memset(s_raw[w][:].rearrange("p g k -> p (g k)").bitcast(I32), 0)
+        nc.vector.memset(zeros[:], 0.0)
         nc.vector.memset(gate_rows[:], 0.0)
         nc.vector.memset(scale_col[TILES * BLOCKS : P, :], 0.0)
         nc.vector.memset(tiny[:], TINY)
@@ -94,11 +94,13 @@ def tile_generalpreferenceskewembeddingscores_d2p_kernel(
             for i in range(count):
                 codes_in[a * NT + first + i] = (t, i)
 
-        def load_weight(w, words, scale_rows):
+        def load_words(w, words):
             nc.sync.dma_start(
                 out=w_raw[w][:].rearrange("p g b -> p (g b)").bitcast(I32).rearrange("p (g c) -> p g c", g=G),
                 in_=words.bitcast(I32).rearrange("g p c -> p g c"),
             )
+
+        def load_scale_rows(w, scale_rows):
             src = scale_rows.bitcast(I32).rearrange("g (q r) c -> q r g c", r=4)
             dst = s_raw[w][:].rearrange("p g k -> p (g k)").bitcast(I32).rearrange("p (g c) -> p g c", g=G)
             for q in range(4):
@@ -109,10 +111,12 @@ def tile_generalpreferenceskewembeddingscores_d2p_kernel(
         )
         load_h(0, 0, 1)
         nc.scalar.dma_start(out=gate_in[0:NP, :], in_=gate)
-        load_h(0, 1, 1)
-        load_h(0, 2, 2)
-        load_weight(WB, wb_words, wb_scales)
-        load_weight(WA, wa_words, wa_scales)
+        load_h(0, 1, 2)
+        load_scale_rows(WB, wb_scales)
+        load_words(WB, wb_words)
+        load_words(WA, wa_words)
+        load_scale_rows(WA, wa_scales)
+        load_h(0, 3, 1)
         load_h(1, 0, 2)
         load_h(1, 2, 2)
 
@@ -120,7 +124,6 @@ def tile_generalpreferenceskewembeddingscores_d2p_kernel(
         e_codes = [sb.tile([P, 3, N], U32, name=f"e_codes{a}", align_bytes=64) for a in range(NP)]
         e_scales = [sb.tile([P, 3, N], U8, name=f"e_scales{a}", align_bytes=64) for a in range(NP)]
         score, neg_s, sig, logs, res, upper = {}, {}, {}, {}, {}, {}
-        lam = sb.tile([P, NP, 4], F32, name="lam")
         g_abs = sb.tile([P, NP * 4], F32, name="g_abs")
         preload = sb.tile([P, 1], F32, name="preload")
         horner = sb.tile([P, NP * 4, TERMS + 1], F32, name="horner")
@@ -134,6 +137,8 @@ def tile_generalpreferenceskewembeddingscores_d2p_kernel(
             spread = bank(SPREAD_BANK, [P, P], "spread")
             nc.tensor.transpose(spread[:], scale_col[:].to_broadcast([P, P]), ident[:])
             nc.vector.tensor_copy(out=scales[:], in_=spread[:, 0 : TILES * BLOCKS])
+
+        gate_v = []
 
         def gate_order():
             nc.scalar.copy(
@@ -156,8 +161,13 @@ def tile_generalpreferenceskewembeddingscores_d2p_kernel(
                     v[:, NP * t : NP * (t + 1)], lhsT=gate_rows[:, P * t : P * (t + 1)], rhs=pick[:],
                     start=True, stop=True,
                 )
-            nc.scalar.activation(out=g_abs[:], in_=v[:], func=ACT.Abs)
-            nc.scalar.activation(out=addend[:, :, TERMS], in_=v[:], func=ACT.Relu)
+            gate_v.append(v)
+
+        def gate_abs():
+            nc.scalar.activation(out=g_abs[:], in_=gate_v[0][:], func=ACT.Abs)
+            nc.scalar.activation(out=addend[:, :, TERMS], in_=gate_v[0][:], func=ACT.Relu)
+
+        def gate_z():
             nc.scalar.activation(
                 out=factor[:, :, TERMS], in_=g_abs[:], func=ACT.Sigmoid, scale=-1.0, bias=neg_ln2[:]
             )
@@ -175,20 +185,19 @@ def tile_generalpreferenceskewembeddingscores_d2p_kernel(
                 op0=ALU.mult,
                 op1=ALU.add,
             )
-            nc.scalar.copy(out=lam[:], in_=horner[:, :, TERMS].rearrange("p (t a) -> p a t", a=NP))
 
         def widen(T, g):
             t, i = codes_in[T]
-            on_scalar = g == 1 and T in SCALAR_WIDENS
+            on_scalar = (T, g) in SCALAR_WIDENS
             if on_scalar:
-                plain[T] = sb.tile([P, 512], BF16, name=f"plain{T}", align_bytes=64)
+                plain[T, g] = sb.tile([P, 512], BF16, name=f"plain{T}_{g}", align_bytes=64)
             elif T not in wide:
                 wide[T] = sb.tile([P, D], BF16, name=f"wide{T}", align_bytes=64)
             for j in range(4):
                 src = t[:, i, P * (4 * g + j) : P * (4 * g + j + 1)].bitcast(FP8)
                 scale = scales[:, BLOCKS * T + 4 * g + j : BLOCKS * T + 4 * g + j + 1]
                 if on_scalar:
-                    nc.scalar.activation(out=plain[T][:, P * j : P * (j + 1)], in_=src, func=ACT.Copy, scale=scale)
+                    nc.scalar.activation(out=plain[T, g][:, P * j : P * (j + 1)], in_=src, func=ACT.Copy, scale=scale)
                 else:
                     pairs = wide[T][:, 512 * g : 512 * (g + 1)].rearrange("p (u w e) -> p w u e", u=2, e=2)
                     nc.vector.tensor_scalar(
@@ -199,27 +208,36 @@ def tile_generalpreferenceskewembeddingscores_d2p_kernel(
                         op0=ALU.mult,
                     )
 
-        def turn(T):
-            turned[T] = bank(TURN_BANKS[T % 4], [P, 2 * G, P], f"turned{T}")
-            for g in range(G):
+        def turn(T, passes=range(G)):
+            t = bank(TURN_BANKS[len(turned) % 4], [P, 2 * len(passes), P], f"turned{T}_{passes[0]}")
+            turned[T, passes[0]] = t
+            for n, g in enumerate(passes):
                 for u in range(2):
-                    if g == 1 and T in SCALAR_WIDENS:
-                        src = plain[T][:].bitcast(F32)[:, u : 256 : 2]
+                    if (T, g) in SCALAR_WIDENS:
+                        src = plain[T, g][:].bitcast(F32)[:, u : 256 : 2]
                     else:
                         src = wide[T][:].bitcast(F32)[:, 256 * g + P * u : 256 * g + P * (u + 1)]
-                    nc.tensor.transpose(turned[T][:, 2 * g + u, :], src, ident[:])
+                    nc.tensor.transpose(t[:, 2 * n + u, :], src, ident[:])
 
-        def copy_turned(T):
-            grouped[T] = sb.tile([P, G * P * 4], BF16, name=f"grouped{T}", align_bytes=64)
+        def copy_turned(T, passes=range(G)):
+            if T not in grouped:
+                grouped[T] = sb.tile([P, G * P * 4], BF16, name=f"grouped{T}", align_bytes=64)
+            cols = slice(512 * passes[0], 512 * (passes[-1] + 1))
             nc.scalar.copy(
-                out=grouped[T][:].bitcast(F32).rearrange("p (g n u) -> p g n u", n=P, u=2),
-                in_=turned[T][:].rearrange("p (g u) n -> p g n u", u=2),
+                out=grouped[T][:, cols].bitcast(F32).rearrange("p (g n u) -> p g n u", n=P, u=2),
+                in_=turned[T, passes[0]][:].rearrange("p (g u) n -> p g n u", u=2),
             )
 
-        def quant_h(T):
-            h_codes[T] = sb.tile([P, G * P], U32, name=f"h_codes{T}", align_bytes=64)
-            h_scales[T] = sb.tile([P, G * P], U8, name=f"h_scales{T}", align_bytes=64)
-            nc.vector.quantize_mx(out=h_codes[T][:].bitcast(FP8X4), scales=h_scales[T][:], in_=grouped[T][:])
+        def quant_h(T, passes=range(G)):
+            if T not in h_codes:
+                h_codes[T] = sb.tile([P, G * P], U32, name=f"h_codes{T}", align_bytes=64)
+                h_scales[T] = sb.tile([P, G * P], U8, name=f"h_scales{T}", align_bytes=64)
+            first, last = passes[0], passes[-1] + 1
+            nc.vector.quantize_mx(
+                out=h_codes[T][:, P * first : P * last].bitcast(FP8X4),
+                scales=h_scales[T][:, P * first : P * last],
+                in_=grouped[T][:, 512 * first : 512 * last],
+            )
 
         def permute(w):
             for dst, src, x in (
@@ -231,19 +249,21 @@ def tile_generalpreferenceskewembeddingscores_d2p_kernel(
                     in_=src.bitcast(I32).rearrange("p (g q t x) -> p g q t x", g=G, t=4, x=x),
                 )
 
-        def project(w, T):
+        def project(w, T, by_pass=False):
             acc = prod[w, T] = bank(2 + 2 * (T % 2) + w, [P, 4, P], f"prod{w}_{T}")
-            for t in range(4):
-                for g in range(G):
-                    nc.tensor.matmul_mx(
-                        out=acc[:, t, :],
-                        lhsT=w_perm[w][:, g, t, :].bitcast(FP4X4),
-                        lhsT_scale=s_perm[w][:, g, t, :],
-                        rhs=h_codes[T][:, P * g : P * (g + 1)].bitcast(FP8X4),
-                        rhs_scale=h_scales[T][:, P * g : P * (g + 1)],
-                        start=(g == 0),
-                        stop=(g == G - 1),
-                    )
+            steps = [(t, g) for t in range(4) for g in range(G)]
+            if by_pass:
+                steps = [(t, g) for g in range(G) for t in range(4)]
+            for n, (t, g) in enumerate(steps):
+                nc.tensor.matmul_mx(
+                    out=acc[:, t, :],
+                    lhsT=w_perm[w][:, g, t, :].bitcast(FP4X4),
+                    lhsT_scale=s_perm[w][:, g, t, :],
+                    rhs=h_codes[T][:, P * g : P * (g + 1)].bitcast(FP8X4),
+                    rhs_scale=h_scales[T][:, P * g : P * (g + 1)],
+                    start=(n == 0 if by_pass else g == 0),
+                    stop=(n == len(steps) - 1 if by_pass else g == G - 1),
+                )
 
         def emb_run(k, T, count):
             if (k, T // 2) not in emb:
@@ -252,6 +272,7 @@ def tile_generalpreferenceskewembeddingscores_d2p_kernel(
 
         def make_al(T):
             a = T // NT
+            lam = horner[:, :, TERMS].rearrange("p (t a) -> p a t", a=NP)
             nc.vector.tensor_tensor(
                 out=emb_run(AL, T, 1).rearrange("p (n t) -> p n t", t=4),
                 in0=prod[WA, T][:].rearrange("p t n -> p n t"),
@@ -262,7 +283,7 @@ def tile_generalpreferenceskewembeddingscores_d2p_kernel(
         def make_b(T):
             src = prod[WB, T][:].rearrange("p t n -> p n t")
             nc.scalar.copy(out=emb_run(BP, T, 1).rearrange("p (n t) -> p n t", t=4), in_=src)
-            if T >= SCALAR_NEGATES:
+            if T in SCALAR_NEGATES:
                 nc.scalar.activation(
                     out=emb_run(BN, T, 1).rearrange("p (n t) -> p n t", t=4), in_=src, func=ACT.Copy, scale=-1.0
                 )
@@ -357,53 +378,57 @@ def tile_generalpreferenceskewembeddingscores_d2p_kernel(
             nc.sync.dma_start(out=out[a, P * j : P * (j + 1), part], in_=res[T][:, part])
 
         def begin(T):
-            project(WB, T)
+            project(WB, T, T == 0)
             make_b(T)
             if T > 0:
                 make_al(T - 1)
 
         nc.scalar.activation(out=preload[:], in_=tiny[:], func=ACT.Sigmoid)
-        warm_tensor(1)
+        warm_tensor(2)
         gate_order()
         gate_constants()
         spread_scales()
         warm_tensor(2)
+        gate_turn()
+        warm_tensor(1)
         for T in range(3):
             for g in range(G):
                 widen(T, g)
-        for T in range(2):
-            turn(T)
-            warm_tensor(1)
-            copy_turned(T)
-        permute(WB)
-        turn(2)
-        gate_turn()
+        for g in range(G):
+            turn(0, (g,))
+            copy_turned(0, (g,))
         warm_tensor(1)
-        widen(3, 0)
-        quant_h(0)
+        gate_abs()
+        turn(1)
+        copy_turned(1)
+        gate_z()
+        turn(2)
         copy_turned(2)
         gate_square()
+        permute(WB)
+        for g in range(G):
+            quant_h(0, (g,))
         permute(WA)
-        widen(3, 1)
+        widen(3, 0)
         quant_h(1)
 
-        begin(0)
-        widen(4, 0)
-        widen(5, 1)
-        gate_series()
-        widen(4, 1)
-        quant_h(2)
-        widen(5, 0)
+        project(WB, 0, True)
+        make_b(0)
         project(WA, 0)
-
-        begin(1)
-        widen(6, 0)
+        widen(5, 1)
+        for T, g in ((3, 1), (4, 0), (4, 1), (5, 0)):
+            widen(T, g)
+        project(WB, 1)
+        make_b(1)
         project(WA, 1)
+        gate_series()
+        quant_h(2)
+        make_al(0)
+        widen(6, 0)
         for T in (3, 4, 5):
             turn(T)
             copy_turned(T)
-            if T != 4:
-                widen(6 if T == 3 else 7, 1)
+        widen(6, 1)
 
         begin(2)
         quant_h(3)
@@ -413,6 +438,7 @@ def tile_generalpreferenceskewembeddingscores_d2p_kernel(
         quant_h(4)
         project(WA, 2)
 
+        widen(7, 1)
         begin(3)
         quant_h(5)
         quant_emb((AL, BN), 0, 2)
@@ -430,7 +456,6 @@ def tile_generalpreferenceskewembeddingscores_d2p_kernel(
 
         begin(5)
         quant_h(7)
-        negate_b(4, 1)
         project(WA, 5)
 
         begin(6)

@@ -29,8 +29,8 @@ ACT = mybir.ActivationFunctionType
 WB, WA = 0, 1
 AL, BP, BN = 0, 1, 2
 
-SCALAR_WIDENS = ((1, 1), (2, 1), (5, 1), (6, 0), (6, 1), (7, 1))
-SCALAR_NEGATES = (4, 5, 6, 7)
+SCALAR_WIDENS = ((1, 1), (2, 1), (5, 1), (6, 1), (7, 1))
+SCALAR_NEGATES = (5, 6, 7)
 PACKS = ((3,), (0, 2), (1, 5), (4, 6), (7,))
 
 TURN_BANKS = (0, 1, 6, 7)
@@ -456,6 +456,7 @@ def tile_generalpreferenceskewembeddingscores_d2p_kernel(
 
         begin(5)
         quant_h(7)
+        negate_b(4, 1)
         project(WA, 5)
 
         begin(6)

@@ -29,13 +29,13 @@ ACT = mybir.ActivationFunctionType
 WB, WA = 0, 1
 AL, BP, BN = 0, 1, 2
 
-SCALAR_WIDENS = ((1, 1), (2, 1), (5, 1), (6, 1), (7, 1))
+MODES = "AAABABAAAAABABAB"
 SCALAR_NEGATES = (5, 6, 7)
 PACKS = ((3,), (0, 2), (1, 5), (4, 6), (7,))
 
 TURN_BANKS = (0, 1, 6, 7)
-PACK_BANKS = (6, 0, 1, 7, 2)
-UPPER_BANKS = {0: 3, 1: 4, 2: 5, 4: 0, 5: 6, 6: 1}
+PACK_BANKS = (6, 0, 1, 7, 2, 3)
+UPPER_BANKS = {0: 4, 1: 5, 2: 6, 4: 0, 5: 1, 6: 7}
 SPREAD_BANK, WARM_BANK, GATE_BANK = 3, 4, 5
 
 
@@ -59,7 +59,8 @@ def tile_generalpreferenceskewembeddingscores_d2p_kernel(
         w_perm = [sb.tile([P, G, 4, 256], U8, name=f"w_perm{w}", align_bytes=64) for w in range(2)]
         s_raw = [sb.tile([P, G, K], U8, name=f"s_raw{w}", align_bytes=64) for w in range(2)]
         s_perm = [sb.tile([P, G, 4, P], U8, name=f"s_perm{w}", align_bytes=64) for w in range(2)]
-        scales = sb.tile([P, TILES * BLOCKS], F32, name="scales")
+        scales = sb.tile([P, TILES * G], F32, name="scales")
+        row_scales = sb.tile([P, TILES * BLOCKS], F32, name="row_scales")
         scale_col = sb.tile([P, 1], F32, name="scale_col")
         tiny = sb.tile([P, 1], F32, name="tiny")
         odd = sb.tile([P, NP * 4, TERMS], F32, name="odd")
@@ -73,11 +74,11 @@ def tile_generalpreferenceskewembeddingscores_d2p_kernel(
             odd[:], pattern=[[0, NP * 4], [-2, TERMS]], base=2 * TERMS - 1, channel_multiplier=0,
             allow_small_or_imprecise_dtypes=True,
         )
+        nc.vector.memset(zeros[:], 0.0)
         nc.vector.memset(ident[:], 0.0)
         make_identity(nc, ident[:], nomemset=True)
         for w in range(2):
             nc.vector.memset(s_raw[w][:].rearrange("p g k -> p (g k)").bitcast(I32), 0)
-        nc.vector.memset(zeros[:], 0.0)
         nc.vector.memset(gate_rows[:], 0.0)
         nc.vector.memset(scale_col[TILES * BLOCKS : P, :], 0.0)
         nc.vector.memset(tiny[:], TINY)
@@ -111,19 +112,19 @@ def tile_generalpreferenceskewembeddingscores_d2p_kernel(
         )
         load_h(0, 0, 1)
         nc.scalar.dma_start(out=gate_in[0:NP, :], in_=gate)
-        load_h(0, 1, 2)
+        load_h(0, 1, 1)
+        load_h(0, 2, 2)
         load_scale_rows(WB, wb_scales)
         load_words(WB, wb_words)
+        load_h(1, 0, 2)
         load_words(WA, wa_words)
         load_scale_rows(WA, wa_scales)
-        load_h(0, 3, 1)
-        load_h(1, 0, 2)
         load_h(1, 2, 2)
 
-        wide, plain, turned, grouped, h_codes, h_scales, prod, emb = {}, {}, {}, {}, {}, {}, {}, {}
+        wide, turned, grouped, h_codes, h_scales, prod, emb = {}, {}, {}, {}, {}, {}, {}
         e_codes = [sb.tile([P, 3, N], U32, name=f"e_codes{a}", align_bytes=64) for a in range(NP)]
         e_scales = [sb.tile([P, 3, N], U8, name=f"e_scales{a}", align_bytes=64) for a in range(NP)]
-        score, neg_s, sig, logs, res, upper = {}, {}, {}, {}, {}, {}
+        score, neg_s, sig, logs, res, upper, off, shared = {}, {}, {}, {}, {}, {}, {}, {}
         g_abs = sb.tile([P, NP * 4], F32, name="g_abs")
         preload = sb.tile([P, 1], F32, name="preload")
         horner = sb.tile([P, NP * 4, TERMS + 1], F32, name="horner")
@@ -136,9 +137,14 @@ def tile_generalpreferenceskewembeddingscores_d2p_kernel(
         def spread_scales():
             spread = bank(SPREAD_BANK, [P, P], "spread")
             nc.tensor.transpose(spread[:], scale_col[:].to_broadcast([P, P]), ident[:])
-            nc.vector.tensor_copy(out=scales[:], in_=spread[:, 0 : TILES * BLOCKS])
+            nc.vector.tensor_copy(out=row_scales[:], in_=spread[:, 0 : TILES * BLOCKS])
 
-        gate_v = []
+        def pass_scales():
+            for q in range(4):
+                rows = slice(32 * q, 32 * (q + 1))
+                nc.vector.tensor_copy(out=scales[rows, :], in_=row_scales[rows, q : TILES * BLOCKS : 4])
+
+        gate_v, turn_banks, words, plain = [], [], {}, {}
 
         def gate_order():
             nc.scalar.copy(
@@ -186,35 +192,45 @@ def tile_generalpreferenceskewembeddingscores_d2p_kernel(
                 op1=ALU.add,
             )
 
-        def widen(T, g):
+        def widen(T, passes=range(G)):
             t, i = codes_in[T]
-            on_scalar = (T, g) in SCALAR_WIDENS
-            if on_scalar:
-                plain[T, g] = sb.tile([P, 512], BF16, name=f"plain{T}_{g}", align_bytes=64)
-            elif T not in wide:
+            if T not in wide:
                 wide[T] = sb.tile([P, D], BF16, name=f"wide{T}", align_bytes=64)
-            for j in range(4):
-                src = t[:, i, P * (4 * g + j) : P * (4 * g + j + 1)].bitcast(FP8)
-                scale = scales[:, BLOCKS * T + 4 * g + j : BLOCKS * T + 4 * g + j + 1]
-                if on_scalar:
-                    nc.scalar.activation(out=plain[T, g][:, P * j : P * (j + 1)], in_=src, func=ACT.Copy, scale=scale)
-                else:
-                    pairs = wide[T][:, 512 * g : 512 * (g + 1)].rearrange("p (u w e) -> p w u e", u=2, e=2)
-                    nc.vector.tensor_scalar(
-                        out=pairs[:, 32 * j : 32 * (j + 1)],
-                        in0=src.rearrange("p (w u e) -> p w u e", u=2, e=2),
-                        scalar1=scale,
-                        scalar2=None,
-                        op0=ALU.mult,
-                    )
+            first, last = passes[0], passes[-1] + 1
+            if MODES[G * T + first] in "AB":
+                for g in passes:
+                    if MODES[G * T + g] == "B":
+                        plain[T, g] = sb.tile([P, 512], BF16, name=f"plain{T}_{g}", align_bytes=64)
+                    for j in range(4):
+                        src = t[:, i, P * (4 * g + j) : P * (4 * g + j + 1)].bitcast(FP8)
+                        scale = row_scales[:, BLOCKS * T + 4 * g + j : BLOCKS * T + 4 * g + j + 1]
+                        if MODES[G * T + g] == "B":
+                            nc.scalar.activation(out=plain[T, g][:, P * j : P * (j + 1)], in_=src, func=ACT.Copy, scale=scale)
+                        else:
+                            pairs = wide[T][:, 512 * g : 512 * (g + 1)].rearrange("p (u w e) -> p w u e", u=2, e=2)
+                            nc.vector.tensor_scalar(
+                                out=pairs[:, 32 * j : 32 * (j + 1)],
+                                in0=src.rearrange("p (w u e) -> p w u e", u=2, e=2),
+                                scalar1=scale,
+                                scalar2=None,
+                                op0=ALU.mult,
+                            )
+                return
+            nc.gpsimd.tensor_copy(
+                out=wide[T][:, 512 * first : 512 * last], in_=t[:, i, 512 * first : 512 * last].bitcast(FP8)
+            )
 
         def turn(T, passes=range(G)):
-            t = bank(TURN_BANKS[len(turned) % 4], [P, 2 * len(passes), P], f"turned{T}_{passes[0]}")
-            turned[T, passes[0]] = t
+            t = bank(TURN_BANKS[len(turn_banks) % 4], [P, 2 * len(passes), P], f"turned{T}_{passes[0]}")
+            turn_banks.append(t)
+            words[T, passes[0]] = t
             for n, g in enumerate(passes):
+                turned[T, g] = t[:].bitcast(BF16)[:, 2 * n : 2 * n + 2, :]
                 for u in range(2):
-                    if (T, g) in SCALAR_WIDENS:
+                    if MODES[G * T + g] == "B":
                         src = plain[T, g][:].bitcast(F32)[:, u : 256 : 2]
+                    elif MODES[G * T + g] in "CDE":
+                        src = wide[T][:].bitcast(F32)[:, 256 * g + u : 256 * (g + 1) : 2]
                     else:
                         src = wide[T][:].bitcast(F32)[:, 256 * g + P * u : 256 * g + P * (u + 1)]
                     nc.tensor.transpose(t[:, 2 * n + u, :], src, ident[:])
@@ -222,11 +238,29 @@ def tile_generalpreferenceskewembeddingscores_d2p_kernel(
         def copy_turned(T, passes=range(G)):
             if T not in grouped:
                 grouped[T] = sb.tile([P, G * P * 4], BF16, name=f"grouped{T}", align_bytes=64)
-            cols = slice(512 * passes[0], 512 * (passes[-1] + 1))
-            nc.scalar.copy(
-                out=grouped[T][:, cols].bitcast(F32).rearrange("p (g n u) -> p g n u", n=P, u=2),
-                in_=turned[T, passes[0]][:].rearrange("p (g u) n -> p g n u", u=2),
-            )
+            if MODES[G * T + passes[0]] in "ABE":
+                cols = slice(512 * passes[0], 512 * (passes[-1] + 1))
+                nc.scalar.copy(
+                    out=grouped[T][:, cols].bitcast(F32).rearrange("p (g n u) -> p g n u", n=P, u=2),
+                    in_=words[T, passes[0]][:].rearrange("p (g u) n -> p g n u", u=2),
+                )
+                return
+            for g in passes:
+                on_vector = MODES[G * T + g] == "D"
+                dst = grouped[T][:, 512 * g : 512 * (g + 1)].rearrange("p (n u e) -> p n u e", u=2, e=2)
+                src = turned[T, g].rearrange("p u (n e) -> p n u e", e=2)
+                scale = scales[:, G * T + g : G * T + g + 1]
+                if on_vector:
+                    nc.vector.tensor_scalar(out=dst, in0=src, scalar1=scale, scalar2=None, op0=ALU.mult)
+                else:
+                    nc.scalar.activation(out=dst, in_=src, func=ACT.Copy, scale=scale)
+
+        def scale_h(T, passes=range(G)):
+            for g in passes:
+                cols = grouped[T][:, 512 * g : 512 * (g + 1)]
+                nc.vector.tensor_scalar(
+                    out=cols, in0=cols, scalar1=scales[:, G * T + g : G * T + g + 1], scalar2=None, op0=ALU.mult
+                )
 
         def quant_h(T, passes=range(G)):
             if T not in h_codes:
@@ -239,11 +273,12 @@ def tile_generalpreferenceskewembeddingscores_d2p_kernel(
                 in_=grouped[T][:, 512 * first : 512 * last],
             )
 
-        def permute(w):
-            for dst, src, x in (
+        def permute(w, parts=(0, 1)):
+            both = (
                 (w_perm[w][:].rearrange("p g t b -> p (g t b)"), w_raw[w][:].rearrange("p g b -> p (g b)"), 4),
                 (s_perm[w][:].rearrange("p g t b -> p (g t b)"), s_raw[w][:].rearrange("p g b -> p (g b)"), 2),
-            ):
+            )
+            for dst, src, x in [both[n] for n in parts]:
                 nc.vector.tensor_copy(
                     out=dst.bitcast(I32).rearrange("p (g t q x) -> p g q t x", g=G, t=4, x=x),
                     in_=src.bitcast(I32).rearrange("p (g q t x) -> p g q t x", g=G, t=4, x=x),
@@ -280,9 +315,12 @@ def tile_generalpreferenceskewembeddingscores_d2p_kernel(
                 op=ALU.mult,
             )
 
-        def make_b(T):
+        def make_b(T, on_vector=False):
             src = prod[WB, T][:].rearrange("p t n -> p n t")
-            nc.scalar.copy(out=emb_run(BP, T, 1).rearrange("p (n t) -> p n t", t=4), in_=src)
+            if on_vector:
+                nc.vector.tensor_copy(out=emb_run(BP, T, 1).rearrange("p (n t) -> p n t", t=4), in_=src)
+            else:
+                nc.scalar.copy(out=emb_run(BP, T, 1).rearrange("p (n t) -> p n t", t=4), in_=src)
             if T in SCALAR_NEGATES:
                 nc.scalar.activation(
                     out=emb_run(BN, T, 1).rearrange("p (n t) -> p n t", t=4), in_=src, func=ACT.Copy, scale=-1.0
@@ -307,8 +345,10 @@ def tile_generalpreferenceskewembeddingscores_d2p_kernel(
                 place[T] = (n, slice(first, first + P * (T % NT + 1)))
                 first = place[T][1].stop
 
+        pack_width = [place[pack[-1]][1].stop for pack in PACKS][0:4] + [256, 256]
+
         def scores(n):
-            score[n] = bank(PACK_BANKS[n], [P, N], f"score{n}")
+            score[n] = bank(PACK_BANKS[n], [P, pack_width[n]], f"score{n}")
             for T in PACKS[n]:
                 a, j = divmod(T, NT)
                 width = P * (j + 1)
@@ -326,16 +366,50 @@ def tile_generalpreferenceskewembeddingscores_d2p_kernel(
                             start=(stationary == BN),
                             stop=(stationary == AL),
                         )
-            sig[n] = sb.tile([P, N], F32, name=f"sig{n}")
+
+        def score_pass(T, stationary, lo, hi, start, stop):
+            a, j = divmod(T, NT)
+            n, cols = half_place(T, lo)
+            if n not in score:
+                score[n] = bank(PACK_BANKS[n], [P, pack_width[n]], f"score{n}")
+            moving = AL if stationary == BN else BP
+            rows = slice(P * j, P * (j + 1))
+            nc.tensor.matmul_mx(
+                out=score[n][:, lo - cols : hi - cols],
+                lhsT=e_codes[a][:, stationary, rows].bitcast(FP8X4),
+                lhsT_scale=e_scales[a][:, stationary, rows],
+                rhs=e_codes[a][:, moving, lo:hi].bitcast(FP8X4),
+                rhs_scale=e_scales[a][:, moving, lo:hi],
+                start=start,
+                stop=stop,
+            )
+
+        def half_place(T, lo):
+            return (4, 0) if lo < 256 else (5, 256)
+
+        def lower_half(h):
+            if 7 not in res:
+                res[7] = sb.tile([P, N], F32, name="res7")
+            nc.vector.scalar_tensor_tensor(
+                out=res[7][:, 256 * h : 256 * (h + 1)], in0=neg7[:, 256 * h : 256 * (h + 1)], scalar=-1.0, in1=logs[4 + h][:], op0=ALU.mult, op1=ALU.min
+            )
+
+        neg7 = sb.tile([P, N], F32, name="neg7")
+
+        def keep_half(h):
+            nc.vector.tensor_scalar(out=neg7[:, 256 * h : 256 * (h + 1)], in0=score[4 + h][:], scalar1=-C, scalar2=None, op0=ALU.mult)
+
+        def sigmoid(n):
+            sig[n] = sb.tile([P, pack_width[n]], F32, name=f"sig{n}")
             nc.scalar.activation(out=sig[n][:], in_=score[n][:], func=ACT.Sigmoid, scale=C)
 
         def keep_neg_s(n):
-            neg_s[n] = sb.tile([P, N], F32, name=f"neg_s{n}")
+            neg_s[n] = sb.tile([P, pack_width[n]], F32, name=f"neg_s{n}")
             nc.vector.tensor_scalar(out=neg_s[n][:], in0=score[n][:], scalar1=-C, scalar2=None, op0=ALU.mult)
 
         def log(n, cols):
             if n not in logs:
-                logs[n] = sb.tile([P, N], F32, name=f"logs{n}")
+                logs[n] = sb.tile([P, pack_width[n]], F32, name=f"logs{n}")
             nc.scalar.activation(out=logs[n][:, cols], in_=sig[n][:, cols], func=ACT.Ln, bias=tiny[:])
 
         def lower(T, part):
@@ -351,9 +425,53 @@ def tile_generalpreferenceskewembeddingscores_d2p_kernel(
                 op1=ALU.min,
             )
 
+        def lower_ps(T, part):
+            n, cols = place[T]
+            if T not in res:
+                res[T] = sb.tile([P, N], F32, name=f"res{T}")
+            nc.vector.scalar_tensor_tensor(
+                out=res[T][:, part],
+                in0=score[n][:, cols][:, part],
+                scalar=C,
+                in1=logs[n][:, cols][:, part],
+                op0=ALU.mult,
+                op1=ALU.min,
+            )
+
+        def keep_off(T):
+            n, cols = place[T]
+            width = P * (T % NT)
+            off[T] = sb.tile([P, width], F32, name=f"off{T}")
+            nc.vector.tensor_scalar(
+                out=off[T][:], in0=score[n][:, cols][:, 0:width], scalar1=-C, scalar2=None, op0=ALU.mult
+            )
+
+        def upper_t(T):
+            n, cols = place[T]
+            width = P * (T % NT)
+            off[T] = sb.tile([P, width], F32, name=f"off{T}")
+            nc.vector.scalar_tensor_tensor(
+                out=off[T][:],
+                in0=score[n][:, cols][:, 0:width],
+                scalar=-C,
+                in1=res[T][:, 0:width],
+                op0=ALU.mult,
+                op1=ALU.add,
+            )
+
+        def turn_upper(row, b, first=0):
+            a, i = divmod(row, NT)
+            if first == 0:
+                shared[b] = bank(b, [P, N], f"upper{row}")
+            upper[row] = shared[b][:, first : first + N - P * (i + 1)]
+            for j in range(i + 1, NT):
+                nc.tensor.transpose(
+                    upper[row][:, P * (j - i - 1) : P * (j - i)], off[a * NT + j][:, P * i : P * (i + 1)], ident[:]
+                )
+
         def mirror(src, T, opening):
             a, j = divmod(T, NT)
-            for i in range(j):
+            for i in reversed(range(j)):
                 row = a * NT + i
                 if row not in upper:
                     upper[row] = bank(UPPER_BANKS[row], [P, N - P * (i + 1)], f"upper{row}")
@@ -388,112 +506,128 @@ def tile_generalpreferenceskewembeddingscores_d2p_kernel(
         gate_order()
         gate_constants()
         spread_scales()
-        warm_tensor(2)
+        warm_tensor(1)
         gate_turn()
         warm_tensor(1)
-        for T in range(3):
+        for T in range(2):
             for g in range(G):
-                widen(T, g)
-        for g in range(G):
-            turn(0, (g,))
-            copy_turned(0, (g,))
+                widen(T, (g,))
+        widen(2, (1,))
+        widen(3)
+        widen(2, (0,))
+        turn(0)
+        warm_tensor(1)
+        turn(1)
         warm_tensor(1)
         gate_abs()
-        turn(1)
-        copy_turned(1)
+        copy_turned(0)
         gate_z()
-        turn(2)
-        copy_turned(2)
+        copy_turned(1)
         gate_square()
-        permute(WB)
-        for g in range(G):
-            quant_h(0, (g,))
-        permute(WA)
-        widen(3, 0)
+        turn(2)
+        turn(3)
+        copy_turned(2)
+        permute(WB, (1,))
+        quant_h(0)
+        permute(WB, (0,))
         quant_h(1)
-
-        project(WB, 0, True)
-        make_b(0)
-        project(WA, 0)
-        widen(5, 1)
-        for T, g in ((3, 1), (4, 0), (4, 1), (5, 0)):
-            widen(T, g)
+        permute(WA)
+        project(WB, 0)
         project(WB, 1)
-        make_b(1)
+        project(WA, 0)
         project(WA, 1)
-        gate_series()
+        widen(5)
+        make_b(0)
         quant_h(2)
+        widen(4, (0,))
+        gate_series()
+        widen(4, (1,))
+        widen(6)
+        make_b(1)
+        project(WB, 2)
+        copy_turned(3)
         make_al(0)
-        widen(6, 0)
-        for T in (3, 4, 5):
-            turn(T)
-            copy_turned(T)
-        widen(6, 1)
-
-        begin(2)
-        quant_h(3)
-        widen(7, 0)
-        negate_b(0, 2)
-        quant_emb((BP,), 0, 2)
-        quant_h(4)
+        make_al(1)
+        turn(4)
+        turn(5)
+        copy_turned(4)
+        make_b(2)
+        copy_turned(5)
         project(WA, 2)
-
-        widen(7, 1)
+        quant_h(3)
+        widen(7)
+        quant_h(4)
+        quant_emb((BP,), 0, 2)
         begin(3)
-        quant_h(5)
-        quant_emb((AL, BN), 0, 2)
         project(WA, 3)
+        quant_h(5)
+        negate_b(0, 2)
+        begin(4)
         for T in (6, 7):
             turn(T)
             copy_turned(T)
-
-        begin(4)
         negate_b(2, 2)
+        quant_emb((AL, BN), 0, 2)
+        project(WA, 4)
         quant_emb((BP,), 2, 2)
         quant_h(6)
-        quant_emb((AL, BN), 2, 2)
-        project(WA, 4)
-
         begin(5)
+        quant_emb((AL, BN), 2, 2)
         quant_h(7)
-        negate_b(4, 1)
         project(WA, 5)
-
         begin(6)
+        scores(0)
+        sigmoid(0)
+        negate_b(4, 1)
         quant_emb((BP, AL, BN), 4, 2)
         project(WA, 6)
-
         begin(7)
+        scores(1)
+        sigmoid(1)
         quant_emb((BP, AL, BN), 6, 1)
         quant_emb((BP,), 7, 1)
-        scores(0)
         project(WA, 7)
         make_al(7)
         quant_emb((BN, AL), 7, 1)
-        for n in range(1, len(PACKS)):
+        for n in range(2, 4):
             scores(n)
-
-        for n in range(len(PACKS)):
+            sigmoid(n)
+        score_pass(7, BN, 0, 256, True, False)
+        score_pass(7, BN, 256, 384, True, False)
+        score_pass(7, AL, 0, 256, False, True)
+        sigmoid(4)
+        score_pass(7, BN, 384, 512, False, False)
+        score_pass(7, AL, 256, 512, False, True)
+        sigmoid(5)
+        for n in range(4):
             keep_neg_s(n)
+        for h in range(2):
+            keep_half(h)
         for a in range(NP):
             for T in range(a * NT + NT - 1, a * NT, -1):
                 n, cols = place[T]
-                mirror(neg_s[n][:, cols], T, True)
+                mirror(neg7 if T == 7 else neg_s[n][:, cols], T, True)
         whole = slice(0, N)
-        for T in (3, 7):
-            for half in (slice(0, N // 2), slice(N // 2, N)):
-                log(place[T][0], half)
-                lower(T, half)
-                store(T, half)
-            mirror(res[T], T, False)
+        for part in (slice(0, 256), slice(256, 512)):
+            log(0, part)
+            lower(3, part)
+            store(3, part)
+        mirror(res[3], 3, False)
+        for h in range(2):
+            log(4 + h, slice(0, 256))
+            lower_half(h)
+            store(7, slice(256 * h, 256 * (h + 1)))
+        mirror(res[7], 7, False)
         for T in (2, 6):
             log(*place[T])
         log(place[1][0], whole)
         for T in (0, 4):
             log(*place[T])
+        res[2] = sb.tile([P, N], F32, name="res2")
+        res[6] = sb.tile([P, N], F32, name="res6")
         for T in (2, 6):
-            lower(T, slice(0, 3 * P))
             copy_upper(T, True)
+            lower(T, slice(0, 3 * P))
             store(T, whole)
             mirror(res[T], T, False)
         for T in (1, 5):

@@ -27,8 +27,9 @@ ALU = mybir.AluOpType
 ACT = mybir.ActivationFunctionType
 
 WB, WA = 0, 1
-AL, BP, BN = 0, 1, 2
+BP, BN, AL = 0, 1, 2
 
+SINGLE_FROM = 6
 MODES = "AAABABAAAAABABAB"
 SCALAR_NEGATES = (5, 6, 7)
 PACKS = ((3,), (0, 2), (1, 5), (4, 6), (7,))
@@ -122,8 +123,8 @@ def tile_generalpreferenceskewembeddingscores_d2p_kernel(
         load_h(1, 2, 2)
 
         wide, turned, grouped, h_codes, h_scales, prod, emb = {}, {}, {}, {}, {}, {}, {}
-        e_codes = [sb.tile([P, 3, N], U32, name=f"e_codes{a}", align_bytes=64) for a in range(NP)]
-        e_scales = [sb.tile([P, 3, N], U8, name=f"e_scales{a}", align_bytes=64) for a in range(NP)]
+        e_codes = [sb.tile([P, 3 * N], U32, name=f"e_codes{a}", align_bytes=64) for a in range(NP)]
+        e_scales = [sb.tile([P, 3 * N], U8, name=f"e_scales{a}", align_bytes=64) for a in range(NP)]
         score, neg_s, sig, logs, res, upper, off, shared = {}, {}, {}, {}, {}, {}, {}, {}
         g_abs = sb.tile([P, NP * 4], F32, name="g_abs")
         preload = sb.tile([P, 1], F32, name="preload")
@@ -147,7 +148,7 @@ def tile_generalpreferenceskewembeddingscores_d2p_kernel(
         gate_v, turn_banks, words, plain = [], [], {}, {}
 
         def gate_order():
-            nc.scalar.copy(
+            nc.vector.tensor_copy(
                 out=gate_rows[0:NP, :].rearrange("a (t q r) -> a t q r", t=4, r=8),
                 in_=gate_in[0:NP, :].rearrange("a (q t r) -> a t q r", t=4, r=8),
             )
@@ -300,10 +301,20 @@ def tile_generalpreferenceskewembeddingscores_d2p_kernel(
                     stop=(n == len(steps) - 1 if by_pass else g == G - 1),
                 )
 
+        def column(k, T):
+            j = T % NT
+            if T >= SINGLE_FROM:
+                return 3 * P * j + P * k
+            return 6 * P * (j // 2) + 2 * P * k + P * (j % 2)
+
+        def emb_cols(T, first, width):
+            if T // 2 not in emb:
+                emb[T // 2] = sb.tile([P, 6 * 512], BF16, name=f"emb{T // 2}", align_bytes=64)
+            first = first - 6 * P * (T % NT // 2)
+            return emb[T // 2][:, 4 * first : 4 * (first + width)]
+
         def emb_run(k, T, count):
-            if (k, T // 2) not in emb:
-                emb[k, T // 2] = sb.tile([P, 2, 512], BF16, name=f"emb{k}_{T // 2}", align_bytes=64)
-            return emb[k, T // 2][:, T % 2 : T % 2 + count, :].rearrange("p i n -> p (i n)")
+            return emb_cols(T, column(k, T), P * count)
 
         def make_al(T):
             a = T // NT
@@ -332,11 +343,26 @@ def tile_generalpreferenceskewembeddingscores_d2p_kernel(
             )
 
         def quant_emb(kinds, T, count):
-            a, cols = T // NT, slice(P * (T % NT), P * (T % NT + count))
-            for k in kinds:
-                nc.vector.quantize_mx(
-                    out=e_codes[a][:, k, cols].bitcast(FP8X4), scales=e_scales[a][:, k, cols], in_=emb_run(k, T, count)
-                )
+            a, first, width = T // NT, column(kinds[0], T), P * count * len(kinds)
+            nc.vector.quantize_mx(
+                out=e_codes[a][:, first : first + width].bitcast(FP8X4),
+                scales=e_scales[a][:, first : first + width],
+                in_=emb_cols(T, first, width),
+            )
+
+        def mx_pass(x, stationary, T, first, count, start, stop):
+            a, moving = T // NT, AL if stationary == BN else BP
+            rows = slice(column(stationary, T), column(stationary, T) + P)
+            cols = slice(column(moving, first), column(moving, first) + P * count)
+            nc.tensor.matmul_mx(
+                out=x,
+                lhsT=e_codes[a][:, rows].bitcast(FP8X4),
+                lhsT_scale=e_scales[a][:, rows],
+                rhs=e_codes[a][:, cols].bitcast(FP8X4),
+                rhs_scale=e_scales[a][:, cols],
+                start=start,
+                stop=stop,
+            )
 
         place = {}
         for n, pack in enumerate(PACKS):
@@ -353,18 +379,12 @@ def tile_generalpreferenceskewembeddingscores_d2p_kernel(
                 a, j = divmod(T, NT)
                 width = P * (j + 1)
                 x = score[n][:, place[T][1]]
-                rows = slice(P * j, P * (j + 1))
-                cuts = [(0, 256), (256, 384)] if width == 384 else [(0, width)]
-                for lo, hi in cuts:
-                    for stationary, moving in ((BN, AL), (AL, BP)):
-                        nc.tensor.matmul_mx(
-                            out=x[:, lo:hi],
-                            lhsT=e_codes[a][:, stationary, rows].bitcast(FP8X4),
-                            lhsT_scale=e_scales[a][:, stationary, rows],
-                            rhs=e_codes[a][:, moving, lo:hi].bitcast(FP8X4),
-                            rhs_scale=e_scales[a][:, moving, lo:hi],
-                            start=(stationary == BN),
-                            stop=(stationary == AL),
+                for i in range(0, j + 1, 2):
+                    count = min(2, j + 1 - i)
+                    for stationary in (BN, AL):
+                        mx_pass(
+                            x[:, P * i : P * (i + count)], stationary, T, a * NT + i, count,
+                            stationary == BN, stationary == AL,
                         )
 
         def score_pass(T, stationary, lo, hi, start, stop):
@@ -372,17 +392,7 @@ def tile_generalpreferenceskewembeddingscores_d2p_kernel(
             n, cols = half_place(T, lo)
             if n not in score:
                 score[n] = bank(PACK_BANKS[n], [P, pack_width[n]], f"score{n}")
-            moving = AL if stationary == BN else BP
-            rows = slice(P * j, P * (j + 1))
-            nc.tensor.matmul_mx(
-                out=score[n][:, lo - cols : hi - cols],
-                lhsT=e_codes[a][:, stationary, rows].bitcast(FP8X4),
-                lhsT_scale=e_scales[a][:, stationary, rows],
-                rhs=e_codes[a][:, moving, lo:hi].bitcast(FP8X4),
-                rhs_scale=e_scales[a][:, moving, lo:hi],
-                start=start,
-                stop=stop,
-            )
+            mx_pass(score[n][:, lo - cols : hi - cols], stationary, T, a * NT + lo // P, (hi - lo) // P, start, stop)
 
         def half_place(T, lo):
             return (4, 0) if lo < 256 else (5, 256)
@@ -503,9 +513,9 @@ def tile_generalpreferenceskewembeddingscores_d2p_kernel(
 
         nc.scalar.activation(out=preload[:], in_=tiny[:], func=ACT.Sigmoid)
         warm_tensor(2)
-        gate_order()
         gate_constants()
         spread_scales()
+        gate_order()
         warm_tensor(1)
         gate_turn()
         warm_tensor(1)
@@ -557,39 +567,38 @@ def tile_generalpreferenceskewembeddingscores_d2p_kernel(
         quant_h(3)
         widen(7)
         quant_h(4)
-        quant_emb((BP,), 0, 2)
         begin(3)
         project(WA, 3)
-        quant_h(5)
         negate_b(0, 2)
+        quant_h(5)
+        quant_emb((BP, BN), 0, 2)
         begin(4)
         for T in (6, 7):
             turn(T)
             copy_turned(T)
         negate_b(2, 2)
-        quant_emb((AL, BN), 0, 2)
+        quant_emb((AL,), 0, 2)
         project(WA, 4)
-        quant_emb((BP,), 2, 2)
+        quant_emb((BP, BN), 2, 2)
         quant_h(6)
         begin(5)
-        quant_emb((AL, BN), 2, 2)
+        quant_emb((AL,), 2, 2)
         quant_h(7)
         project(WA, 5)
         begin(6)
         scores(0)
         sigmoid(0)
         negate_b(4, 1)
-        quant_emb((BP, AL, BN), 4, 2)
+        quant_emb((AL,), 4, 2)
         project(WA, 6)
         begin(7)
-        scores(1)
-        sigmoid(1)
-        quant_emb((BP, AL, BN), 6, 1)
-        quant_emb((BP,), 7, 1)
+        quant_emb((BP, BN), 4, 2)
+        quant_emb((BP, BN, AL), 6, 1)
         project(WA, 7)
         make_al(7)
-        quant_emb((BN, AL), 7, 1)
-        for n in range(2, 4):
+        quant_emb((BP, BN), 7, 1)
+        quant_emb((AL,), 7, 1)
+        for n in range(1, 4):
             scores(n)
             sigmoid(n)
         score_pass(7, BN, 0, 256, True, False)
@@ -597,7 +606,8 @@ def tile_generalpreferenceskewembeddingscores_d2p_kernel(
         score_pass(7, AL, 0, 256, False, True)
         sigmoid(4)
         score_pass(7, BN, 384, 512, False, False)
-        score_pass(7, AL, 256, 512, False, True)
+        score_pass(7, AL, 256, 384, False, False)
+        score_pass(7, AL, 384, 512, False, True)
         sigmoid(5)
         for n in range(4):
             keep_neg_s(n)
@@ -620,20 +630,25 @@ def tile_generalpreferenceskewembeddingscores_d2p_kernel(
         mirror(res[7], 7, False)
         for T in (2, 6):
             log(*place[T])
-        log(place[1][0], whole)
-        for T in (0, 4):
-            log(*place[T])
         res[2] = sb.tile([P, N], F32, name="res2")
         res[6] = sb.tile([P, N], F32, name="res6")
-        for T in (2, 6):
-            copy_upper(T, True)
-            lower(T, slice(0, 3 * P))
-            store(T, whole)
-            mirror(res[T], T, False)
+        copy_upper(2, False)
+        lower(2, slice(0, 2 * P))
+        store(2, slice(0, 2 * P))
+        mirror(res[2], 2, False)
+        lower(2, slice(2 * P, 3 * P))
+        store(2, slice(2 * P, N))
+        log(*place[1])
+        copy_upper(6, False)
+        lower(6, slice(0, 3 * P))
+        store(6, whole)
+        mirror(res[6], 6, False)
+        for T in (5, 0, 4):
+            log(*place[T])
         for T in (1, 5):
             lower(T, slice(0, 2 * P))
             mirror(res[T], T, False)
-            copy_upper(T, False)
+            copy_upper(T, T == 1)
             store(T, whole)
         for T in (0, 4):
             lower(T, slice(0, P))

@@ -125,7 +125,9 @@ def tile_generalpreferenceskewembeddingscores_d2p_kernel(
         wide, turned, grouped, h_codes, h_scales, prod, emb = {}, {}, {}, {}, {}, {}, {}
         e_codes = [sb.tile([P, 3 * N], U32, name=f"e_codes{a}", align_bytes=64) for a in range(NP)]
         e_scales = [sb.tile([P, 3 * N], U8, name=f"e_scales{a}", align_bytes=64) for a in range(NP)]
-        score, neg_s, sig, logs, res, upper, off, shared = {}, {}, {}, {}, {}, {}, {}, {}
+        score, neg_s, sig, logs, upper, off, shared = {}, {}, {}, {}, {}, {}, {}
+        rows_out = [sb.tile([P, NP * N], F32, name=f"rows_out{j}") for j in range(NT)]
+        res = {T: rows_out[T % NT][:, N * (T // NT) : N * (T // NT + 1)] for T in range(TILES)}
         g_abs = sb.tile([P, NP * 4], F32, name="g_abs")
         preload = sb.tile([P, 1], F32, name="preload")
         horner = sb.tile([P, NP * 4, TERMS + 1], F32, name="horner")
@@ -326,16 +328,14 @@ def tile_generalpreferenceskewembeddingscores_d2p_kernel(
                 op=ALU.mult,
             )
 
-        def make_b(T, on_vector=False):
+        def make_b(T, kinds=None):
             src = prod[WB, T][:].rearrange("p t n -> p n t")
-            if on_vector:
-                nc.vector.tensor_copy(out=emb_run(BP, T, 1).rearrange("p (n t) -> p n t", t=4), in_=src)
-            else:
-                nc.scalar.copy(out=emb_run(BP, T, 1).rearrange("p (n t) -> p n t", t=4), in_=src)
-            if T in SCALAR_NEGATES:
-                nc.scalar.activation(
-                    out=emb_run(BN, T, 1).rearrange("p (n t) -> p n t", t=4), in_=src, func=ACT.Copy, scale=-1.0
-                )
+            for k in kinds or ((BP, BN) if T in SCALAR_NEGATES else (BP,)):
+                dst = emb_run(k, T, 1).rearrange("p (n t) -> p n t", t=4)
+                if k == BP:
+                    nc.scalar.copy(out=dst, in_=src)
+                else:
+                    nc.scalar.activation(out=dst, in_=src, func=ACT.Copy, scale=-1.0)
 
         def negate_b(T, count):
             nc.vector.tensor_scalar(
@@ -398,8 +398,6 @@ def tile_generalpreferenceskewembeddingscores_d2p_kernel(
             return (4, 0) if lo < 256 else (5, 256)
 
         def lower_half(h):
-            if 7 not in res:
-                res[7] = sb.tile([P, N], F32, name="res7")
             nc.vector.scalar_tensor_tensor(
                 out=res[7][:, 256 * h : 256 * (h + 1)], in0=neg7[:, 256 * h : 256 * (h + 1)], scalar=-1.0, in1=logs[4 + h][:], op0=ALU.mult, op1=ALU.min
             )
@@ -424,8 +422,6 @@ def tile_generalpreferenceskewembeddingscores_d2p_kernel(
 
         def lower(T, part):
             n, cols = place[T]
-            if T not in res:
-                res[T] = sb.tile([P, N], F32, name=f"res{T}")
             nc.vector.scalar_tensor_tensor(
                 out=res[T][:, part],
                 in0=neg_s[n][:, cols][:, part],
@@ -437,8 +433,6 @@ def tile_generalpreferenceskewembeddingscores_d2p_kernel(
 
         def lower_ps(T, part):
             n, cols = place[T]
-            if T not in res:
-                res[T] = sb.tile([P, N], F32, name=f"res{T}")
             nc.vector.scalar_tensor_tensor(
                 out=res[T][:, part],
                 in0=score[n][:, cols][:, part],
@@ -501,12 +495,18 @@ def tile_generalpreferenceskewembeddingscores_d2p_kernel(
             else:
                 nc.scalar.copy(out=res[T][:, cols], in_=upper[T][:])
 
-        def store(T, part):
+        def store(T, part, queue=nc.sync):
             a, j = divmod(T, NT)
-            nc.sync.dma_start(out=out[a, P * j : P * (j + 1), part], in_=res[T][:, part])
+            queue.dma_start(out=out[a, P * j : P * (j + 1), part], in_=res[T][:, part])
+
+        def store_both(j):
+            nc.sync.dma_start(
+                out=out[:, P * j : P * (j + 1), :].rearrange("a p n -> p a n"),
+                in_=rows_out[j][:].rearrange("p (a n) -> p a n", a=NP),
+            )
 
         def begin(T):
-            project(WB, T, T == 0)
+            project(WB, T)
             make_b(T)
             if T > 0:
                 make_al(T - 1)
@@ -523,8 +523,8 @@ def tile_generalpreferenceskewembeddingscores_d2p_kernel(
             for g in range(G):
                 widen(T, (g,))
         widen(2, (1,))
-        widen(3)
         widen(2, (0,))
+        widen(3)
         turn(0)
         warm_tensor(1)
         turn(1)
@@ -537,9 +537,8 @@ def tile_generalpreferenceskewembeddingscores_d2p_kernel(
         turn(2)
         turn(3)
         copy_turned(2)
-        permute(WB, (1,))
+        permute(WB)
         quant_h(0)
-        permute(WB, (0,))
         quant_h(1)
         permute(WA)
         project(WB, 0)
@@ -549,50 +548,57 @@ def tile_generalpreferenceskewembeddingscores_d2p_kernel(
         widen(5)
         make_b(0)
         quant_h(2)
+        copy_turned(3)
         widen(4, (0,))
         gate_series()
-        widen(4, (1,))
-        widen(6)
         make_b(1)
-        project(WB, 2)
-        copy_turned(3)
+        widen(6, (1,))
+        widen(4, (1,))
         make_al(0)
-        make_al(1)
-        turn(4)
-        turn(5)
-        copy_turned(4)
-        make_b(2)
-        copy_turned(5)
-        project(WA, 2)
         quant_h(3)
-        widen(7)
-        quant_h(4)
-        begin(3)
-        project(WA, 3)
-        negate_b(0, 2)
-        quant_h(5)
-        quant_emb((BP, BN), 0, 2)
-        begin(4)
-        for T in (6, 7):
+        project(WB, 2)
+        project(WA, 2)
+        widen(7, (1,))
+        widen(6, (0,))
+        make_al(1)
+        widen(7, (0,))
+        make_b(2)
+        project(WB, 3)
+        for T in (4, 5, 6, 7):
             turn(T)
-            copy_turned(T)
-        negate_b(2, 2)
+        project(WA, 3)
+        make_al(2)
+        negate_b(0, 2)
+        copy_turned(4)
+        copy_turned(5)
+        make_b(3)
         quant_emb((AL,), 0, 2)
+        quant_h(4)
+        quant_emb((BP, BN), 0, 2)
+        project(WB, 4)
         project(WA, 4)
+        copy_turned(6)
+        quant_h(5)
+        negate_b(2, 2)
+        make_al(3)
+        make_b(4)
+        copy_turned(7)
+        project(WB, 5)
         quant_emb((BP, BN), 2, 2)
         quant_h(6)
-        begin(5)
-        quant_emb((AL,), 2, 2)
-        quant_h(7)
+        make_al(4)
         project(WA, 5)
+        make_b(5)
+        quant_emb((AL,), 2, 2)
+        negate_b(4, 1)
+        quant_h(7)
         begin(6)
         scores(0)
         sigmoid(0)
-        negate_b(4, 1)
-        quant_emb((AL,), 4, 2)
+        quant_emb((BP, BN), 4, 2)
         project(WA, 6)
         begin(7)
-        quant_emb((BP, BN), 4, 2)
+        quant_emb((AL,), 4, 2)
         quant_emb((BP, BN, AL), 6, 1)
         project(WA, 7)
         make_al(7)
@@ -630,8 +636,6 @@ def tile_generalpreferenceskewembeddingscores_d2p_kernel(
         mirror(res[7], 7, False)
         for T in (2, 6):
             log(*place[T])
-        res[2] = sb.tile([P, N], F32, name="res2")
-        res[6] = sb.tile([P, N], F32, name="res6")
         copy_upper(2, False)
         lower(2, slice(0, 2 * P))
         store(2, slice(0, 2 * P))

@@ -29,13 +29,19 @@ ACT = mybir.ActivationFunctionType
 WB, WA = 0, 1
 BP, BN, AL = 0, 1, 2
 
+MX_ALIGN = 256
+
+SCALAR_WIDENS = (1, 2, 5, 6, 7)
+REGROUPED = (7,)
+SCALAR_NEGATES = 5
 SINGLE_FROM = 6
-MODES = "AAABABAAAAABABAB"
-SCALAR_NEGATES = (5, 6, 7)
-PACKS = ((3,), (0, 2), (1, 5), (4, 6), (7,))
+
+ROW_ORDER = (3, 0, 2, 1, 5, 4, 6, 7)
+TRIANGLE = NP * P * NT * (NT + 1) // 2
+PIECES = [(lo, lo + N) for lo in range(0, TRIANGLE - N, N)] + [(lo, lo + N // 2) for lo in (TRIANGLE - N, TRIANGLE - N // 2)]
 
 TURN_BANKS = (0, 1, 6, 7)
-PACK_BANKS = (6, 0, 1, 7, 2, 3)
+PIECE_BANKS = (6, 0, 1, 7, 2, 3)
 UPPER_BANKS = {0: 4, 1: 5, 2: 6, 4: 0, 5: 1, 6: 7}
 SPREAD_BANK, WARM_BANK, GATE_BANK = 3, 4, 5
 
@@ -57,11 +63,10 @@ def tile_generalpreferenceskewembeddingscores_d2p_kernel(
         ident = sb.tile([P, P], F32, name="ident")
         pick = sb.tile([P, NP], BF16, name="pick")
         w_raw = [sb.tile([P, G, 1024], U8, name=f"w_raw{w}", align_bytes=64) for w in range(2)]
-        w_perm = [sb.tile([P, G, 4, 256], U8, name=f"w_perm{w}", align_bytes=64) for w in range(2)]
+        w_perm = [sb.tile([P, G, 4, 256], U8, name=f"w_perm{w}", align_bytes=MX_ALIGN) for w in range(2)]
         s_raw = [sb.tile([P, G, K], U8, name=f"s_raw{w}", align_bytes=64) for w in range(2)]
-        s_perm = [sb.tile([P, G, 4, P], U8, name=f"s_perm{w}", align_bytes=64) for w in range(2)]
-        scales = sb.tile([P, TILES * G], F32, name="scales")
-        row_scales = sb.tile([P, TILES * BLOCKS], F32, name="row_scales")
+        s_perm = [sb.tile([P, G, 4, P], U8, name=f"s_perm{w}", align_bytes=MX_ALIGN) for w in range(2)]
+        scales = sb.tile([P, TILES * BLOCKS], F32, name="scales")
         scale_col = sb.tile([P, 1], F32, name="scale_col")
         tiny = sb.tile([P, 1], F32, name="tiny")
         odd = sb.tile([P, NP * 4, TERMS], F32, name="odd")
@@ -122,12 +127,14 @@ def tile_generalpreferenceskewembeddingscores_d2p_kernel(
         load_scale_rows(WA, wa_scales)
         load_h(1, 2, 2)
 
-        wide, turned, grouped, h_codes, h_scales, prod, emb = {}, {}, {}, {}, {}, {}, {}
-        e_codes = [sb.tile([P, 3 * N], U32, name=f"e_codes{a}", align_bytes=64) for a in range(NP)]
-        e_scales = [sb.tile([P, 3 * N], U8, name=f"e_scales{a}", align_bytes=64) for a in range(NP)]
-        score, neg_s, sig, logs, upper, off, shared = {}, {}, {}, {}, {}, {}, {}
-        rows_out = [sb.tile([P, NP * N], F32, name=f"rows_out{j}") for j in range(NT)]
-        res = {T: rows_out[T % NT][:, N * (T // NT) : N * (T // NT + 1)] for T in range(TILES)}
+        wide, plain, turned, grouped, h_codes, h_scales, prod, emb = {}, {}, {}, {}, {}, {}, {}, {}
+        e_codes = [sb.tile([P, 3 * N], U32, name=f"e_codes{a}", align_bytes=MX_ALIGN) for a in range(NP)]
+        e_scales = [sb.tile([P, 3 * N], U8, name=f"e_scales{a}", align_bytes=MX_ALIGN) for a in range(NP)]
+        score, upper = {}, {}
+        sig = sb.tile([P, TRIANGLE], F32, name="sig")
+        neg_s = sb.tile([P, TRIANGLE], F32, name="neg_s")
+        logs = sb.tile([P, TRIANGLE], F32, name="logs")
+        res = [sb.tile([P, N], F32, name=f"res{T}") for T in range(TILES)]
         g_abs = sb.tile([P, NP * 4], F32, name="g_abs")
         preload = sb.tile([P, 1], F32, name="preload")
         horner = sb.tile([P, NP * 4, TERMS + 1], F32, name="horner")
@@ -140,14 +147,7 @@ def tile_generalpreferenceskewembeddingscores_d2p_kernel(
         def spread_scales():
             spread = bank(SPREAD_BANK, [P, P], "spread")
             nc.tensor.transpose(spread[:], scale_col[:].to_broadcast([P, P]), ident[:])
-            nc.vector.tensor_copy(out=row_scales[:], in_=spread[:, 0 : TILES * BLOCKS])
-
-        def pass_scales():
-            for q in range(4):
-                rows = slice(32 * q, 32 * (q + 1))
-                nc.vector.tensor_copy(out=scales[rows, :], in_=row_scales[rows, q : TILES * BLOCKS : 4])
-
-        gate_v, turn_banks, words, plain = [], [], {}, {}
+            nc.vector.tensor_copy(out=scales[:], in_=spread[:, 0 : TILES * BLOCKS])
 
         def gate_order():
             nc.vector.tensor_copy(
@@ -170,11 +170,11 @@ def tile_generalpreferenceskewembeddingscores_d2p_kernel(
                     v[:, NP * t : NP * (t + 1)], lhsT=gate_rows[:, P * t : P * (t + 1)], rhs=pick[:],
                     start=True, stop=True,
                 )
-            gate_v.append(v)
+            return v
 
-        def gate_abs():
-            nc.scalar.activation(out=g_abs[:], in_=gate_v[0][:], func=ACT.Abs)
-            nc.scalar.activation(out=addend[:, :, TERMS], in_=gate_v[0][:], func=ACT.Relu)
+        def gate_abs(v):
+            nc.scalar.activation(out=g_abs[:], in_=v[:], func=ACT.Abs)
+            nc.scalar.activation(out=addend[:, :, TERMS], in_=v[:], func=ACT.Relu)
 
         def gate_z():
             nc.scalar.activation(
@@ -195,113 +195,81 @@ def tile_generalpreferenceskewembeddingscores_d2p_kernel(
                 op1=ALU.add,
             )
 
-        def widen(T, passes=range(G)):
+        def widen(T, g):
             t, i = codes_in[T]
+            on_scalar = g == 1 and T in SCALAR_WIDENS
+            if on_scalar:
+                plain[T] = sb.tile([P, 512], BF16, name=f"plain{T}", align_bytes=64)
+            elif T not in wide:
+                wide[T] = sb.tile([P, D], BF16, name=f"wide{T}", align_bytes=64)
+            for j in range(4):
+                src = t[:, i, P * (4 * g + j) : P * (4 * g + j + 1)].bitcast(FP8)
+                scale = scales[:, BLOCKS * T + 4 * g + j : BLOCKS * T + 4 * g + j + 1]
+                if on_scalar:
+                    nc.scalar.activation(out=plain[T][:, P * j : P * (j + 1)], in_=src, func=ACT.Copy, scale=scale)
+                else:
+                    pairs = wide[T][:, 512 * g : 512 * (g + 1)].rearrange("p (u w e) -> p w u e", u=2, e=2)
+                    nc.vector.tensor_scalar(
+                        out=pairs[:, 32 * j : 32 * (j + 1)],
+                        in0=src.rearrange("p (w u e) -> p w u e", u=2, e=2),
+                        scalar1=scale,
+                        scalar2=None,
+                        op0=ALU.mult,
+                    )
+
+        def regroup(T):
             if T not in wide:
                 wide[T] = sb.tile([P, D], BF16, name=f"wide{T}", align_bytes=64)
-            first, last = passes[0], passes[-1] + 1
-            if MODES[G * T + first] in "AB":
-                for g in passes:
-                    if MODES[G * T + g] == "B":
-                        plain[T, g] = sb.tile([P, 512], BF16, name=f"plain{T}_{g}", align_bytes=64)
-                    for j in range(4):
-                        src = t[:, i, P * (4 * g + j) : P * (4 * g + j + 1)].bitcast(FP8)
-                        scale = row_scales[:, BLOCKS * T + 4 * g + j : BLOCKS * T + 4 * g + j + 1]
-                        if MODES[G * T + g] == "B":
-                            nc.scalar.activation(out=plain[T, g][:, P * j : P * (j + 1)], in_=src, func=ACT.Copy, scale=scale)
-                        else:
-                            pairs = wide[T][:, 512 * g : 512 * (g + 1)].rearrange("p (u w e) -> p w u e", u=2, e=2)
-                            nc.vector.tensor_scalar(
-                                out=pairs[:, 32 * j : 32 * (j + 1)],
-                                in0=src.rearrange("p (w u e) -> p w u e", u=2, e=2),
-                                scalar1=scale,
-                                scalar2=None,
-                                op0=ALU.mult,
-                            )
-                return
-            nc.gpsimd.tensor_copy(
-                out=wide[T][:, 512 * first : 512 * last], in_=t[:, i, 512 * first : 512 * last].bitcast(FP8)
+            nc.vector.tensor_copy(
+                out=wide[T][:].bitcast(F32)[:, 256:512].rearrange("p (u w) -> p u w", u=2),
+                in_=plain[T][:].bitcast(F32).rearrange("p (w u) -> p u w", u=2),
             )
 
-        def turn(T, passes=range(G)):
-            t = bank(TURN_BANKS[len(turn_banks) % 4], [P, 2 * len(passes), P], f"turned{T}_{passes[0]}")
-            turn_banks.append(t)
-            words[T, passes[0]] = t
-            for n, g in enumerate(passes):
-                turned[T, g] = t[:].bitcast(BF16)[:, 2 * n : 2 * n + 2, :]
+        def turn(T):
+            turned[T] = bank(TURN_BANKS[T % 4], [P, 2 * G, P], f"turned{T}")
+            for g in range(G):
                 for u in range(2):
-                    if MODES[G * T + g] == "B":
-                        src = plain[T, g][:].bitcast(F32)[:, u : 256 : 2]
-                    elif MODES[G * T + g] in "CDE":
-                        src = wide[T][:].bitcast(F32)[:, 256 * g + u : 256 * (g + 1) : 2]
+                    if g == 1 and T in SCALAR_WIDENS and T not in REGROUPED:
+                        src = plain[T][:].bitcast(F32)[:, u : 256 : 2]
                     else:
                         src = wide[T][:].bitcast(F32)[:, 256 * g + P * u : 256 * g + P * (u + 1)]
-                    nc.tensor.transpose(t[:, 2 * n + u, :], src, ident[:])
+                    nc.tensor.transpose(turned[T][:, 2 * g + u, :], src, ident[:])
 
-        def copy_turned(T, passes=range(G)):
-            if T not in grouped:
-                grouped[T] = sb.tile([P, G * P * 4], BF16, name=f"grouped{T}", align_bytes=64)
-            if MODES[G * T + passes[0]] in "ABE":
-                cols = slice(512 * passes[0], 512 * (passes[-1] + 1))
-                nc.scalar.copy(
-                    out=grouped[T][:, cols].bitcast(F32).rearrange("p (g n u) -> p g n u", n=P, u=2),
-                    in_=words[T, passes[0]][:].rearrange("p (g u) n -> p g n u", u=2),
-                )
-                return
-            for g in passes:
-                on_vector = MODES[G * T + g] == "D"
-                dst = grouped[T][:, 512 * g : 512 * (g + 1)].rearrange("p (n u e) -> p n u e", u=2, e=2)
-                src = turned[T, g].rearrange("p u (n e) -> p n u e", e=2)
-                scale = scales[:, G * T + g : G * T + g + 1]
-                if on_vector:
-                    nc.vector.tensor_scalar(out=dst, in0=src, scalar1=scale, scalar2=None, op0=ALU.mult)
-                else:
-                    nc.scalar.activation(out=dst, in_=src, func=ACT.Copy, scale=scale)
-
-        def scale_h(T, passes=range(G)):
-            for g in passes:
-                cols = grouped[T][:, 512 * g : 512 * (g + 1)]
-                nc.vector.tensor_scalar(
-                    out=cols, in0=cols, scalar1=scales[:, G * T + g : G * T + g + 1], scalar2=None, op0=ALU.mult
-                )
-
-        def quant_h(T, passes=range(G)):
-            if T not in h_codes:
-                h_codes[T] = sb.tile([P, G * P], U32, name=f"h_codes{T}", align_bytes=64)
-                h_scales[T] = sb.tile([P, G * P], U8, name=f"h_scales{T}", align_bytes=64)
-            first, last = passes[0], passes[-1] + 1
-            nc.vector.quantize_mx(
-                out=h_codes[T][:, P * first : P * last].bitcast(FP8X4),
-                scales=h_scales[T][:, P * first : P * last],
-                in_=grouped[T][:, 512 * first : 512 * last],
+        def copy_turned(T):
+            grouped[T] = sb.tile([P, G * P * 4], BF16, name=f"grouped{T}", align_bytes=64)
+            nc.scalar.copy(
+                out=grouped[T][:].bitcast(F32).rearrange("p (g n u) -> p g n u", n=P, u=2),
+                in_=turned[T][:].rearrange("p (g u) n -> p g n u", u=2),
             )
 
-        def permute(w, parts=(0, 1)):
-            both = (
+        def quant_h(T):
+            h_codes[T] = sb.tile([P, G * P], U32, name=f"h_codes{T}", align_bytes=MX_ALIGN)
+            h_scales[T] = sb.tile([P, G * P], U8, name=f"h_scales{T}", align_bytes=MX_ALIGN)
+            nc.vector.quantize_mx(out=h_codes[T][:].bitcast(FP8X4), scales=h_scales[T][:], in_=grouped[T][:])
+
+        def permute(w):
+            for dst, src, x in (
                 (w_perm[w][:].rearrange("p g t b -> p (g t b)"), w_raw[w][:].rearrange("p g b -> p (g b)"), 4),
                 (s_perm[w][:].rearrange("p g t b -> p (g t b)"), s_raw[w][:].rearrange("p g b -> p (g b)"), 2),
-            )
-            for dst, src, x in [both[n] for n in parts]:
+            ):
                 nc.vector.tensor_copy(
                     out=dst.bitcast(I32).rearrange("p (g t q x) -> p g q t x", g=G, t=4, x=x),
                     in_=src.bitcast(I32).rearrange("p (g q t x) -> p g q t x", g=G, t=4, x=x),
                 )
 
-        def project(w, T, by_pass=False):
+        def project(w, T):
             acc = prod[w, T] = bank(2 + 2 * (T % 2) + w, [P, 4, P], f"prod{w}_{T}")
-            steps = [(t, g) for t in range(4) for g in range(G)]
-            if by_pass:
-                steps = [(t, g) for g in range(G) for t in range(4)]
-            for n, (t, g) in enumerate(steps):
-                nc.tensor.matmul_mx(
-                    out=acc[:, t, :],
-                    lhsT=w_perm[w][:, g, t, :].bitcast(FP4X4),
-                    lhsT_scale=s_perm[w][:, g, t, :],
-                    rhs=h_codes[T][:, P * g : P * (g + 1)].bitcast(FP8X4),
-                    rhs_scale=h_scales[T][:, P * g : P * (g + 1)],
-                    start=(n == 0 if by_pass else g == 0),
-                    stop=(n == len(steps) - 1 if by_pass else g == G - 1),
-                )
+            for t in range(4):
+                for g in range(G):
+                    nc.tensor.matmul_mx(
+                        out=acc[:, t, :],
+                        lhsT=w_perm[w][:, g, t, :].bitcast(FP4X4),
+                        lhsT_scale=s_perm[w][:, g, t, :],
+                        rhs=h_codes[T][:, P * g : P * (g + 1)].bitcast(FP8X4),
+                        rhs_scale=h_scales[T][:, P * g : P * (g + 1)],
+                        start=(g == 0),
+                        stop=(g == G - 1),
+                    )
 
         def column(k, T):
             j = T % NT
@@ -309,37 +277,37 @@ def tile_generalpreferenceskewembeddingscores_d2p_kernel(
                 return 3 * P * j + P * k
             return 6 * P * (j // 2) + 2 * P * k + P * (j % 2)
 
-        def emb_cols(T, first, width):
+        def emb_run(k, T, width):
             if T // 2 not in emb:
-                emb[T // 2] = sb.tile([P, 6 * 512], BF16, name=f"emb{T // 2}", align_bytes=64)
-            first = first - 6 * P * (T % NT // 2)
+                emb[T // 2] = sb.tile([P, 6 * P * 4], BF16, name=f"emb{T // 2}", align_bytes=64)
+            first = column(k, T) - 6 * P * (T % NT // 2)
             return emb[T // 2][:, 4 * first : 4 * (first + width)]
-
-        def emb_run(k, T, count):
-            return emb_cols(T, column(k, T), P * count)
 
         def make_al(T):
             a = T // NT
             lam = horner[:, :, TERMS].rearrange("p (t a) -> p a t", a=NP)
             nc.vector.tensor_tensor(
-                out=emb_run(AL, T, 1).rearrange("p (n t) -> p n t", t=4),
+                out=emb_run(AL, T, P).rearrange("p (n t) -> p n t", t=4),
                 in0=prod[WA, T][:].rearrange("p t n -> p n t"),
                 in1=lam[:, a : a + 1, :].to_broadcast([P, P, 4]),
                 op=ALU.mult,
             )
 
-        def make_b(T, kinds=None):
+        def make_b(T):
             src = prod[WB, T][:].rearrange("p t n -> p n t")
-            for k in kinds or ((BP, BN) if T in SCALAR_NEGATES else (BP,)):
-                dst = emb_run(k, T, 1).rearrange("p (n t) -> p n t", t=4)
-                if k == BP:
-                    nc.scalar.copy(out=dst, in_=src)
-                else:
-                    nc.scalar.activation(out=dst, in_=src, func=ACT.Copy, scale=-1.0)
+            nc.scalar.copy(out=emb_run(BP, T, P).rearrange("p (n t) -> p n t", t=4), in_=src)
+            if T >= SCALAR_NEGATES:
+                nc.scalar.activation(
+                    out=emb_run(BN, T, P).rearrange("p (n t) -> p n t", t=4), in_=src, func=ACT.Copy, scale=-1.0
+                )
 
         def negate_b(T, count):
             nc.vector.tensor_scalar(
-                out=emb_run(BN, T, count), in0=emb_run(BP, T, count), scalar1=-1.0, scalar2=None, op0=ALU.mult
+                out=emb_run(BN, T, P * count),
+                in0=emb_run(BP, T, P * count),
+                scalar1=-1.0,
+                scalar2=None,
+                op0=ALU.mult,
             )
 
         def quant_emb(kinds, T, count):
@@ -347,15 +315,28 @@ def tile_generalpreferenceskewembeddingscores_d2p_kernel(
             nc.vector.quantize_mx(
                 out=e_codes[a][:, first : first + width].bitcast(FP8X4),
                 scales=e_scales[a][:, first : first + width],
-                in_=emb_cols(T, first, width),
+                in_=emb_run(kinds[0], T, width),
             )
 
-        def mx_pass(x, stationary, T, first, count, start, stop):
+        row_start, first = {}, 0
+        for T in ROW_ORDER:
+            row_start[T] = first
+            first = first + P * (T % NT + 1)
+
+        def row(T, lo, hi):
+            return slice(row_start[T] + lo, row_start[T] + hi)
+
+        def score_pass(stationary, T, i, count, start, stop):
             a, moving = T // NT, AL if stationary == BN else BP
+            at = row(T, P * i, P * (i + count))
+            n = max(m for m, (lo, hi) in enumerate(PIECES) if lo <= at.start)
+            lo, hi = PIECES[n]
+            if n not in score:
+                score[n] = bank(PIECE_BANKS[n], [P, hi - lo], f"score{n}")
             rows = slice(column(stationary, T), column(stationary, T) + P)
-            cols = slice(column(moving, first), column(moving, first) + P * count)
+            cols = slice(column(moving, a * NT + i), column(moving, a * NT + i) + P * count)
             nc.tensor.matmul_mx(
-                out=x,
+                out=score[n][:, at.start - lo : at.stop - lo],
                 lhsT=e_codes[a][:, rows].bitcast(FP8X4),
                 lhsT_scale=e_scales[a][:, rows],
                 rhs=e_codes[a][:, cols].bitcast(FP8X4),
@@ -364,123 +345,41 @@ def tile_generalpreferenceskewembeddingscores_d2p_kernel(
                 stop=stop,
             )
 
-        place = {}
-        for n, pack in enumerate(PACKS):
-            first = 0
-            for T in pack:
-                place[T] = (n, slice(first, first + P * (T % NT + 1)))
-                first = place[T][1].stop
-
-        pack_width = [place[pack[-1]][1].stop for pack in PACKS][0:4] + [256, 256]
-
-        def scores(n):
-            score[n] = bank(PACK_BANKS[n], [P, pack_width[n]], f"score{n}")
-            for T in PACKS[n]:
-                a, j = divmod(T, NT)
-                width = P * (j + 1)
-                x = score[n][:, place[T][1]]
-                for i in range(0, j + 1, 2):
-                    count = min(2, j + 1 - i)
-                    for stationary in (BN, AL):
-                        mx_pass(
-                            x[:, P * i : P * (i + count)], stationary, T, a * NT + i, count,
-                            stationary == BN, stationary == AL,
-                        )
-
-        def score_pass(T, stationary, lo, hi, start, stop):
-            a, j = divmod(T, NT)
-            n, cols = half_place(T, lo)
-            if n not in score:
-                score[n] = bank(PACK_BANKS[n], [P, pack_width[n]], f"score{n}")
-            mx_pass(score[n][:, lo - cols : hi - cols], stationary, T, a * NT + lo // P, (hi - lo) // P, start, stop)
-
-        def half_place(T, lo):
-            return (4, 0) if lo < 256 else (5, 256)
-
-        def lower_half(h):
-            nc.vector.scalar_tensor_tensor(
-                out=res[7][:, 256 * h : 256 * (h + 1)], in0=neg7[:, 256 * h : 256 * (h + 1)], scalar=-1.0, in1=logs[4 + h][:], op0=ALU.mult, op1=ALU.min
-            )
-
-        neg7 = sb.tile([P, N], F32, name="neg7")
-
-        def keep_half(h):
-            nc.vector.tensor_scalar(out=neg7[:, 256 * h : 256 * (h + 1)], in0=score[4 + h][:], scalar1=-C, scalar2=None, op0=ALU.mult)
+        def score_row(T):
+            width = T % NT + 1
+            for i in range(0, width, 2):
+                score_pass(BN, T, i, min(2, width - i), True, False)
+                score_pass(AL, T, i, min(2, width - i), False, True)
 
         def sigmoid(n):
-            sig[n] = sb.tile([P, pack_width[n]], F32, name=f"sig{n}")
-            nc.scalar.activation(out=sig[n][:], in_=score[n][:], func=ACT.Sigmoid, scale=C)
+            nc.scalar.activation(out=sig[:, slice(*PIECES[n])], in_=score[n][:], func=ACT.Sigmoid, scale=C)
 
         def keep_neg_s(n):
-            neg_s[n] = sb.tile([P, pack_width[n]], F32, name=f"neg_s{n}")
-            nc.vector.tensor_scalar(out=neg_s[n][:], in0=score[n][:], scalar1=-C, scalar2=None, op0=ALU.mult)
-
-        def log(n, cols):
-            if n not in logs:
-                logs[n] = sb.tile([P, pack_width[n]], F32, name=f"logs{n}")
-            nc.scalar.activation(out=logs[n][:, cols], in_=sig[n][:, cols], func=ACT.Ln, bias=tiny[:])
-
-        def lower(T, part):
-            n, cols = place[T]
-            nc.vector.scalar_tensor_tensor(
-                out=res[T][:, part],
-                in0=neg_s[n][:, cols][:, part],
-                scalar=-1.0,
-                in1=logs[n][:, cols][:, part],
-                op0=ALU.mult,
-                op1=ALU.min,
-            )
-
-        def lower_ps(T, part):
-            n, cols = place[T]
-            nc.vector.scalar_tensor_tensor(
-                out=res[T][:, part],
-                in0=score[n][:, cols][:, part],
-                scalar=C,
-                in1=logs[n][:, cols][:, part],
-                op0=ALU.mult,
-                op1=ALU.min,
-            )
-
-        def keep_off(T):
-            n, cols = place[T]
-            width = P * (T % NT)
-            off[T] = sb.tile([P, width], F32, name=f"off{T}")
             nc.vector.tensor_scalar(
-                out=off[T][:], in0=score[n][:, cols][:, 0:width], scalar1=-C, scalar2=None, op0=ALU.mult
+                out=neg_s[:, slice(*PIECES[n])], in0=score[n][:], scalar1=-C, scalar2=None, op0=ALU.mult
             )
 
-        def upper_t(T):
-            n, cols = place[T]
-            width = P * (T % NT)
-            off[T] = sb.tile([P, width], F32, name=f"off{T}")
+        def log(T, lo, hi):
+            nc.scalar.activation(out=logs[:, row(T, lo, hi)], in_=sig[:, row(T, lo, hi)], func=ACT.Ln, bias=tiny[:])
+
+        def lower(T, lo, hi):
             nc.vector.scalar_tensor_tensor(
-                out=off[T][:],
-                in0=score[n][:, cols][:, 0:width],
-                scalar=-C,
-                in1=res[T][:, 0:width],
+                out=res[T][:, lo:hi],
+                in0=neg_s[:, row(T, lo, hi)],
+                scalar=-1.0,
+                in1=logs[:, row(T, lo, hi)],
                 op0=ALU.mult,
-                op1=ALU.add,
+                op1=ALU.min,
             )
-
-        def turn_upper(row, b, first=0):
-            a, i = divmod(row, NT)
-            if first == 0:
-                shared[b] = bank(b, [P, N], f"upper{row}")
-            upper[row] = shared[b][:, first : first + N - P * (i + 1)]
-            for j in range(i + 1, NT):
-                nc.tensor.transpose(
-                    upper[row][:, P * (j - i - 1) : P * (j - i)], off[a * NT + j][:, P * i : P * (i + 1)], ident[:]
-                )
 
         def mirror(src, T, opening):
             a, j = divmod(T, NT)
             for i in reversed(range(j)):
-                row = a * NT + i
-                if row not in upper:
-                    upper[row] = bank(UPPER_BANKS[row], [P, N - P * (i + 1)], f"upper{row}")
+                above = a * NT + i
+                if above not in upper:
+                    upper[above] = bank(UPPER_BANKS[above], [P, N - P * (i + 1)], f"upper{above}")
                 nc.tensor.matmul(
-                    upper[row][:, P * (j - i - 1) : P * (j - i)],
+                    upper[above][:, P * (j - i - 1) : P * (j - i)],
                     lhsT=src[:, P * i : P * (i + 1)],
                     rhs=ident[:],
                     is_transpose=True,
@@ -495,21 +394,9 @@ def tile_generalpreferenceskewembeddingscores_d2p_kernel(
             else:
                 nc.scalar.copy(out=res[T][:, cols], in_=upper[T][:])
 
-        def store(T, part, queue=nc.sync):
+        def store(T, lo, hi):
             a, j = divmod(T, NT)
-            queue.dma_start(out=out[a, P * j : P * (j + 1), part], in_=res[T][:, part])
-
-        def store_both(j):
-            nc.sync.dma_start(
-                out=out[:, P * j : P * (j + 1), :].rearrange("a p n -> p a n"),
-                in_=rows_out[j][:].rearrange("p (a n) -> p a n", a=NP),
-            )
-
-        def begin(T):
-            project(WB, T)
-            make_b(T)
-            if T > 0:
-                make_al(T - 1)
+            nc.sync.dma_start(out=out[a, P * j : P * (j + 1), lo:hi], in_=res[T][:, lo:hi])
 
         nc.scalar.activation(out=preload[:], in_=tiny[:], func=ACT.Sigmoid)
         warm_tensor(2)
@@ -517,19 +404,15 @@ def tile_generalpreferenceskewembeddingscores_d2p_kernel(
         spread_scales()
         gate_order()
         warm_tensor(1)
-        gate_turn()
+        gate_v = gate_turn()
         warm_tensor(1)
-        for T in range(2):
+        for T in range(NT):
             for g in range(G):
-                widen(T, (g,))
-        widen(2, (1,))
-        widen(2, (0,))
-        widen(3)
-        turn(0)
-        warm_tensor(1)
-        turn(1)
-        warm_tensor(1)
-        gate_abs()
+                widen(T, g)
+        for T in range(2):
+            turn(T)
+            warm_tensor(1)
+        gate_abs(gate_v)
         copy_turned(0)
         gate_z()
         copy_turned(1)
@@ -541,30 +424,32 @@ def tile_generalpreferenceskewembeddingscores_d2p_kernel(
         quant_h(0)
         quant_h(1)
         permute(WA)
-        project(WB, 0)
-        project(WB, 1)
-        project(WA, 0)
-        project(WA, 1)
-        widen(5)
+
+        for w in (WB, WA):
+            for T in range(2):
+                project(w, T)
+        widen(5, 0)
+        widen(5, 1)
         make_b(0)
         quant_h(2)
         copy_turned(3)
-        widen(4, (0,))
+        widen(4, 0)
         gate_series()
         make_b(1)
-        widen(6, (1,))
-        widen(4, (1,))
+        widen(6, 1)
+        widen(4, 1)
         make_al(0)
         quant_h(3)
         project(WB, 2)
         project(WA, 2)
-        widen(7, (1,))
-        widen(6, (0,))
+        widen(7, 1)
+        widen(6, 0)
         make_al(1)
-        widen(7, (0,))
+        widen(7, 0)
+        regroup(7)
         make_b(2)
         project(WB, 3)
-        for T in (4, 5, 6, 7):
+        for T in range(NT, TILES):
             turn(T)
         project(WA, 3)
         make_al(2)
@@ -575,6 +460,7 @@ def tile_generalpreferenceskewembeddingscores_d2p_kernel(
         quant_emb((AL,), 0, 2)
         quant_h(4)
         quant_emb((BP, BN), 0, 2)
+
         project(WB, 4)
         project(WA, 4)
         copy_turned(6)
@@ -592,70 +478,71 @@ def tile_generalpreferenceskewembeddingscores_d2p_kernel(
         quant_emb((AL,), 2, 2)
         negate_b(4, 1)
         quant_h(7)
-        begin(6)
-        scores(0)
+        project(WB, 6)
+        make_b(6)
+        make_al(5)
+        score_row(3)
         sigmoid(0)
         quant_emb((BP, BN), 4, 2)
         project(WA, 6)
-        begin(7)
+        project(WB, 7)
+        make_b(7)
+        make_al(6)
         quant_emb((AL,), 4, 2)
         quant_emb((BP, BN, AL), 6, 1)
         project(WA, 7)
         make_al(7)
         quant_emb((BP, BN), 7, 1)
         quant_emb((AL,), 7, 1)
+
         for n in range(1, 4):
-            scores(n)
+            for T in ROW_ORDER[2 * n - 1 : 2 * n + 1]:
+                score_row(T)
             sigmoid(n)
-        score_pass(7, BN, 0, 256, True, False)
-        score_pass(7, BN, 256, 384, True, False)
-        score_pass(7, AL, 0, 256, False, True)
+        score_pass(BN, 7, 0, 2, True, False)
+        score_pass(BN, 7, 2, 1, True, False)
+        score_pass(AL, 7, 0, 2, False, True)
         sigmoid(4)
-        score_pass(7, BN, 384, 512, False, False)
-        score_pass(7, AL, 256, 384, False, False)
-        score_pass(7, AL, 384, 512, False, True)
+        score_pass(BN, 7, 3, 1, False, False)
+        score_pass(AL, 7, 2, 1, False, False)
+        score_pass(AL, 7, 3, 1, False, True)
         sigmoid(5)
-        for n in range(4):
+
+        for n in range(len(PIECES)):
             keep_neg_s(n)
-        for h in range(2):
-            keep_half(h)
         for a in range(NP):
             for T in range(a * NT + NT - 1, a * NT, -1):
-                n, cols = place[T]
-                mirror(neg7 if T == 7 else neg_s[n][:, cols], T, True)
-        whole = slice(0, N)
-        for part in (slice(0, 256), slice(256, 512)):
-            log(0, part)
-            lower(3, part)
-            store(3, part)
-        mirror(res[3], 3, False)
-        for h in range(2):
-            log(4 + h, slice(0, 256))
-            lower_half(h)
-            store(7, slice(256 * h, 256 * (h + 1)))
-        mirror(res[7], 7, False)
+                mirror(neg_s[:, row(T, 0, P * (T % NT))], T, True)
+        half = N // 2
+        for T in (3, 7):
+            for lo in (0, half):
+                log(T, lo, lo + half)
+                lower(T, lo, lo + half)
+                store(T, lo, lo + half)
+            mirror(res[T], T, False)
         for T in (2, 6):
-            log(*place[T])
+            log(T, 0, 3 * P)
         copy_upper(2, False)
-        lower(2, slice(0, 2 * P))
-        store(2, slice(0, 2 * P))
+        lower(2, 0, half)
+        store(2, 0, half)
         mirror(res[2], 2, False)
-        lower(2, slice(2 * P, 3 * P))
-        store(2, slice(2 * P, N))
-        log(*place[1])
+        lower(2, half, 3 * P)
+        store(2, half, N)
+        log(1, 0, 2 * P)
         copy_upper(6, False)
-        lower(6, slice(0, 3 * P))
-        store(6, whole)
+        lower(6, 0, 3 * P)
+        store(6, 0, N)
         mirror(res[6], 6, False)
-        for T in (5, 0, 4):
-            log(*place[T])
+        log(5, 0, 2 * P)
+        for T in (0, 4):
+            log(T, 0, P)
         for T in (1, 5):
-            lower(T, slice(0, 2 * P))
+            lower(T, 0, 2 * P)
             mirror(res[T], T, False)
             copy_upper(T, T == 1)
-            store(T, whole)
+            store(T, 0, N)
         for T in (0, 4):
-            lower(T, slice(0, P))
+            lower(T, 0, P)
         for T in (0, 4):
             copy_upper(T, T == 4)
-            store(T, whole)
+            store(T, 0, N)

import math
from contextlib import ExitStack

import concourse.mybir as mybir
from concourse.masks import make_identity

NP, N, D, K = 2, 512, 1024, 512
P = 128
NT = N // P
TILES = NP * NT
G = D // 512
BLOCKS = D // P
FLOPS = 2 * NP * (2 * N * D * K + N * N * K)
C = K ** -0.5
TINY = 2.0 ** -60
TERMS = 9

F32 = mybir.dt.float32
BF16 = mybir.dt.bfloat16
I32 = mybir.dt.int32
U32 = mybir.dt.uint32
U8 = mybir.dt.uint8
FP8 = mybir.dt.float8_e4m3fn
FP8X4 = mybir.dt.float8_e4m3fn_x4
FP4X4 = mybir.dt.float4_e2m1fn_x4
ALU = mybir.AluOpType
ACT = mybir.ActivationFunctionType

WB, WA = 0, 1
BP, BN, AL = 0, 1, 2

MX_ALIGN = 256

SCALAR_WIDENS = (1, 2, 5, 6, 7)
REGROUPED = (7,)
SCALAR_NEGATES = 5
SINGLE_FROM = 6

ROW_ORDER = (3, 0, 2, 1, 5, 4, 6, 7)
TRIANGLE = NP * P * NT * (NT + 1) // 2
PIECES = [(lo, lo + N) for lo in range(0, TRIANGLE - N, N)] + [(lo, lo + N // 2) for lo in (TRIANGLE - N, TRIANGLE - N // 2)]

TURN_BANKS = (0, 1, 6, 7)
PIECE_BANKS = (6, 0, 1, 7, 2, 3)
UPPER_BANKS = {0: 4, 1: 5, 2: 6, 4: 0, 5: 1, 6: 7}
SPREAD_BANK, WARM_BANK, GATE_BANK = 3, 4, 5


def tile_generalpreferenceskewembeddingscores_d2p_kernel(
    tc, h_bytes, h_scale, wa_words, wa_scales, wb_words, wb_scales, gate, out
):
    nc = tc.nc
    with ExitStack() as ctx:
        sb = ctx.enter_context(tc.tile_pool(name="sb", bufs=1))
        ps = ctx.enter_context(tc.psum_pool(name="ps", bufs=1))
        ctx.enter_context(tc.manual_schedule())

        def bank(b, shape, name):
            return ps.tile(shape, F32, name=name, tag=f"bank{b}")

        gate_in = sb.tile([P, K], BF16, name="gate_in")
        gate_rows = sb.tile([P, K], BF16, name="gate_rows")
        ident = sb.tile([P, P], F32, name="ident")
        pick = sb.tile([P, NP], BF16, name="pick")
        w_raw = [sb.tile([P, G, 1024], U8, name=f"w_raw{w}", align_bytes=64) for w in range(2)]
        w_perm = [sb.tile([P, G, 4, 256], U8, name=f"w_perm{w}", align_bytes=MX_ALIGN) for w in range(2)]
        s_raw = [sb.tile([P, G, K], U8, name=f"s_raw{w}", align_bytes=64) for w in range(2)]
        s_perm = [sb.tile([P, G, 4, P], U8, name=f"s_perm{w}", align_bytes=MX_ALIGN) for w in range(2)]
        scales = sb.tile([P, TILES * BLOCKS], F32, name="scales")
        scale_col = sb.tile([P, 1], F32, name="scale_col")
        tiny = sb.tile([P, 1], F32, name="tiny")
        odd = sb.tile([P, NP * 4, TERMS], F32, name="odd")
        half_odd = sb.tile([P, NP * 4, TERMS], F32, name="half_odd")
        neg_ln2 = sb.tile([P, 1], F32, name="neg_ln2")
        factor = sb.tile([P, NP * 4, TERMS + 1], F32, name="factor")
        addend = sb.tile([P, NP * 4, TERMS + 1], F32, name="addend")
        zeros = sb.tile([P, N], BF16, name="zeros")

        nc.gpsimd.iota(
            odd[:], pattern=[[0, NP * 4], [-2, TERMS]], base=2 * TERMS - 1, channel_multiplier=0,
            allow_small_or_imprecise_dtypes=True,
        )
        nc.vector.memset(zeros[:], 0.0)
        nc.vector.memset(ident[:], 0.0)
        make_identity(nc, ident[:], nomemset=True)
        for w in range(2):
            nc.vector.memset(s_raw[w][:].rearrange("p g k -> p (g k)").bitcast(I32), 0)
        nc.vector.memset(gate_rows[:], 0.0)
        nc.vector.memset(scale_col[TILES * BLOCKS : P, :], 0.0)
        nc.vector.memset(tiny[:], TINY)
        nc.vector.memset(factor[:, :, 0:1], 0.0)

        codes_in = {}

        def load_h(a, first, count):
            t = sb.tile([P, count, D], U8, name=f"h_bytes{a}_{first}", align_bytes=64)
            nc.sync.dma_start(
                out=t[:],
                in_=h_bytes[a, first * P : (first + count) * P, :].rearrange("(i p) k -> p i k", p=P),
            )
            for i in range(count):
                codes_in[a * NT + first + i] = (t, i)

        def load_words(w, words):
            nc.sync.dma_start(
                out=w_raw[w][:].rearrange("p g b -> p (g b)").bitcast(I32).rearrange("p (g c) -> p g c", g=G),
                in_=words.bitcast(I32).rearrange("g p c -> p g c"),
            )

        def load_scale_rows(w, scale_rows):
            src = scale_rows.bitcast(I32).rearrange("g (q r) c -> q r g c", r=4)
            dst = s_raw[w][:].rearrange("p g k -> p (g k)").bitcast(I32).rearrange("p (g c) -> p g c", g=G)
            for q in range(4):
                nc.sync.dma_start(out=dst[32 * q : 32 * q + 4], in_=src[q])

        nc.scalar.dma_start(
            out=scale_col[0 : TILES * BLOCKS, :], in_=h_scale.rearrange("a i (j o) -> (a i j) o", o=1)
        )
        load_h(0, 0, 1)
        nc.scalar.dma_start(out=gate_in[0:NP, :], in_=gate)
        load_h(0, 1, 1)
        load_h(0, 2, 2)
        load_scale_rows(WB, wb_scales)
        load_words(WB, wb_words)
        load_h(1, 0, 2)
        load_words(WA, wa_words)
        load_scale_rows(WA, wa_scales)
        load_h(1, 2, 2)

        wide, plain, turned, grouped, h_codes, h_scales, prod, emb = {}, {}, {}, {}, {}, {}, {}, {}
        e_codes = [sb.tile([P, 3 * N], U32, name=f"e_codes{a}", align_bytes=MX_ALIGN) for a in range(NP)]
        e_scales = [sb.tile([P, 3 * N], U8, name=f"e_scales{a}", align_bytes=MX_ALIGN) for a in range(NP)]
        score, upper = {}, {}
        sig = sb.tile([P, TRIANGLE], F32, name="sig")
        neg_s = sb.tile([P, TRIANGLE], F32, name="neg_s")
        logs = sb.tile([P, TRIANGLE], F32, name="logs")
        res = [sb.tile([P, N], F32, name=f"res{T}") for T in range(TILES)]
        g_abs = sb.tile([P, NP * 4], F32, name="g_abs")
        preload = sb.tile([P, 1], F32, name="preload")
        horner = sb.tile([P, NP * 4, TERMS + 1], F32, name="horner")

        def warm_tensor(count):
            for i in range(count):
                unread = bank(WARM_BANK, [P, N], "unread")
                nc.tensor.matmul(unread[:], lhsT=zeros[:, 0:P], rhs=zeros[:], start=True, stop=True)

        def spread_scales():
            spread = bank(SPREAD_BANK, [P, P], "spread")
            nc.tensor.transpose(spread[:], scale_col[:].to_broadcast([P, P]), ident[:])
            nc.vector.tensor_copy(out=scales[:], in_=spread[:, 0 : TILES * BLOCKS])

        def gate_order():
            nc.vector.tensor_copy(
                out=gate_rows[0:NP, :].rearrange("a (t q r) -> a t q r", t=4, r=8),
                in_=gate_in[0:NP, :].rearrange("a (q t r) -> a t q r", t=4, r=8),
            )

        def gate_constants():
            nc.vector.tensor_scalar(out=half_odd[:], in0=odd[:], scalar1=0.5, scalar2=None, op0=ALU.mult)
            nc.vector.tensor_scalar(
                out=neg_ln2[:], in0=odd[:, 0, TERMS - 1 : TERMS], scalar1=-math.log(2.0), scalar2=None, op0=ALU.mult
            )
            nc.vector.reciprocal(out=addend[:, :, 0:TERMS], in_=half_odd[:])
            nc.vector.tensor_copy(out=pick[:], in_=ident[:, 0:NP])

        def gate_turn():
            v = bank(GATE_BANK, [P, NP * 4], "v")
            for t in range(4):
                nc.tensor.matmul(
                    v[:, NP * t : NP * (t + 1)], lhsT=gate_rows[:, P * t : P * (t + 1)], rhs=pick[:],
                    start=True, stop=True,
                )
            return v

        def gate_abs(v):
            nc.scalar.activation(out=g_abs[:], in_=v[:], func=ACT.Abs)
            nc.scalar.activation(out=addend[:, :, TERMS], in_=v[:], func=ACT.Relu)

        def gate_z():
            nc.scalar.activation(
                out=factor[:, :, TERMS], in_=g_abs[:], func=ACT.Sigmoid, scale=-1.0, bias=neg_ln2[:]
            )

        def gate_square():
            z = factor[:, :, TERMS : TERMS + 1].to_broadcast([P, NP * 4, TERMS - 1])
            nc.scalar.activation(out=factor[:, :, 1:TERMS], in_=z, func=ACT.Square)

        def gate_series():
            nc.vector.tensor_tensor_scan(
                out=horner[:].rearrange("p c n -> p (c n)"),
                data0=factor[:].rearrange("p c n -> p (c n)"),
                data1=addend[:].rearrange("p c n -> p (c n)"),
                initial=0.0,
                op0=ALU.mult,
                op1=ALU.add,
            )

        def widen(T, g):
            t, i = codes_in[T]
            on_scalar = g == 1 and T in SCALAR_WIDENS
            if on_scalar:
                plain[T] = sb.tile([P, 512], BF16, name=f"plain{T}", align_bytes=64)
            elif T not in wide:
                wide[T] = sb.tile([P, D], BF16, name=f"wide{T}", align_bytes=64)
            for j in range(4):
                src = t[:, i, P * (4 * g + j) : P * (4 * g + j + 1)].bitcast(FP8)
                scale = scales[:, BLOCKS * T + 4 * g + j : BLOCKS * T + 4 * g + j + 1]
                if on_scalar:
                    nc.scalar.activation(out=plain[T][:, P * j : P * (j + 1)], in_=src, func=ACT.Copy, scale=scale)
                else:
                    pairs = wide[T][:, 512 * g : 512 * (g + 1)].rearrange("p (u w e) -> p w u e", u=2, e=2)
                    nc.vector.tensor_scalar(
                        out=pairs[:, 32 * j : 32 * (j + 1)],
                        in0=src.rearrange("p (w u e) -> p w u e", u=2, e=2),
                        scalar1=scale,
                        scalar2=None,
                        op0=ALU.mult,
                    )

        def regroup(T):
            if T not in wide:
                wide[T] = sb.tile([P, D], BF16, name=f"wide{T}", align_bytes=64)
            nc.vector.tensor_copy(
                out=wide[T][:].bitcast(F32)[:, 256:512].rearrange("p (u w) -> p u w", u=2),
                in_=plain[T][:].bitcast(F32).rearrange("p (w u) -> p u w", u=2),
            )

        def turn(T):
            turned[T] = bank(TURN_BANKS[T % 4], [P, 2 * G, P], f"turned{T}")
            for g in range(G):
                for u in range(2):
                    if g == 1 and T in SCALAR_WIDENS and T not in REGROUPED:
                        src = plain[T][:].bitcast(F32)[:, u : 256 : 2]
                    else:
                        src = wide[T][:].bitcast(F32)[:, 256 * g + P * u : 256 * g + P * (u + 1)]
                    nc.tensor.transpose(turned[T][:, 2 * g + u, :], src, ident[:])

        def copy_turned(T):
            grouped[T] = sb.tile([P, G * P * 4], BF16, name=f"grouped{T}", align_bytes=64)
            nc.scalar.copy(
                out=grouped[T][:].bitcast(F32).rearrange("p (g n u) -> p g n u", n=P, u=2),
                in_=turned[T][:].rearrange("p (g u) n -> p g n u", u=2),
            )

        def quant_h(T):
            h_codes[T] = sb.tile([P, G * P], U32, name=f"h_codes{T}", align_bytes=MX_ALIGN)
            h_scales[T] = sb.tile([P, G * P], U8, name=f"h_scales{T}", align_bytes=MX_ALIGN)
            nc.vector.quantize_mx(out=h_codes[T][:].bitcast(FP8X4), scales=h_scales[T][:], in_=grouped[T][:])

        def permute(w):
            for dst, src, x in (
                (w_perm[w][:].rearrange("p g t b -> p (g t b)"), w_raw[w][:].rearrange("p g b -> p (g b)"), 4),
                (s_perm[w][:].rearrange("p g t b -> p (g t b)"), s_raw[w][:].rearrange("p g b -> p (g b)"), 2),
            ):
                nc.vector.tensor_copy(
                    out=dst.bitcast(I32).rearrange("p (g t q x) -> p g q t x", g=G, t=4, x=x),
                    in_=src.bitcast(I32).rearrange("p (g q t x) -> p g q t x", g=G, t=4, x=x),
                )

        def project(w, T):
            acc = prod[w, T] = bank(2 + 2 * (T % 2) + w, [P, 4, P], f"prod{w}_{T}")
            for t in range(4):
                for g in range(G):
                    nc.tensor.matmul_mx(
                        out=acc[:, t, :],
                        lhsT=w_perm[w][:, g, t, :].bitcast(FP4X4),
                        lhsT_scale=s_perm[w][:, g, t, :],
                        rhs=h_codes[T][:, P * g : P * (g + 1)].bitcast(FP8X4),
                        rhs_scale=h_scales[T][:, P * g : P * (g + 1)],
                        start=(g == 0),
                        stop=(g == G - 1),
                    )

        def column(k, T):
            j = T % NT
            if T >= SINGLE_FROM:
                return 3 * P * j + P * k
            return 6 * P * (j // 2) + 2 * P * k + P * (j % 2)

        def emb_run(k, T, width):
            if T // 2 not in emb:
                emb[T // 2] = sb.tile([P, 6 * P * 4], BF16, name=f"emb{T // 2}", align_bytes=64)
            first = column(k, T) - 6 * P * (T % NT // 2)
            return emb[T // 2][:, 4 * first : 4 * (first + width)]

        def make_al(T):
            a = T // NT
            lam = horner[:, :, TERMS].rearrange("p (t a) -> p a t", a=NP)
            nc.vector.tensor_tensor(
                out=emb_run(AL, T, P).rearrange("p (n t) -> p n t", t=4),
                in0=prod[WA, T][:].rearrange("p t n -> p n t"),
                in1=lam[:, a : a + 1, :].to_broadcast([P, P, 4]),
                op=ALU.mult,
            )

        def make_b(T):
            src = prod[WB, T][:].rearrange("p t n -> p n t")
            nc.scalar.copy(out=emb_run(BP, T, P).rearrange("p (n t) -> p n t", t=4), in_=src)
            if T >= SCALAR_NEGATES:
                nc.scalar.activation(
                    out=emb_run(BN, T, P).rearrange("p (n t) -> p n t", t=4), in_=src, func=ACT.Copy, scale=-1.0
                )

        def negate_b(T, count):
            nc.vector.tensor_scalar(
                out=emb_run(BN, T, P * count),
                in0=emb_run(BP, T, P * count),
                scalar1=-1.0,
                scalar2=None,
                op0=ALU.mult,
            )

        def quant_emb(kinds, T, count):
            a, first, width = T // NT, column(kinds[0], T), P * count * len(kinds)
            nc.vector.quantize_mx(
                out=e_codes[a][:, first : first + width].bitcast(FP8X4),
                scales=e_scales[a][:, first : first + width],
                in_=emb_run(kinds[0], T, width),
            )

        row_start, first = {}, 0
        for T in ROW_ORDER:
            row_start[T] = first
            first = first + P * (T % NT + 1)

        def row(T, lo, hi):
            return slice(row_start[T] + lo, row_start[T] + hi)

        def score_pass(stationary, T, i, count, start, stop):
            a, moving = T // NT, AL if stationary == BN else BP
            at = row(T, P * i, P * (i + count))
            n = max(m for m, (lo, hi) in enumerate(PIECES) if lo <= at.start)
            lo, hi = PIECES[n]
            if n not in score:
                score[n] = bank(PIECE_BANKS[n], [P, hi - lo], f"score{n}")
            rows = slice(column(stationary, T), column(stationary, T) + P)
            cols = slice(column(moving, a * NT + i), column(moving, a * NT + i) + P * count)
            nc.tensor.matmul_mx(
                out=score[n][:, at.start - lo : at.stop - lo],
                lhsT=e_codes[a][:, rows].bitcast(FP8X4),
                lhsT_scale=e_scales[a][:, rows],
                rhs=e_codes[a][:, cols].bitcast(FP8X4),
                rhs_scale=e_scales[a][:, cols],
                start=start,
                stop=stop,
            )

        def score_row(T):
            width = T % NT + 1
            for i in range(0, width, 2):
                score_pass(BN, T, i, min(2, width - i), True, False)
                score_pass(AL, T, i, min(2, width - i), False, True)

        def sigmoid(n):
            nc.scalar.activation(out=sig[:, slice(*PIECES[n])], in_=score[n][:], func=ACT.Sigmoid, scale=C)

        def keep_neg_s(n):
            nc.vector.tensor_scalar(
                out=neg_s[:, slice(*PIECES[n])], in0=score[n][:], scalar1=-C, scalar2=None, op0=ALU.mult
            )

        def log(T, lo, hi):
            nc.scalar.activation(out=logs[:, row(T, lo, hi)], in_=sig[:, row(T, lo, hi)], func=ACT.Ln, bias=tiny[:])

        def lower(T, lo, hi):
            nc.vector.scalar_tensor_tensor(
                out=res[T][:, lo:hi],
                in0=neg_s[:, row(T, lo, hi)],
                scalar=-1.0,
                in1=logs[:, row(T, lo, hi)],
                op0=ALU.mult,
                op1=ALU.min,
            )

        def mirror(src, T, opening):
            a, j = divmod(T, NT)
            for i in reversed(range(j)):
                above = a * NT + i
                if above not in upper:
                    upper[above] = bank(UPPER_BANKS[above], [P, N - P * (i + 1)], f"upper{above}")
                nc.tensor.matmul(
                    upper[above][:, P * (j - i - 1) : P * (j - i)],
                    lhsT=src[:, P * i : P * (i + 1)],
                    rhs=ident[:],
                    is_transpose=True,
                    start=(opening and j == NT - 1),
                    stop=(not opening and j == i + 1),
                )

        def copy_upper(T, on_vector):
            cols = slice(P * (T % NT + 1), N)
            if on_vector:
                nc.vector.tensor_copy(out=res[T][:, cols], in_=upper[T][:])
            else:
                nc.scalar.copy(out=res[T][:, cols], in_=upper[T][:])

        def store(T, lo, hi):
            a, j = divmod(T, NT)
            nc.sync.dma_start(out=out[a, P * j : P * (j + 1), lo:hi], in_=res[T][:, lo:hi])

        nc.scalar.activation(out=preload[:], in_=tiny[:], func=ACT.Sigmoid)
        warm_tensor(2)
        gate_constants()
        spread_scales()
        gate_order()
        warm_tensor(1)
        gate_v = gate_turn()
        warm_tensor(1)
        for T in range(NT):
            for g in range(G):
                widen(T, g)
        for T in range(2):
            turn(T)
            warm_tensor(1)
        gate_abs(gate_v)
        copy_turned(0)
        gate_z()
        copy_turned(1)
        gate_square()
        turn(2)
        turn(3)
        copy_turned(2)
        permute(WB)
        quant_h(0)
        quant_h(1)
        permute(WA)

        for w in (WB, WA):
            for T in range(2):
                project(w, T)
        widen(5, 0)
        widen(5, 1)
        make_b(0)
        quant_h(2)
        copy_turned(3)
        widen(4, 0)
        gate_series()
        make_b(1)
        widen(6, 1)
        widen(4, 1)
        make_al(0)
        quant_h(3)
        project(WB, 2)
        project(WA, 2)
        widen(7, 1)
        widen(6, 0)
        make_al(1)
        widen(7, 0)
        regroup(7)
        make_b(2)
        project(WB, 3)
        for T in range(NT, TILES):
            turn(T)
        project(WA, 3)
        make_al(2)
        negate_b(0, 2)
        copy_turned(4)
        copy_turned(5)
        make_b(3)
        quant_emb((AL,), 0, 2)
        quant_h(4)
        quant_emb((BP, BN), 0, 2)

        project(WB, 4)
        project(WA, 4)
        copy_turned(6)
        quant_h(5)
        negate_b(2, 2)
        make_al(3)
        make_b(4)
        copy_turned(7)
        project(WB, 5)
        quant_emb((BP, BN), 2, 2)
        quant_h(6)
        make_al(4)
        project(WA, 5)
        make_b(5)
        quant_emb((AL,), 2, 2)
        negate_b(4, 1)
        quant_h(7)
        project(WB, 6)
        make_b(6)
        make_al(5)
        score_row(3)
        sigmoid(0)
        quant_emb((BP, BN), 4, 2)
        project(WA, 6)
        project(WB, 7)
        make_b(7)
        make_al(6)
        quant_emb((AL,), 4, 2)
        quant_emb((BP, BN, AL), 6, 1)
        project(WA, 7)
        make_al(7)
        quant_emb((BP, BN), 7, 1)
        quant_emb((AL,), 7, 1)

        for n in range(1, 4):
            for T in ROW_ORDER[2 * n - 1 : 2 * n + 1]:
                score_row(T)
            sigmoid(n)
        score_pass(BN, 7, 0, 2, True, False)
        score_pass(BN, 7, 2, 1, True, False)
        score_pass(AL, 7, 0, 2, False, True)
        sigmoid(4)
        score_pass(BN, 7, 3, 1, False, False)
        score_pass(AL, 7, 2, 1, False, False)
        score_pass(AL, 7, 3, 1, False, True)
        sigmoid(5)

        for n in range(len(PIECES)):
            keep_neg_s(n)
        for a in range(NP):
            for T in range(a * NT + NT - 1, a * NT, -1):
                mirror(neg_s[:, row(T, 0, P * (T % NT))], T, True)
        half = N // 2
        for T in (3, 7):
            for lo in (0, half):
                log(T, lo, lo + half)
                lower(T, lo, lo + half)
                store(T, lo, lo + half)
            mirror(res[T], T, False)
        for T in (2, 6):
            log(T, 0, 3 * P)
        copy_upper(2, False)
        lower(2, 0, half)
        store(2, 0, half)
        mirror(res[2], 2, False)
        lower(2, half, 3 * P)
        store(2, half, N)
        log(1, 0, 2 * P)
        copy_upper(6, False)
        lower(6, 0, 3 * P)
        store(6, 0, N)
        mirror(res[6], 6, False)
        log(5, 0, 2 * P)
        for T in (0, 4):
            log(T, 0, P)
        for T in (1, 5):
            lower(T, 0, 2 * P)
            mirror(res[T], T, False)
            copy_upper(T, T == 1)
            store(T, 0, N)
        for T in (0, 4):
            lower(T, 0, P)
        for T in (0, 4):
            copy_upper(T, T == 4)
            store(T, 0, N)
